import numpy as np
import ml_dtypes


def mxq(x, axis, fmt="e4m3"):
    dtype, down = {"e4m3": (ml_dtypes.float8_e4m3fn, 7), "e5m2": (ml_dtypes.float8_e5m2, 14)}[fmt]
    v = np.moveaxis(np.asarray(x, np.float32).astype(ml_dtypes.bfloat16).astype(np.float64), axis, -1)
    blocks = v.reshape(v.shape[:-1] + (-1, 32))
    amax = np.abs(blocks).max(-1, keepdims=True)
    byte = np.maximum(np.where(amax > 0, np.frexp(amax)[1] - 1 + 127, 0) - down, 1)
    scale = np.exp2(byte - 127.0)
    codes = (blocks / scale).astype(np.float32).astype(dtype).astype(np.float64)
    return np.moveaxis((codes * scale).reshape(v.shape), -1, axis)


WIDE = False


def mx_kscale(k):
    if not WIDE:
        return np.ones(k)
    levels = np.array([10, -10, 5, -5, 0])
    if k % 512:
        return np.exp2(np.random.permutation(np.resize(levels, k // 32))).repeat(32)
    a = np.empty((k // 512, 16))
    for p in range(k // 512):
        a[p, :8] = np.random.permutation(np.resize(levels, 8))
        for g in range(8):
            far = levels[np.abs(levels - a[p, g]) >= 10]
            a[p, g + 8] = far[np.random.randint(len(far))]
    return np.exp2(a.ravel()).repeat(32)


def f64(x):
    return np.asarray(x).astype(np.float64)


def striped(idx):
    return np.tile(idx.reshape(-1, 16).T, (8, 1)).astype(np.uint16)


def unstriped(offs):
    return offs[:16].T.reshape(-1).astype(np.int64)


E2M1 = np.array([0.0, 0.5, 1.0, 1.5, 2.0, 3.0, 4.0, 6.0, -0.0, -0.5, -1.0, -1.5, -2.0, -3.0, -4.0, -6.0])


def pack_weight(w, fmt):
    k, n = w.shape
    w = f64(np.asarray(w, np.float32).astype(ml_dtypes.bfloat16)).reshape(k // 32, 32, n)
    amax = np.abs(w).max(1)
    if fmt == "e4m3":
        byte = np.frexp(amax)[1] - 1 + 127 - 7
    else:
        mant, ex = np.frexp(amax / 6.0)
        byte = np.where(mant > 0.5, ex, ex - 1) + 127
    byte = np.clip(np.where(amax > 0, byte, 1), 1, 254)
    scaled = (w * np.exp2(127.0 - byte)[:, None, :]).reshape(k, n).astype(np.float32)
    by_word = np.ascontiguousarray(scaled.reshape(k // 512, 128, 4, n).transpose(0, 1, 3, 2))
    if fmt == "e4m3":
        words = by_word.astype(ml_dtypes.float8_e4m3fn).view(np.uint8)
    else:
        c = by_word.astype(ml_dtypes.float4_e2m1fn).view(np.uint8) & 0xF
        words = (c[..., 0::2] | (c[..., 1::2] << 4)).reshape(k // 512, 128, 2 * n)
    return np.ascontiguousarray(words), np.ascontiguousarray(byte.astype(np.uint8).reshape(k // 512, 16, n))


def unpack_weight(words, scales, fmt):
    g, _, n = scales.shape
    words = np.ascontiguousarray(words).reshape(g, 128, n, -1)
    if fmt == "e4m3":
        vals = words.view(ml_dtypes.float8_e4m3fn).astype(np.float64)
    else:
        nib = np.empty((g, 128, n, 4), np.uint8)
        nib[..., 0::2] = words & 0xF
        nib[..., 1::2] = words >> 4
        vals = E2M1[nib]
    vals = vals * np.repeat(np.exp2(scales.astype(np.float64) - 127.0), 8, axis=1)[..., None]
    return vals.transpose(0, 1, 3, 2).reshape(g * 512, n)


def gelu(v):
    return 0.5 * v * (1.0 + np.tanh(np.sqrt(2.0 / np.pi) * (v + 0.044715 * v**3)))


def striped8(idx):
    return np.concatenate([v.reshape(-1, 16).T for v in idx]).astype(np.uint16)


def unstriped8(offs):
    return np.stack([offs[16 * g:16 * g + 16].T.reshape(-1) for g in range(8)]).astype(np.int64)


def runs(v, idx8):
    k = np.arange(v.shape[0])
    return v[k[:, None], idx8[k % 512 // 64]]


K, M, H, N, T, S = 1024, 512, 1024, 512, 2048, 1024

def setup_inputs():
    n = np.random.standard_normal
    s = mx_kscale(K)[:, None]
    s2 = mx_kscale(M)[:, None]
    u = mx_kscale(H)[:, None]
    tab_words, tab_scales = pack_weight(np.abs(n((K, T))) * np.exp(1.0 * n((1, T))) * s, "e4m3")
    tab2_words, tab2_scales = pack_weight(np.abs(n((M, T))) * np.exp(0.8 * n((1, T))) * s2, "e4m3")
    wa = np.abs(n((K, H))) * (2.0 / K) * np.exp(0.5 * n((1, H))) / s
    w4_words, w4_scales = pack_weight(np.abs(n((M, H))) * (2.0 / M) * np.exp(0.5 * n((1, H))) / s2, "e2m1")
    wr = n((H, N)) / np.sqrt(H) / u
    w8_words, w8_scales = pack_weight(n((H, N)) / np.sqrt(H) / u, "e4m3")
    return {"tab_words": tab_words, "tab_scales": tab_scales,
            "offs": striped8(np.stack([np.random.permutation(T)[:S] for _ in range(8)])),
            "tab2_words": tab2_words, "tab2_scales": tab2_scales,
            "offs2": striped(np.random.permutation(T)[:S]),
            "wa": wa.astype(np.float32),
            "w4_words": w4_words, "w4_scales": w4_scales,
            "gain": (np.exp(0.3 * n(H)) * u[:, 0]).astype(np.float32),
            "wr": wr.astype(np.float32),
            "w8_words": w8_words, "w8_scales": w8_scales}

def reference(tab_words, tab_scales, offs, tab2_words, tab2_scales, offs2, wa, w4_words, w4_scales, gain, wr, w8_words, w8_scales):
    v = runs(unpack_weight(tab_words, tab_scales, "e4m3"), unstriped8(offs))
    v2 = unpack_weight(tab2_words, tab2_scales, "e4m3")[:, unstriped(offs2)]
    w4 = unpack_weight(w4_words, w4_scales, "e2m1")
    w8 = unpack_weight(w8_words, w8_scales, "e4m3")
    a = mxq(f64(wa), 0, "e4m3").T @ v
    b = w4.T @ v2
    d = np.log1p(a) - np.log1p(b)
    e = d * f64(gain)[:, None]
    sq = e * d
    return mxq(f64(wr), 0, "e4m3").T @ mxq(e, 0, "e4m3") + w8.T @ mxq(sq, 0, "e4m3")

@@ -1,0 +1,294 @@
+from contextlib import ExitStack
+
+import concourse.mybir as mybir
+
+K, M, H, N, T, S = 1024, 512, 1024, 512, 2048, 1024
+FLOPS = 2 * S * (K * H + M * H + 2 * H * N)
+
+F32 = mybir.dt.float32
+BF16 = mybir.dt.bfloat16
+I32 = mybir.dt.int32
+U32 = mybir.dt.uint32
+U16 = mybir.dt.uint16
+U8 = mybir.dt.uint8
+FP8X4 = mybir.dt.float8_e4m3fn_x4
+FP4X4 = mybir.dt.float4_e2m1fn_x4
+ACT = mybir.ActivationFunctionType
+ALU = mybir.AluOpType
+
+P = 128
+PACK = 4
+KP = P * PACK
+HALF = 512
+UNIT = 256
+
+
+def tile_list_metabolite_annotation_scores_kernel(
+    tc, tab_words, tab_scales, offs, tab2_words, tab2_scales, offs2, wa, w4_words, w4_scales,
+    gain, wr, w8_words, w8_scales, out,
+):
+    nc = tc.nc
+    with ExitStack() as ctx:
+        keep = ctx.enter_context(tc.tile_pool(name="keep", bufs=1))
+        stage = ctx.enter_context(tc.tile_pool(name="stage", bufs=3))
+        work = ctx.enter_context(tc.tile_pool(name="work", bufs=2))
+        psum = ctx.enter_context(tc.psum_pool(name="psum", bufs=4))
+
+        def kept(name, shape, dtype):
+            return keep.tile(shape, dtype, name=name, align_bytes=64)
+
+        list8 = keep.tile([P, S // 16], U16, name="list8")
+        list1 = keep.tile([P, S // 16], U16, name="list1")
+        tab2_sc = keep.tile([P, T], U8, name="tab2_sc", tag="raw1", align_bytes=64)
+        tab_sc = kept("tab_sc", [P, T], U8)
+        w4_sc_raw = kept("w4_sc_raw", [P, H], U8)
+        one = keep.tile([P, 1], F32, name="one", tag="raw0", align_bytes=64)
+        warm = keep.tile([P, 1], F32, name="warm", tag="tab_w0", align_bytes=64)
+
+        nc.vector.memset(tab2_sc[:].bitcast(I32), 0)
+        nc.gpsimd.memset(one[:], 1.0)
+        nc.gpsimd.memset(w4_sc_raw[:].bitcast(I32), 0)
+        nc.vector.memset(tab_sc[:].bitcast(I32), 0)
+
+        nc.sync.dma_start(list1[:], offs2)
+        nc.sync.dma_start(list8[:], offs)
+        for d in range(4):
+            nc.scalar.dma_start(out=tab2_sc[:].bitcast(I32)[32 * d : 32 * d + 4, :],
+                                in_=tab2_scales[0].bitcast(I32)[4 * d : 4 * d + 4, :])
+        nc.scalar.activation(out=warm[:], in_=one[:], func=ACT.Ln, bias=1.0)
+        w4_raw = keep.tile([P, 2 * H], U8, name="w4_raw", tag="tab_w1", align_bytes=64)
+        nc.sync.dma_start(out=w4_raw[:].bitcast(I32), in_=w4_words[0].bitcast(I32))
+        for d in range(4):
+            nc.gpsimd.dma_start(out=w4_sc_raw[:].bitcast(I32)[32 * d : 32 * d + 4, :],
+                                in_=w4_scales[0].bitcast(I32)[4 * d : 4 * d + 4, :])
+        for a in range(2):
+            for r in range(2):
+                nc.scalar.dma_start(out=tab_sc[:].bitcast(I32)[4 * a + r : P : 16, :],
+                                    in_=tab_scales[a].bitcast(I32)[r:16:2, :])
+
+        g = kept("g", [P, 2, PACK], F32)
+        nc.gpsimd.dma_start(out=g[:], in_=gain.rearrange("(b p t) -> p b t", b=2, t=PACK))
+
+        def load_words(name, src, width):
+            t = keep.tile([P, width], U32, name=name, tag=name, align_bytes=64)
+            nc.sync.dma_start(out=t[:].bitcast(I32), in_=src.rearrange("p t i -> p (t i)").bitcast(I32))
+            return t
+
+        def load_rows(name, src, tag):
+            t = keep.tile([P, PACK, HALF], F32, name=name, tag=tag, align_bytes=64)
+            nc.sync.dma_start(out=t[:], in_=src.rearrange("(p j) c -> p j c", j=PACK))
+            return t
+
+        wa_raw = {}
+        tab2_w = load_words("tab2_w", tab2_words[0], T)
+        wa_raw[0, 0] = load_rows("wa_raw00", wa[0:KP, 0:KP], "raw0")
+        tab_w = [load_words("tab_w0", tab_words[0], T)]
+
+        v2_sc = kept("v2_sc", [P, S], U8)
+        nc.vector.tensor_copy(v2_sc[:], tab2_sc[:].indirect(list1[:]))
+        wa_raw[1, 0] = load_rows("wa_raw10", wa[KP : 2 * KP, 0:KP], "raw1")
+        v2_w = []
+        for h in range(2):
+            v2_w.append(keep.tile([P, HALF], U32, name="v2_w%d" % h, tag="v2_w%d" % h, align_bytes=64))
+        nc.vector.tensor_copy(v2_w[0][:], tab2_w[:].indirect(list1[:, 0:32]))
+        w4_w = kept("w4_w", [P, 2 * H], U8)
+        nc.vector.tensor_copy(
+            out=w4_w[:].bitcast(U16).rearrange("p (b t m) -> p b m t", b=2, t=PACK),
+            in_=w4_raw[:].bitcast(U16).rearrange("p (b m t) -> p b m t", b=2, t=PACK))
+        w4_sc = kept("w4_sc", [P, H], U8)
+        nc.vector.tensor_copy(
+            out=w4_sc[:].rearrange("p (b t m) -> p b m t", b=2, t=PACK),
+            in_=w4_sc_raw[:].rearrange("p (b m t) -> p b m t", b=2, t=PACK))
+
+        tab_w.append(load_words("tab_w1", tab_words[1], T))
+        nc.vector.tensor_copy(v2_w[1][:], tab2_w[:].indirect(list1[:, 32:64]))
+
+        wa_w, wa_sc = {}, {}
+
+        def round_wa(a, b):
+            t = stage.tile([P, PACK * KP], BF16, name="rounded", align_bytes=64)
+            nc.scalar.copy(out=t[:].rearrange("p (t m j) -> p m j t", t=PACK, j=PACK),
+                           in_=wa_raw[a, b][:].rearrange("p j (m t) -> p m j t", t=PACK))
+            return t
+
+        def quantise(name, rounded):
+            w = kept(name + "_w", [P, KP], U32)
+            sc = kept(name + "_sc", [P, KP], U8)
+            nc.vector.quantize_mx(out=w[:].bitcast(FP8X4), scales=sc[:], in_=rounded[:])
+            return w, sc
+
+        log_b = {}
+
+        def library(b, h):
+            lb = kept("log_b%d%d" % (b, h), [P, PACK, HALF], F32)
+            for t in range(PACK):
+                c = (PACK * b + t) * P
+                bank = psum.tile([P, HALF], F32, name="first")
+                nc.tensor.matmul_mx(out=bank[:], lhsT=w4_w[:, 2 * c : 2 * (c + P)].bitcast(FP4X4),
+                                    lhsT_scale=w4_sc[:, c : c + P], rhs=v2_w[h][:].bitcast(FP8X4),
+                                    rhs_scale=v2_sc[:, h * HALF : (h + 1) * HALF], start=True, stop=True)
+                nc.scalar.activation(out=lb[:, t, :], in_=bank[:], func=ACT.Ln, bias=1.0)
+            log_b[b, h] = lb
+
+        rounded0 = [round_wa(a, 0) for a in range(2)]
+        library(0, 0)
+        wa_raw[0, 1] = load_rows("wa_raw01", wa[0:KP, KP : 2 * KP], "raw0")
+        wa_raw[1, 1] = load_rows("wa_raw11", wa[KP : 2 * KP, KP : 2 * KP], "tab2_w")
+        wr_raw = [load_rows("wr_raw0", wr[0:KP, :], "raw1")]
+
+        picked_sc = kept("picked_sc", [P, S], U8)
+        nc.vector.tensor_copy(picked_sc[:], tab_sc[:].indirect(list8[:]))
+        v_sc = kept("v_sc", [P, S], U8)
+        nc.vector.tensor_copy(v_sc[:].bitcast(I32), picked_sc[:].bitcast(I32))
+        for a in range(2):
+            for r in range(2):
+                nc.sync.dma_start(out=v_sc[:].bitcast(I32)[4 * a + 2 + r : P : 32, :],
+                                    in_=picked_sc[:].bitcast(I32)[16 + 4 * a + r : P : 32, :])
+        v_w = {}
+
+        def gather_sample(a, h):
+            t = kept("v_w%d%d" % (a, h), [P, HALF], U32)
+            nc.vector.tensor_copy(t[:], tab_w[a][:].indirect(list8[:, 32 * h : 32 * (h + 1)]))
+            v_w[a, h] = t
+
+        for h in range(2):
+            gather_sample(0, h)
+        wa_w[0, 0], wa_sc[0, 0] = quantise("wa00", rounded0[0])
+        gather_sample(1, 0)
+        wa_w[1, 0], wa_sc[1, 0] = quantise("wa10", rounded0[1])
+        library(0, 1)
+        gather_sample(1, 1)
+        wr_raw.append(load_rows("wr_raw1", wr[KP : 2 * KP, :], "tab_w0"))
+
+        diff, scaled, mixed, es_w, es_sc = {}, {}, {}, {}, {}
+
+        def front(b, j0, width):
+            h, off = divmod(j0, HALF)
+            per_bank = HALF // width
+            d = work.tile([P, PACK, width], F32, name="log_a", bufs=3)
+            for t0 in range(0, PACK, per_bank):
+                bank = psum.tile([P, per_bank, width], F32, name="first")
+                for u in range(per_bank):
+                    cols = slice((t0 + u) * P, (t0 + u + 1) * P)
+                    for a in range(2):
+                        nc.tensor.matmul_mx(
+                            out=bank[:, u, :], lhsT=wa_w[a, b][:, cols].bitcast(FP8X4),
+                            lhsT_scale=wa_sc[a, b][:, cols],
+                            rhs=v_w[a, h][:, off : off + width].bitcast(FP8X4),
+                            rhs_scale=v_sc[4 * a : P, j0 : j0 + width],
+                            start=(a == 0), stop=(a == 1))
+                nc.scalar.activation(out=d[:, t0 : t0 + per_bank, :], in_=bank[:], func=ACT.Ln, bias=1.0)
+            nc.vector.tensor_tensor(out=d[:], in0=d[:], in1=log_b[b, h][:, :, off : off + width], op=ALU.subtract)
+            e = work.tile([P, PACK, width], F32, name="scaled", bufs=3)
+            for t in range(PACK):
+                nc.scalar.activation(out=e[:, t, :], in_=d[:, t, :], func=ACT.Copy, scale=g[:, b, t : t + 1])
+            diff[b, j0], scaled[b, j0] = d, e
+
+        def back(b, j0, width):
+            both = work.tile([P, 2, width * PACK], BF16, name="both", align_bytes=64)
+            woven = "p (c i t) -> p c t i"
+            flat = "p t (c i) -> p c t i"
+            nc.vector.tensor_tensor(out=both[:, 1, :].rearrange(woven, i=4, t=PACK),
+                                    in0=scaled[b, j0][:].rearrange(flat, i=4),
+                                    in1=diff[b, j0][:].rearrange(flat, i=4), op=ALU.mult)
+            nc.vector.tensor_copy(out=both[:, 0, :].rearrange(woven, i=4, t=PACK),
+                                  in_=scaled[b, j0][:].rearrange(flat, i=4))
+            mixed[b, j0] = both
+
+        def quantise_unit(b, j0, width):
+            w = kept("es_w%d_%d" % (b, j0), [P, 2 * width], U32)
+            sc = kept("es_sc%d_%d" % (b, j0), [P, 2 * width], U8)
+            nc.vector.quantize_mx(out=w[:].bitcast(FP8X4), scales=sc[:],
+                                  in_=mixed[b, j0][:].rearrange("p s c -> p (s c)"))
+            es_w[b, j0], es_sc[b, j0] = w, sc
+
+        wr_w, wr_sc = {}, {}
+
+        def prepare_wr(b):
+            t = stage.tile([P, PACK * KP], BF16, name="rounded", align_bytes=64)
+            nc.vector.tensor_copy(out=t[:].rearrange("p (c i j) -> p c j i", i=4, j=PACK),
+                                  in_=wr_raw[b][:].rearrange("p j (c i) -> p c j i", i=4))
+            return t
+
+        banks = {}
+
+        def score_passes(b, q, j0, width, first, last):
+            src = (b, q * UNIT) if b == 0 else (b, j0)
+            full = UNIT if b == 0 else width
+            o = j0 - q * UNIT
+            for pair in range(2):
+                if first:
+                    banks[q, pair] = psum.tile([P, 2, UNIT], F32, name="second")
+                for u in range(2):
+                    nt = 2 * pair + u
+                    cols = slice(nt * P, (nt + 1) * P)
+                    dst = banks[q, pair][:, u, o : o + width]
+                    nc.tensor.matmul_mx(out=dst, lhsT=wr_w[b][:, cols].bitcast(FP8X4), lhsT_scale=wr_sc[b][:, cols],
+                                        rhs=es_w[src][:, 0:full].bitcast(FP8X4), rhs_scale=es_sc[src][:, 0:full],
+                                        start=(first and u == 0), stop=False)
+                    nc.tensor.matmul_mx(out=dst, lhsT=w8_w[:, b, cols].bitcast(FP8X4),
+                                        lhsT_scale=w8_sc[:, b * N + nt * P : b * N + (nt + 1) * P],
+                                        rhs=es_w[src][:, full : 2 * full].bitcast(FP8X4),
+                                        rhs_scale=es_sc[src][:, full : 2 * full],
+                                        start=False, stop=(last and u == 1))
+
+        def store(q, split):
+            rows = out.rearrange("(nt p) j -> p nt j", p=P)[:, :, q * UNIT : (q + 1) * UNIT]
+            res = [work.tile([P, 2, UNIT], F32, name="res%d" % pair) for pair in range(2)]
+            nc.scalar.copy(out=res[0][:], in_=banks[q, 0][:])
+            if split:
+                nc.vector.tensor_copy(out=res[1][:], in_=banks[q, 1][:])
+            else:
+                nc.scalar.copy(out=res[1][:], in_=banks[q, 1][:])
+            for pair in range(2):
+                nc.sync.dma_start(out=rows[:, 2 * pair : 2 * pair + 2, :], in_=res[pair][:])
+
+        quarters = S // UNIT
+        units = [(b, q * UNIT, UNIT) for b in range(2) for q in range(quarters)]
+        units = units[:-1] + [(1, S - UNIT, UNIT // 2), (1, S - UNIT // 2, UNIT // 2)]
+        pending = {}
+
+        def finish(b, j0, width):
+            quantise_unit(b, j0, width)
+            if b == 1:
+                q = j0 // UNIT
+                last = (j0 + width) % UNIT == 0
+                score_passes(1, q, j0, width, False, last)
+                if last:
+                    store(q, q == quarters - 1)
+
+        for step in range(len(units) + 1):
+            if step < len(units):
+                front(*units[step])
+            if 2 <= step < len(units):
+                finish(*units[step - 2])
+            if step >= 1:
+                back(*units[step - 1])
+                b, j0, width = units[step - 1]
+                if b == 1 and j0 % UNIT == 0:
+                    score_passes(0, j0 // UNIT, j0, UNIT, True, False)
+            if step == len(units):
+                finish(*units[step - 2])
+                finish(*units[step - 1])
+            if step == 0:
+                library(1, 0)
+            if step == 1:
+                pending[0] = round_wa(0, 1)
+                pending[1] = round_wa(1, 1)
+                library(1, 1)
+                w8_w = keep.tile([P, 2, N], U32, name="w8_w", tag="v2_w0", align_bytes=64)
+                nc.sync.dma_start(out=w8_w[:].bitcast(I32),
+                                  in_=w8_words.rearrange("b p n i -> p b (n i)").bitcast(I32))
+                w8_sc = keep.tile([P, 2 * N], U8, name="w8_sc", tag="v2_w1", align_bytes=64)
+                nc.vector.memset(w8_sc[:].bitcast(I32), 0)
+                for d in range(4):
+                    nc.sync.dma_start(
+                        out=w8_sc[:].bitcast(I32).rearrange("p (a n) -> p a n", a=2)[32 * d : 32 * d + 4],
+                        in_=w8_scales.bitcast(I32)[:, 4 * d : 4 * d + 4, :].rearrange("a r n -> r a n"))
+            if step == 2:
+                for a in range(2):
+                    wa_w[a, 1], wa_sc[a, 1] = quantise("wa%d1" % a, pending[a])
+            if step in (2, 3):
+                pending[step + 1] = prepare_wr(step - 2)
+            if step in (3, 4):
+                wr_w[step - 3], wr_sc[step - 3] = quantise("wr%d" % (step - 3), pending[step])

@@ -39,9 +39,9 @@ def tile_list_metabolite_annotation_scores_kernel(
 
         list8 = keep.tile([P, S // 16], U16, name="list8")
         list1 = keep.tile([P, S // 16], U16, name="list1")
-        tab2_sc = keep.tile([P, T], U8, name="tab2_sc", tag="raw1", align_bytes=64)
-        tab_sc = kept("tab_sc", [P, T], U8)
-        w4_sc_raw = kept("w4_sc_raw", [P, H], U8)
+        tab2_sc = keep.tile([P, T], U8, name="tab2_sc", tag="tab_w1", align_bytes=64)
+        tab_sc = keep.tile([P, T], U8, name="tab_sc", tag="raw2", align_bytes=64)
+        w4_sc_raw = keep.tile([P, H], U8, name="w4_sc_raw", tag="picked", align_bytes=64)
         one = keep.tile([P, 1], F32, name="one", tag="raw0", align_bytes=64)
         warm = keep.tile([P, 1], F32, name="warm", tag="tab_w0", align_bytes=64)
 
@@ -56,15 +56,13 @@ def tile_list_metabolite_annotation_scores_kernel(
             nc.scalar.dma_start(out=tab2_sc[:].bitcast(I32)[32 * d : 32 * d + 4, :],
                                 in_=tab2_scales[0].bitcast(I32)[4 * d : 4 * d + 4, :])
         nc.scalar.activation(out=warm[:], in_=one[:], func=ACT.Ln, bias=1.0)
-        w4_raw = keep.tile([P, 2 * H], U8, name="w4_raw", tag="tab_w1", align_bytes=64)
+        w4_raw = keep.tile([P, 2 * H], U8, name="w4_raw", tag="raw1", align_bytes=64)
         nc.sync.dma_start(out=w4_raw[:].bitcast(I32), in_=w4_words[0].bitcast(I32))
         for d in range(4):
-            nc.gpsimd.dma_start(out=w4_sc_raw[:].bitcast(I32)[32 * d : 32 * d + 4, :],
+            nc.scalar.dma_start(out=w4_sc_raw[:].bitcast(I32)[32 * d : 32 * d + 4, :],
                                 in_=w4_scales[0].bitcast(I32)[4 * d : 4 * d + 4, :])
         for a in range(2):
-            for r in range(2):
-                nc.scalar.dma_start(out=tab_sc[:].bitcast(I32)[4 * a + r : P : 16, :],
-                                    in_=tab_scales[a].bitcast(I32)[r:16:2, :])
+            nc.scalar.dma_start(out=tab_sc[:].bitcast(I32)[4 * a : P : 8, :], in_=tab_scales[a].bitcast(I32))
 
         g = kept("g", [P, 2, PACK], F32)
         nc.gpsimd.dma_start(out=g[:], in_=gain.rearrange("(b p t) -> p b t", b=2, t=PACK))
@@ -86,7 +84,6 @@ def tile_list_metabolite_annotation_scores_kernel(
 
         v2_sc = kept("v2_sc", [P, S], U8)
         nc.vector.tensor_copy(v2_sc[:], tab2_sc[:].indirect(list1[:]))
-        wa_raw[1, 0] = load_rows("wa_raw10", wa[KP : 2 * KP, 0:KP], "raw1")
         v2_w = []
         for h in range(2):
             v2_w.append(keep.tile([P, HALF], U32, name="v2_w%d" % h, tag="v2_w%d" % h, align_bytes=64))
@@ -95,12 +92,21 @@ def tile_list_metabolite_annotation_scores_kernel(
         nc.vector.tensor_copy(
             out=w4_w[:].bitcast(U16).rearrange("p (b t m) -> p b m t", b=2, t=PACK),
             in_=w4_raw[:].bitcast(U16).rearrange("p (b m t) -> p b m t", b=2, t=PACK))
+        wa_raw[1, 0] = load_rows("wa_raw10", wa[KP : 2 * KP, 0:KP], "raw1")
         w4_sc = kept("w4_sc", [P, H], U8)
         nc.vector.tensor_copy(
             out=w4_sc[:].rearrange("p (b t m) -> p b m t", b=2, t=PACK),
             in_=w4_sc_raw[:].rearrange("p (b m t) -> p b m t", b=2, t=PACK))
 
         tab_w.append(load_words("tab_w1", tab_words[1], T))
+        picked_sc = keep.tile([P, S], U8, name="picked_sc", tag="picked", align_bytes=64)
+        nc.vector.tensor_copy(picked_sc[:], tab_sc[:].indirect(list8[:]))
+        v_sc = kept("v_sc", [P, S], U8)
+        nc.vector.tensor_copy(v_sc[:].bitcast(I32), picked_sc[:].bitcast(I32))
+        for a in range(2):
+            for r in range(1, 4):
+                nc.sync.dma_start(out=v_sc[:].bitcast(I32)[4 * a + r : P : 32, :],
+                                  in_=picked_sc[:].bitcast(I32)[4 * a + 8 * r : P : 32, :])
         nc.vector.tensor_copy(v2_w[1][:], tab2_w[:].indirect(list1[:, 32:64]))
 
         wa_w, wa_sc = {}, {}
@@ -120,7 +126,8 @@ def tile_list_metabolite_annotation_scores_kernel(
         log_b = {}
 
         def library(b, h):
-            lb = kept("log_b%d%d" % (b, h), [P, PACK, HALF], F32)
+            name = "log_b%d%d" % (b, h)
+            lb = keep.tile([P, PACK, HALF], F32, name=name, tag="raw0" if (b, h) == (0, 0) else name, align_bytes=64)
             for t in range(PACK):
                 c = (PACK * b + t) * P
                 bank = psum.tile([P, HALF], F32, name="first")
@@ -132,18 +139,10 @@ def tile_list_metabolite_annotation_scores_kernel(
 
         rounded0 = [round_wa(a, 0) for a in range(2)]
         library(0, 0)
-        wa_raw[0, 1] = load_rows("wa_raw01", wa[0:KP, KP : 2 * KP], "raw0")
+        wa_raw[0, 1] = load_rows("wa_raw01", wa[0:KP, KP : 2 * KP], "raw2")
         wa_raw[1, 1] = load_rows("wa_raw11", wa[KP : 2 * KP, KP : 2 * KP], "tab2_w")
         wr_raw = [load_rows("wr_raw0", wr[0:KP, :], "raw1")]
 
-        picked_sc = kept("picked_sc", [P, S], U8)
-        nc.vector.tensor_copy(picked_sc[:], tab_sc[:].indirect(list8[:]))
-        v_sc = kept("v_sc", [P, S], U8)
-        nc.vector.tensor_copy(v_sc[:].bitcast(I32), picked_sc[:].bitcast(I32))
-        for a in range(2):
-            for r in range(2):
-                nc.sync.dma_start(out=v_sc[:].bitcast(I32)[4 * a + 2 + r : P : 32, :],
-                                    in_=picked_sc[:].bitcast(I32)[16 + 4 * a + r : P : 32, :])
         v_w = {}
 
         def gather_sample(a, h):

@@ -21,6 +21,12 @@ PACK = 4
 KP = P * PACK
 HALF = 512
 UNIT = 256
+ON_VECTOR = 1
+FIRST_S = 0
+LAST_S = 2
+WR_V = 2
+LIB0 = 2
+LIB1 = 3
 
 
 def tile_list_metabolite_annotation_scores_kernel(
@@ -40,32 +46,33 @@ def tile_list_metabolite_annotation_scores_kernel(
         list8 = keep.tile([P, S // 16], U16, name="list8")
         list1 = keep.tile([P, S // 16], U16, name="list1")
         tab2_sc = keep.tile([P, T], U8, name="tab2_sc", tag="tab_w1", align_bytes=64)
-        tab_sc = keep.tile([P, T], U8, name="tab_sc", tag="raw2", align_bytes=64)
-        w4_sc_raw = keep.tile([P, H], U8, name="w4_sc_raw", tag="picked", align_bytes=64)
-        one = keep.tile([P, 1], F32, name="one", tag="raw0", align_bytes=64)
+        w4_sc_raw = kept("w4_sc_raw", [P, H], U8)
+        tab_sc = kept("tab_sc", [P, T], U8)
+        one = kept("one", [P, 1], F32)
         warm = keep.tile([P, 1], F32, name="warm", tag="tab_w0", align_bytes=64)
 
-        nc.vector.memset(tab2_sc[:].bitcast(I32), 0)
-        nc.gpsimd.memset(one[:], 1.0)
-        nc.gpsimd.memset(w4_sc_raw[:].bitcast(I32), 0)
+        nc.gpsimd.memset(tab2_sc[:].bitcast(I32), 0)
         nc.vector.memset(tab_sc[:].bitcast(I32), 0)
+        nc.vector.memset(w4_sc_raw[:].bitcast(I32), 0)
+        nc.vector.memset(one[:], 1.0)
 
         nc.sync.dma_start(list1[:], offs2)
-        nc.sync.dma_start(list8[:], offs)
         for d in range(4):
-            nc.scalar.dma_start(out=tab2_sc[:].bitcast(I32)[32 * d : 32 * d + 4, :],
-                                in_=tab2_scales[0].bitcast(I32)[4 * d : 4 * d + 4, :])
-        nc.scalar.activation(out=warm[:], in_=one[:], func=ACT.Ln, bias=1.0)
+            nc.sync.dma_start(out=tab2_sc[:].bitcast(I32)[32 * d : 32 * d + 4, :],
+                              in_=tab2_scales[0].bitcast(I32)[4 * d : 4 * d + 4, :])
+        nc.sync.dma_start(list8[:], offs)
         w4_raw = keep.tile([P, 2 * H], U8, name="w4_raw", tag="raw1", align_bytes=64)
-        nc.sync.dma_start(out=w4_raw[:].bitcast(I32), in_=w4_words[0].bitcast(I32))
+        for b in range(2):
+            cols = slice(b * KP // 2, (b + 1) * KP // 2)
+            nc.sync.dma_start(out=w4_raw[:].bitcast(I32)[:, cols], in_=w4_words[0].bitcast(I32)[:, cols])
+        g = kept("g", [P, 2, PACK], F32)
+        nc.gpsimd.dma_start(out=g[:], in_=gain.rearrange("(b p t) -> p b t", b=2, t=PACK))
+        for a in range(2):
+            nc.scalar.dma_start(out=tab_sc[:].bitcast(I32)[4 * a : P : 8, :], in_=tab_scales[a].bitcast(I32))
         for d in range(4):
             nc.scalar.dma_start(out=w4_sc_raw[:].bitcast(I32)[32 * d : 32 * d + 4, :],
                                 in_=w4_scales[0].bitcast(I32)[4 * d : 4 * d + 4, :])
-        for a in range(2):
-            nc.scalar.dma_start(out=tab_sc[:].bitcast(I32)[4 * a : P : 8, :], in_=tab_scales[a].bitcast(I32))
-
-        g = kept("g", [P, 2, PACK], F32)
-        nc.gpsimd.dma_start(out=g[:], in_=gain.rearrange("(b p t) -> p b t", b=2, t=PACK))
+        nc.scalar.activation(out=warm[:], in_=one[:], func=ACT.Ln, bias=1.0)
 
         def load_words(name, src, width):
             t = keep.tile([P, width], U32, name=name, tag=name, align_bytes=64)
@@ -127,10 +134,10 @@ def tile_list_metabolite_annotation_scores_kernel(
 
         def library(b, h):
             name = "log_b%d%d" % (b, h)
-            lb = keep.tile([P, PACK, HALF], F32, name=name, tag="raw0" if (b, h) == (0, 0) else name, align_bytes=64)
+            lb = keep.tile([P, PACK, HALF], F32, name=name, tag={(0, 0): "raw0", (0, 1): "tab2_w"}.get((b, h), name), align_bytes=64)
             for t in range(PACK):
                 c = (PACK * b + t) * P
-                bank = psum.tile([P, HALF], F32, name="first")
+                bank = psum.tile([P, HALF], F32, name="second")
                 nc.tensor.matmul_mx(out=bank[:], lhsT=w4_w[:, 2 * c : 2 * (c + P)].bitcast(FP4X4),
                                     lhsT_scale=w4_sc[:, c : c + P], rhs=v2_w[h][:].bitcast(FP8X4),
                                     rhs_scale=v2_sc[:, h * HALF : (h + 1) * HALF], start=True, stop=True)
@@ -139,9 +146,7 @@ def tile_list_metabolite_annotation_scores_kernel(
 
         rounded0 = [round_wa(a, 0) for a in range(2)]
         library(0, 0)
-        wa_raw[0, 1] = load_rows("wa_raw01", wa[0:KP, KP : 2 * KP], "raw2")
-        wa_raw[1, 1] = load_rows("wa_raw11", wa[KP : 2 * KP, KP : 2 * KP], "tab2_w")
-        wr_raw = [load_rows("wr_raw0", wr[0:KP, :], "raw1")]
+        wr_raw = [load_rows("wr_raw0", wr[0:KP, :], "raw1"), load_rows("wr_raw1", wr[KP : 2 * KP, :], "picked")]
 
         v_w = {}
 
@@ -150,21 +155,22 @@ def tile_list_metabolite_annotation_scores_kernel(
             nc.vector.tensor_copy(t[:], tab_w[a][:].indirect(list8[:, 32 * h : 32 * (h + 1)]))
             v_w[a, h] = t
 
-        for h in range(2):
-            gather_sample(0, h)
+        gather_sample(0, 0)
         wa_w[0, 0], wa_sc[0, 0] = quantise("wa00", rounded0[0])
         gather_sample(1, 0)
         wa_w[1, 0], wa_sc[1, 0] = quantise("wa10", rounded0[1])
         library(0, 1)
-        gather_sample(1, 1)
-        wr_raw.append(load_rows("wr_raw1", wr[KP : 2 * KP, :], "tab_w0"))
+        for a in range(2):
+            gather_sample(a, 1)
+        for a in range(2):
+            wa_raw[a, 1] = load_rows("wa_raw%d1" % a, wa[a * KP : (a + 1) * KP, KP : 2 * KP], "tab_w%d" % a)
 
         diff, scaled, mixed, es_w, es_sc = {}, {}, {}, {}, {}
 
-        def front(b, j0, width):
+        def logs(b, j0, width):
             h, off = divmod(j0, HALF)
             per_bank = HALF // width
-            d = work.tile([P, PACK, width], F32, name="log_a", bufs=3)
+            d = work.tile([P, PACK, width], F32, name="log_a", bufs=4)
             for t0 in range(0, PACK, per_bank):
                 bank = psum.tile([P, per_bank, width], F32, name="first")
                 for u in range(per_bank):
@@ -177,11 +183,20 @@ def tile_list_metabolite_annotation_scores_kernel(
                             rhs_scale=v_sc[4 * a : P, j0 : j0 + width],
                             start=(a == 0), stop=(a == 1))
                 nc.scalar.activation(out=d[:, t0 : t0 + per_bank, :], in_=bank[:], func=ACT.Ln, bias=1.0)
+            diff[b, j0] = d
+
+        def differences(b, j0, width):
+            h, off = divmod(j0, HALF)
+            d = diff[b, j0]
             nc.vector.tensor_tensor(out=d[:], in0=d[:], in1=log_b[b, h][:, :, off : off + width], op=ALU.subtract)
             e = work.tile([P, PACK, width], F32, name="scaled", bufs=3)
             for t in range(PACK):
-                nc.scalar.activation(out=e[:, t, :], in_=d[:, t, :], func=ACT.Copy, scale=g[:, b, t : t + 1])
-            diff[b, j0], scaled[b, j0] = d, e
+                if b == 0 and j0 < ON_VECTOR * UNIT:
+                    nc.vector.tensor_scalar(out=e[:, t, :], in0=d[:, t, :], scalar1=g[:, b, t : t + 1], scalar2=None,
+                                            op0=ALU.mult)
+                else:
+                    nc.scalar.activation(out=e[:, t, :], in_=d[:, t, :], func=ACT.Copy, scale=g[:, b, t : t + 1])
+            scaled[b, j0] = e
 
         def back(b, j0, width):
             both = work.tile([P, 2, width * PACK], BF16, name="both", align_bytes=64)
@@ -190,8 +205,8 @@ def tile_list_metabolite_annotation_scores_kernel(
             nc.vector.tensor_tensor(out=both[:, 1, :].rearrange(woven, i=4, t=PACK),
                                     in0=scaled[b, j0][:].rearrange(flat, i=4),
                                     in1=diff[b, j0][:].rearrange(flat, i=4), op=ALU.mult)
-            nc.vector.tensor_copy(out=both[:, 0, :].rearrange(woven, i=4, t=PACK),
-                                  in_=scaled[b, j0][:].rearrange(flat, i=4))
+            copy = nc.scalar.copy if b == 1 and FIRST_S * UNIT <= j0 < LAST_S * UNIT else nc.vector.tensor_copy
+            copy(out=both[:, 0, :].rearrange(woven, i=4, t=PACK), in_=scaled[b, j0][:].rearrange(flat, i=4))
             mixed[b, j0] = both
 
         def quantise_unit(b, j0, width):
@@ -204,8 +219,9 @@ def tile_list_metabolite_annotation_scores_kernel(
         wr_w, wr_sc = {}, {}
 
         def prepare_wr(b):
-            t = stage.tile([P, PACK * KP], BF16, name="rounded", align_bytes=64)
-            nc.vector.tensor_copy(out=t[:].rearrange("p (c i j) -> p c j i", i=4, j=PACK),
+            t = keep.tile([P, PACK * KP], BF16, name="wr_rounded", tag=["raw0", "tab2_w"][b], align_bytes=64)
+            copy = nc.scalar.copy if b >= WR_V else nc.vector.tensor_copy
+            copy(out=t[:].rearrange("p (c i j) -> p c j i", i=4, j=PACK),
                                   in_=wr_raw[b][:].rearrange("p j (c i) -> p c j i", i=4))
             return t
 
@@ -217,7 +233,7 @@ def tile_list_metabolite_annotation_scores_kernel(
             o = j0 - q * UNIT
             for pair in range(2):
                 if first:
-                    banks[q, pair] = psum.tile([P, 2, UNIT], F32, name="second")
+                    banks[q, pair] = psum.tile([P, 2, UNIT], F32, name="first" if q == S // UNIT - 1 else "second")
                 for u in range(2):
                     nt = 2 * pair + u
                     cols = slice(nt * P, (nt + 1) * P)
@@ -247,47 +263,46 @@ def tile_list_metabolite_annotation_scores_kernel(
         units = units[:-1] + [(1, S - UNIT, UNIT // 2), (1, S - UNIT // 2, UNIT // 2)]
         pending = {}
 
-        def finish(b, j0, width):
-            quantise_unit(b, j0, width)
-            if b == 1:
-                q = j0 // UNIT
-                last = (j0 + width) % UNIT == 0
-                score_passes(1, q, j0, width, False, last)
-                if last:
-                    store(q, q == quarters - 1)
+        def scores(b, j0, width):
+            q = j0 // UNIT
+            last = (j0 + width) % UNIT == 0
+            score_passes(1, q, j0, width, False, last)
+            if last:
+                store(q, q == quarters - 1)
 
-        for step in range(len(units) + 1):
-            if step < len(units):
-                front(*units[step])
-            if 2 <= step < len(units):
-                finish(*units[step - 2])
-            if step >= 1:
+        n = len(units)
+        logs(*units[0])
+        for step in range(n + 2):
+            if step + 1 < n:
+                logs(*units[step + 1])
+            if step < n:
+                differences(*units[step])
+            if step >= 2:
+                quantise_unit(*units[step - 2])
+            if 1 <= step <= n:
                 back(*units[step - 1])
                 b, j0, width = units[step - 1]
                 if b == 1 and j0 % UNIT == 0:
                     score_passes(0, j0 // UNIT, j0, UNIT, True, False)
-            if step == len(units):
-                finish(*units[step - 2])
-                finish(*units[step - 1])
-            if step == 0:
-                library(1, 0)
-            if step == 1:
-                pending[0] = round_wa(0, 1)
-                pending[1] = round_wa(1, 1)
-                library(1, 1)
+            if step >= 2 and units[step - 2][0] == 1:
+                scores(*units[step - 2])
+            if step in (0, 1):
+                pending[step] = round_wa(step, 1)
+            if step in (1, 2):
+                wa_w[step - 1, 1], wa_sc[step - 1, 1] = quantise("wa%d1" % (step - 1), pending[step - 1])
+            if step in (LIB0, LIB1):
+                library(1, 0 if step == LIB0 else 1)
+            if step == LIB1:
                 w8_w = keep.tile([P, 2, N], U32, name="w8_w", tag="v2_w0", align_bytes=64)
                 nc.sync.dma_start(out=w8_w[:].bitcast(I32),
                                   in_=w8_words.rearrange("b p n i -> p b (n i)").bitcast(I32))
-                w8_sc = keep.tile([P, 2 * N], U8, name="w8_sc", tag="v2_w1", align_bytes=64)
+                w8_sc = keep.tile([P, 2 * N], U8, name="w8_sc", tag="v2_sc", align_bytes=64)
                 nc.vector.memset(w8_sc[:].bitcast(I32), 0)
                 for d in range(4):
                     nc.sync.dma_start(
                         out=w8_sc[:].bitcast(I32).rearrange("p (a n) -> p a n", a=2)[32 * d : 32 * d + 4],
                         in_=w8_scales.bitcast(I32)[:, 4 * d : 4 * d + 4, :].rearrange("a r n -> r a n"))
-            if step == 2:
-                for a in range(2):
-                    wa_w[a, 1], wa_sc[a, 1] = quantise("wa%d1" % a, pending[a])
-            if step in (2, 3):
-                pending[step + 1] = prepare_wr(step - 2)
-            if step in (3, 4):
-                wr_w[step - 3], wr_sc[step - 3] = quantise("wr%d" % (step - 3), pending[step])
+            if step in (2, 4):
+                pending[step + 1] = prepare_wr(step // 2 - 1)
+            if step in (3, 5):
+                wr_w[step // 2 - 1], wr_sc[step // 2 - 1] = quantise("wr%d" % (step // 2 - 1), pending[step])

@@ -17,16 +17,13 @@ ACT = mybir.ActivationFunctionType
 ALU = mybir.AluOpType
 
 P = 128
-PACK = 4
-KP = P * PACK
+SLOTS = 4
+PASS = P * SLOTS
+QUADRANT = 32
 HALF = 512
 UNIT = 256
-ON_VECTOR = 1
-FIRST_S = 0
-LAST_S = 2
-WR_V = 2
-LIB0 = 2
-LIB1 = 3
+LINE = 4
+GAIN_ON_VECTOR = 2
 
 
 def tile_list_metabolite_annotation_scores_kernel(
@@ -40,269 +37,242 @@ def tile_list_metabolite_annotation_scores_kernel(
         work = ctx.enter_context(tc.tile_pool(name="work", bufs=2))
         psum = ctx.enter_context(tc.psum_pool(name="psum", bufs=4))
 
-        def kept(name, shape, dtype):
-            return keep.tile(shape, dtype, name=name, align_bytes=64)
+        def kept(name, shape, dtype, buffer=None):
+            return keep.tile(shape, dtype, name=name, tag=buffer or name, align_bytes=64)
+
+        def as_words(ap):
+            return ap.bitcast(I32)
 
         list8 = keep.tile([P, S // 16], U16, name="list8")
         list1 = keep.tile([P, S // 16], U16, name="list1")
-        tab2_sc = keep.tile([P, T], U8, name="tab2_sc", tag="tab_w1", align_bytes=64)
+        tab2_sc = kept("tab2_sc", [P, T], U8)
         w4_sc_raw = kept("w4_sc_raw", [P, H], U8)
         tab_sc = kept("tab_sc", [P, T], U8)
+        w4_raw = kept("w4_raw", [P, 2 * H], U8)
         one = kept("one", [P, 1], F32)
-        warm = keep.tile([P, 1], F32, name="warm", tag="tab_w0", align_bytes=64)
+        warm = kept("warm", [P, 1], F32)
 
-        nc.gpsimd.memset(tab2_sc[:].bitcast(I32), 0)
-        nc.vector.memset(tab_sc[:].bitcast(I32), 0)
-        nc.vector.memset(w4_sc_raw[:].bitcast(I32), 0)
+        nc.gpsimd.memset(as_words(tab2_sc[:]), 0)
+        nc.vector.memset(as_words(tab_sc[:]), 0)
+        nc.vector.memset(as_words(w4_sc_raw[:]), 0)
         nc.vector.memset(one[:], 1.0)
 
-        nc.sync.dma_start(list1[:], offs2)
-        for d in range(4):
-            nc.sync.dma_start(out=tab2_sc[:].bitcast(I32)[32 * d : 32 * d + 4, :],
-                              in_=tab2_scales[0].bitcast(I32)[4 * d : 4 * d + 4, :])
-        nc.sync.dma_start(list8[:], offs)
-        w4_raw = keep.tile([P, 2 * H], U8, name="w4_raw", tag="raw1", align_bytes=64)
-        for b in range(2):
-            cols = slice(b * KP // 2, (b + 1) * KP // 2)
-            nc.sync.dma_start(out=w4_raw[:].bitcast(I32)[:, cols], in_=w4_words[0].bitcast(I32)[:, cols])
-        g = kept("g", [P, 2, PACK], F32)
-        nc.gpsimd.dma_start(out=g[:], in_=gain.rearrange("(b p t) -> p b t", b=2, t=PACK))
-        for a in range(2):
-            nc.scalar.dma_start(out=tab_sc[:].bitcast(I32)[4 * a : P : 8, :], in_=tab_scales[a].bitcast(I32))
-        for d in range(4):
-            nc.scalar.dma_start(out=w4_sc_raw[:].bitcast(I32)[32 * d : 32 * d + 4, :],
-                                in_=w4_scales[0].bitcast(I32)[4 * d : 4 * d + 4, :])
+        def load_plane(queue, plane, rows):
+            for d in range(4):
+                queue.dma_start(out=plane[QUADRANT * d : QUADRANT * d + 4], in_=rows(slice(4 * d, 4 * d + 4)))
+
+        def load_table(name, words, buffer):
+            tile = kept(name, [P, T], U32, buffer)
+            nc.sync.dma_start(out=as_words(tile[:]), in_=as_words(words.rearrange("p t i -> p (t i)")))
+            return tile
+
+        def load_rows(name, rows, buffer):
+            tile = kept(name, [P, SLOTS, PASS], F32, buffer)
+            nc.sync.dma_start(out=tile[:], in_=rows.rearrange("(p j) c -> p j c", j=SLOTS))
+            return tile
+
+        def load_wa(kp, rb, buffer):
+            return load_rows("wa_raw%d%d" % (kp, rb), wa[kp * PASS : (kp + 1) * PASS, rb * PASS : (rb + 1) * PASS], buffer)
+
+        def gather_words(name, table, offsets, h):
+            tile = kept(name, [P, HALF], U32)
+            nc.vector.tensor_copy(tile[:], table[:].indirect(offsets[:, h * HALF // 16 : (h + 1) * HALF // 16]))
+            return tile
+
+        for kp in range(2):
+            nc.scalar.dma_start(out=as_words(tab_sc[:])[4 * kp : P : 8, :], in_=as_words(tab_scales[kp]))
         nc.scalar.activation(out=warm[:], in_=one[:], func=ACT.Ln, bias=1.0)
 
-        def load_words(name, src, width):
-            t = keep.tile([P, width], U32, name=name, tag=name, align_bytes=64)
-            nc.sync.dma_start(out=t[:].bitcast(I32), in_=src.rearrange("p t i -> p (t i)").bitcast(I32))
-            return t
-
-        def load_rows(name, src, tag):
-            t = keep.tile([P, PACK, HALF], F32, name=name, tag=tag, align_bytes=64)
-            nc.sync.dma_start(out=t[:], in_=src.rearrange("(p j) c -> p j c", j=PACK))
-            return t
-
         wa_raw = {}
-        tab2_w = load_words("tab2_w", tab2_words[0], T)
-        wa_raw[0, 0] = load_rows("wa_raw00", wa[0:KP, 0:KP], "raw0")
-        tab_w = [load_words("tab_w0", tab_words[0], T)]
+        nc.sync.dma_start(list1[:], offs2)
+        nc.sync.dma_start(out=as_words(w4_raw[:]), in_=as_words(w4_words[0]))
+        load_plane(nc.sync, as_words(tab2_sc[:]), lambda q: as_words(tab2_scales[0])[q, :])
+        tab2_w = load_table("tab2_w", tab2_words[0], None)
+        load_plane(nc.sync, as_words(w4_sc_raw[:]), lambda q: as_words(w4_scales[0])[q, :])
+        wa_raw[0, 0] = load_wa(0, 0, "rows0")
+        nc.sync.dma_start(list8[:], offs)
+        wa_raw[1, 0] = load_wa(1, 0, "rows1")
+        tab_w = [load_table("tab_w%d" % kp, tab_words[kp], "table%d" % kp) for kp in range(2)]
+        gains = kept("gains", [P, 2, SLOTS], F32)
+        nc.gpsimd.dma_start(out=gains[:], in_=gain.rearrange("(b p t) -> p b t", b=2, t=SLOTS))
 
         v2_sc = kept("v2_sc", [P, S], U8)
         nc.vector.tensor_copy(v2_sc[:], tab2_sc[:].indirect(list1[:]))
-        v2_w = []
-        for h in range(2):
-            v2_w.append(keep.tile([P, HALF], U32, name="v2_w%d" % h, tag="v2_w%d" % h, align_bytes=64))
-        nc.vector.tensor_copy(v2_w[0][:], tab2_w[:].indirect(list1[:, 0:32]))
+        v2_w = [gather_words("v2_w0", tab2_w, list1, 0)]
+        by_slot, by_channel = "p (b t m) -> p b m t", "p (b m t) -> p b m t"
         w4_w = kept("w4_w", [P, 2 * H], U8)
-        nc.vector.tensor_copy(
-            out=w4_w[:].bitcast(U16).rearrange("p (b t m) -> p b m t", b=2, t=PACK),
-            in_=w4_raw[:].bitcast(U16).rearrange("p (b m t) -> p b m t", b=2, t=PACK))
-        wa_raw[1, 0] = load_rows("wa_raw10", wa[KP : 2 * KP, 0:KP], "raw1")
+        nc.vector.tensor_copy(out=w4_w[:].bitcast(U16).rearrange(by_slot, b=2, t=SLOTS),
+                              in_=w4_raw[:].bitcast(U16).rearrange(by_channel, b=2, t=SLOTS))
         w4_sc = kept("w4_sc", [P, H], U8)
-        nc.vector.tensor_copy(
-            out=w4_sc[:].rearrange("p (b t m) -> p b m t", b=2, t=PACK),
-            in_=w4_sc_raw[:].rearrange("p (b m t) -> p b m t", b=2, t=PACK))
+        nc.vector.tensor_copy(out=w4_sc[:].rearrange(by_slot, b=2, t=SLOTS),
+                              in_=w4_sc_raw[:].rearrange(by_channel, b=2, t=SLOTS))
 
-        tab_w.append(load_words("tab_w1", tab_words[1], T))
-        picked_sc = keep.tile([P, S], U8, name="picked_sc", tag="picked", align_bytes=64)
+        picked_sc = kept("picked_sc", [P, S], U8, "rows2")
         nc.vector.tensor_copy(picked_sc[:], tab_sc[:].indirect(list8[:]))
         v_sc = kept("v_sc", [P, S], U8)
-        nc.vector.tensor_copy(v_sc[:].bitcast(I32), picked_sc[:].bitcast(I32))
-        for a in range(2):
+        nc.vector.tensor_copy(as_words(v_sc[:]), as_words(picked_sc[:]))
+        for kp in range(2):
             for r in range(1, 4):
-                nc.sync.dma_start(out=v_sc[:].bitcast(I32)[4 * a + r : P : 32, :],
-                                  in_=picked_sc[:].bitcast(I32)[4 * a + 8 * r : P : 32, :])
-        nc.vector.tensor_copy(v2_w[1][:], tab2_w[:].indirect(list1[:, 32:64]))
+                nc.sync.dma_start(out=as_words(v_sc[:])[4 * kp + r : P : QUADRANT, :],
+                                  in_=as_words(picked_sc[:])[4 * kp + 8 * r : P : QUADRANT, :])
+        v2_w.append(gather_words("v2_w1", tab2_w, list1, 1))
 
-        wa_w, wa_sc = {}, {}
+        def round_wa(kp, rb):
+            rounded = stage.tile([P, SLOTS * PASS], BF16, name="wa_rounded", align_bytes=64)
+            nc.scalar.copy(out=rounded[:].rearrange("p (t m j) -> p m j t", t=SLOTS, j=SLOTS),
+                           in_=wa_raw[kp, rb][:].rearrange("p j (m t) -> p m j t", t=SLOTS))
+            return rounded
 
-        def round_wa(a, b):
-            t = stage.tile([P, PACK * KP], BF16, name="rounded", align_bytes=64)
-            nc.scalar.copy(out=t[:].rearrange("p (t m j) -> p m j t", t=PACK, j=PACK),
-                           in_=wa_raw[a, b][:].rearrange("p j (m t) -> p m j t", t=PACK))
-            return t
+        def round_wr(rb, buffer):
+            rounded = kept("wr_rounded%d" % rb, [P, SLOTS * N], BF16, buffer)
+            nc.vector.tensor_copy(out=rounded[:].rearrange("p (c i j) -> p c j i", i=LINE, j=SLOTS),
+                                  in_=wr_raw[rb][:].rearrange("p j (c i) -> p c j i", i=LINE))
+            return rounded
 
-        def quantise(name, rounded):
-            w = kept(name + "_w", [P, KP], U32)
-            sc = kept(name + "_sc", [P, KP], U8)
-            nc.vector.quantize_mx(out=w[:].bitcast(FP8X4), scales=sc[:], in_=rounded[:])
-            return w, sc
+        def quantise(name, rounded, columns):
+            words = kept(name + "_w", [P, columns], U32)
+            plane = kept(name + "_sc", [P, columns], U8)
+            nc.vector.quantize_mx(out=words[:].bitcast(FP8X4), scales=plane[:], in_=rounded)
+            return words, plane
 
         log_b = {}
 
-        def library(b, h):
-            name = "log_b%d%d" % (b, h)
-            lb = keep.tile([P, PACK, HALF], F32, name=name, tag={(0, 0): "raw0", (0, 1): "tab2_w"}.get((b, h), name), align_bytes=64)
-            for t in range(PACK):
-                c = (PACK * b + t) * P
-                bank = psum.tile([P, HALF], F32, name="second")
+        def library_logs(rb, h, buffer=None, banks_of="other"):
+            log_b[rb, h] = kept("log_b%d%d" % (rb, h), [P, SLOTS, HALF], F32, buffer)
+            for t in range(SLOTS):
+                c = (SLOTS * rb + t) * P
+                bank = psum.tile([P, HALF], F32, name=banks_of)
                 nc.tensor.matmul_mx(out=bank[:], lhsT=w4_w[:, 2 * c : 2 * (c + P)].bitcast(FP4X4),
                                     lhsT_scale=w4_sc[:, c : c + P], rhs=v2_w[h][:].bitcast(FP8X4),
                                     rhs_scale=v2_sc[:, h * HALF : (h + 1) * HALF], start=True, stop=True)
-                nc.scalar.activation(out=lb[:, t, :], in_=bank[:], func=ACT.Ln, bias=1.0)
-            log_b[b, h] = lb
+                nc.scalar.activation(out=log_b[rb, h][:, t, :], in_=bank[:], func=ACT.Ln, bias=1.0)
 
-        rounded0 = [round_wa(a, 0) for a in range(2)]
-        library(0, 0)
-        wr_raw = [load_rows("wr_raw0", wr[0:KP, :], "raw1"), load_rows("wr_raw1", wr[KP : 2 * KP, :], "picked")]
+        wa_rounded = {(kp, 0): round_wa(kp, 0) for kp in range(2)}
+        library_logs(0, 0, "rows0")
+        wr_raw = [load_rows("wr_raw0", wr[0:PASS, :], "rows2")]
 
-        v_w = {}
+        wa_q, wr_q, v_w = {}, {}, {}
+        for kp in range(2):
+            v_w[kp, 0] = gather_words("v_w%d0" % kp, tab_w[kp], list8, 0)
+            wa_q[kp, 0] = quantise("wa%d0" % kp, wa_rounded[kp, 0][:], PASS)
+        library_logs(0, 1, "rows1", "sample")
+        for kp in range(2):
+            v_w[kp, 1] = gather_words("v_w%d1" % kp, tab_w[kp], list8, 1)
+        for kp in range(2):
+            wa_raw[kp, 1] = load_wa(kp, 1, "table%d" % kp)
 
-        def gather_sample(a, h):
-            t = kept("v_w%d%d" % (a, h), [P, HALF], U32)
-            nc.vector.tensor_copy(t[:], tab_w[a][:].indirect(list8[:, 32 * h : 32 * (h + 1)]))
-            v_w[a, h] = t
+        diff, scaled, both, both_q, banks = {}, {}, {}, {}, {}
 
-        gather_sample(0, 0)
-        wa_w[0, 0], wa_sc[0, 0] = quantise("wa00", rounded0[0])
-        gather_sample(1, 0)
-        wa_w[1, 0], wa_sc[1, 0] = quantise("wa10", rounded0[1])
-        library(0, 1)
-        for a in range(2):
-            gather_sample(a, 1)
-        for a in range(2):
-            wa_raw[a, 1] = load_rows("wa_raw%d1" % a, wa[a * KP : (a + 1) * KP, KP : 2 * KP], "tab_w%d" % a)
-
-        diff, scaled, mixed, es_w, es_sc = {}, {}, {}, {}, {}
-
-        def logs(b, j0, width):
+        def sample_logs(rb, j0, width):
             h, off = divmod(j0, HALF)
             per_bank = HALF // width
-            d = work.tile([P, PACK, width], F32, name="log_a", bufs=4)
-            for t0 in range(0, PACK, per_bank):
-                bank = psum.tile([P, per_bank, width], F32, name="first")
+            diff[rb, j0] = work.tile([P, SLOTS, width], F32, name="diff", bufs=4)
+            for t0 in range(0, SLOTS, per_bank):
+                bank = psum.tile([P, per_bank, width], F32, name="sample")
                 for u in range(per_bank):
                     cols = slice((t0 + u) * P, (t0 + u + 1) * P)
-                    for a in range(2):
-                        nc.tensor.matmul_mx(
-                            out=bank[:, u, :], lhsT=wa_w[a, b][:, cols].bitcast(FP8X4),
-                            lhsT_scale=wa_sc[a, b][:, cols],
-                            rhs=v_w[a, h][:, off : off + width].bitcast(FP8X4),
-                            rhs_scale=v_sc[4 * a : P, j0 : j0 + width],
-                            start=(a == 0), stop=(a == 1))
-                nc.scalar.activation(out=d[:, t0 : t0 + per_bank, :], in_=bank[:], func=ACT.Ln, bias=1.0)
-            diff[b, j0] = d
+                    for kp in range(2):
+                        words, plane = wa_q[kp, rb]
+                        nc.tensor.matmul_mx(out=bank[:, u, :], lhsT=words[:, cols].bitcast(FP8X4),
+                                            lhsT_scale=plane[:, cols],
+                                            rhs=v_w[kp, h][:, off : off + width].bitcast(FP8X4),
+                                            rhs_scale=v_sc[4 * kp : P, j0 : j0 + width],
+                                            start=(kp == 0), stop=(kp == 1))
+                nc.scalar.activation(out=diff[rb, j0][:, t0 : t0 + per_bank, :], in_=bank[:], func=ACT.Ln, bias=1.0)
 
-        def differences(b, j0, width):
+        def differences(rb, j0, width):
             h, off = divmod(j0, HALF)
-            d = diff[b, j0]
-            nc.vector.tensor_tensor(out=d[:], in0=d[:], in1=log_b[b, h][:, :, off : off + width], op=ALU.subtract)
-            e = work.tile([P, PACK, width], F32, name="scaled", bufs=3)
-            for t in range(PACK):
-                if b == 0 and j0 < ON_VECTOR * UNIT:
-                    nc.vector.tensor_scalar(out=e[:, t, :], in0=d[:, t, :], scalar1=g[:, b, t : t + 1], scalar2=None,
-                                            op0=ALU.mult)
+            d = diff[rb, j0]
+            nc.vector.tensor_tensor(out=d[:], in0=d[:], in1=log_b[rb, h][:, :, off : off + width], op=ALU.subtract)
+            e = work.tile([P, SLOTS, width], F32, name="scaled", bufs=3)
+            for t in range(SLOTS):
+                if rb == 0 and j0 < GAIN_ON_VECTOR * UNIT:
+                    nc.vector.tensor_scalar(out=e[:, t, :], in0=d[:, t, :], scalar1=gains[:, rb, t : t + 1],
+                                            scalar2=None, op0=ALU.mult)
                 else:
-                    nc.scalar.activation(out=e[:, t, :], in_=d[:, t, :], func=ACT.Copy, scale=g[:, b, t : t + 1])
-            scaled[b, j0] = e
+                    nc.scalar.activation(out=e[:, t, :], in_=d[:, t, :], func=ACT.Copy, scale=gains[:, rb, t : t + 1])
+            scaled[rb, j0] = e
 
-        def back(b, j0, width):
-            both = work.tile([P, 2, width * PACK], BF16, name="both", align_bytes=64)
-            woven = "p (c i t) -> p c t i"
-            flat = "p t (c i) -> p c t i"
-            nc.vector.tensor_tensor(out=both[:, 1, :].rearrange(woven, i=4, t=PACK),
-                                    in0=scaled[b, j0][:].rearrange(flat, i=4),
-                                    in1=diff[b, j0][:].rearrange(flat, i=4), op=ALU.mult)
-            copy = nc.scalar.copy if b == 1 and FIRST_S * UNIT <= j0 < LAST_S * UNIT else nc.vector.tensor_copy
-            copy(out=both[:, 0, :].rearrange(woven, i=4, t=PACK), in_=scaled[b, j0][:].rearrange(flat, i=4))
-            mixed[b, j0] = both
+        def products(rb, j0, width):
+            both[rb, j0] = work.tile([P, 2, width * SLOTS], BF16, name="both", align_bytes=64)
+            woven, apart = "p (c i t) -> p c t i", "p t (c i) -> p c t i"
+            e = scaled[rb, j0][:].rearrange(apart, i=LINE)
+            nc.vector.tensor_tensor(out=both[rb, j0][:, 1, :].rearrange(woven, i=LINE, t=SLOTS), in0=e,
+                                    in1=diff[rb, j0][:].rearrange(apart, i=LINE), op=ALU.mult)
+            copy = nc.scalar.copy if rb == 1 and width == UNIT else nc.vector.tensor_copy
+            copy(out=both[rb, j0][:, 0, :].rearrange(woven, i=LINE, t=SLOTS), in_=e)
 
-        def quantise_unit(b, j0, width):
-            w = kept("es_w%d_%d" % (b, j0), [P, 2 * width], U32)
-            sc = kept("es_sc%d_%d" % (b, j0), [P, 2 * width], U8)
-            nc.vector.quantize_mx(out=w[:].bitcast(FP8X4), scales=sc[:],
-                                  in_=mixed[b, j0][:].rearrange("p s c -> p (s c)"))
-            es_w[b, j0], es_sc[b, j0] = w, sc
+        def quantise_unit(rb, j0, width):
+            both_q[rb, j0] = quantise("both%d_%d" % (rb, j0), both[rb, j0][:].rearrange("p s c -> p (s c)"), 2 * width)
 
-        wr_w, wr_sc = {}, {}
-
-        def prepare_wr(b):
-            t = keep.tile([P, PACK * KP], BF16, name="wr_rounded", tag=["raw0", "tab2_w"][b], align_bytes=64)
-            copy = nc.scalar.copy if b >= WR_V else nc.vector.tensor_copy
-            copy(out=t[:].rearrange("p (c i j) -> p c j i", i=4, j=PACK),
-                                  in_=wr_raw[b][:].rearrange("p j (c i) -> p c j i", i=4))
-            return t
-
-        banks = {}
-
-        def score_passes(b, q, j0, width, first, last):
-            src = (b, q * UNIT) if b == 0 else (b, j0)
-            full = UNIT if b == 0 else width
-            o = j0 - q * UNIT
+        def score_passes(rb, j0, width):
+            q, off = divmod(j0, UNIT)
+            words, plane = both_q[rb, j0]
             for pair in range(2):
-                if first:
-                    banks[q, pair] = psum.tile([P, 2, UNIT], F32, name="first" if q == S // UNIT - 1 else "second")
+                if rb == 0:
+                    banks[q, pair] = psum.tile([P, 2, UNIT], F32, name="sample" if j0 + UNIT == S else "other")
                 for u in range(2):
-                    nt = 2 * pair + u
-                    cols = slice(nt * P, (nt + 1) * P)
-                    dst = banks[q, pair][:, u, o : o + width]
-                    nc.tensor.matmul_mx(out=dst, lhsT=wr_w[b][:, cols].bitcast(FP8X4), lhsT_scale=wr_sc[b][:, cols],
-                                        rhs=es_w[src][:, 0:full].bitcast(FP8X4), rhs_scale=es_sc[src][:, 0:full],
-                                        start=(first and u == 0), stop=False)
-                    nc.tensor.matmul_mx(out=dst, lhsT=w8_w[:, b, cols].bitcast(FP8X4),
-                                        lhsT_scale=w8_sc[:, b * N + nt * P : b * N + (nt + 1) * P],
-                                        rhs=es_w[src][:, full : 2 * full].bitcast(FP8X4),
-                                        rhs_scale=es_sc[src][:, full : 2 * full],
-                                        start=False, stop=(last and u == 1))
+                    n0 = (2 * pair + u) * P
+                    cols = slice(n0, n0 + P)
+                    dst = banks[q, pair][:, u, off : off + width]
+                    nc.tensor.matmul_mx(out=dst, lhsT=wr_q[rb][0][:, cols].bitcast(FP8X4), lhsT_scale=wr_q[rb][1][:, cols],
+                                        rhs=words[:, 0:width].bitcast(FP8X4), rhs_scale=plane[:, 0:width],
+                                        start=(rb == 0 and u == 0), stop=False)
+                    nc.tensor.matmul_mx(out=dst, lhsT=w8_w[:, rb, cols].bitcast(FP8X4),
+                                        lhsT_scale=w8_sc[:, rb * N + n0 : rb * N + n0 + P],
+                                        rhs=words[:, width : 2 * width].bitcast(FP8X4),
+                                        rhs_scale=plane[:, width : 2 * width],
+                                        start=False, stop=(rb == 1 and off + width == UNIT and u == 1))
 
-        def store(q, split):
+        def store_scores(q):
             rows = out.rearrange("(nt p) j -> p nt j", p=P)[:, :, q * UNIT : (q + 1) * UNIT]
-            res = [work.tile([P, 2, UNIT], F32, name="res%d" % pair) for pair in range(2)]
-            nc.scalar.copy(out=res[0][:], in_=banks[q, 0][:])
-            if split:
-                nc.vector.tensor_copy(out=res[1][:], in_=banks[q, 1][:])
-            else:
-                nc.scalar.copy(out=res[1][:], in_=banks[q, 1][:])
+            staged = [work.tile([P, 2, UNIT], F32, name="staged%d" % pair) for pair in range(2)]
+            nc.scalar.copy(out=staged[0][:], in_=banks[q, 0][:])
+            copy = nc.vector.tensor_copy if (q + 1) * UNIT == S else nc.scalar.copy
+            copy(out=staged[1][:], in_=banks[q, 1][:])
             for pair in range(2):
-                nc.sync.dma_start(out=rows[:, 2 * pair : 2 * pair + 2, :], in_=res[pair][:])
+                nc.sync.dma_start(out=rows[:, 2 * pair : 2 * pair + 2, :], in_=staged[pair][:])
 
-        quarters = S // UNIT
-        units = [(b, q * UNIT, UNIT) for b in range(2) for q in range(quarters)]
+        units = [(rb, j0, UNIT) for rb in range(2) for j0 in range(0, S, UNIT)]
         units = units[:-1] + [(1, S - UNIT, UNIT // 2), (1, S - UNIT // 2, UNIT // 2)]
-        pending = {}
+        wr_rounded = {}
 
-        def scores(b, j0, width):
-            q = j0 // UNIT
-            last = (j0 + width) % UNIT == 0
-            score_passes(1, q, j0, width, False, last)
-            if last:
-                store(q, q == quarters - 1)
-
-        n = len(units)
-        logs(*units[0])
-        for step in range(n + 2):
-            if step + 1 < n:
-                logs(*units[step + 1])
-            if step < n:
+        sample_logs(*units[0])
+        for step in range(len(units) + 2):
+            if step + 1 < len(units):
+                sample_logs(*units[step + 1])
+            if step < len(units):
                 differences(*units[step])
             if step >= 2:
                 quantise_unit(*units[step - 2])
-            if 1 <= step <= n:
-                back(*units[step - 1])
-                b, j0, width = units[step - 1]
-                if b == 1 and j0 % UNIT == 0:
-                    score_passes(0, j0 // UNIT, j0, UNIT, True, False)
+            if 1 <= step <= len(units):
+                rb, j0, width = units[step - 1]
+                products(rb, j0, width)
+                if rb == 1 and j0 % UNIT == 0:
+                    score_passes(0, j0, UNIT)
             if step >= 2 and units[step - 2][0] == 1:
-                scores(*units[step - 2])
+                rb, j0, width = units[step - 2]
+                score_passes(rb, j0, width)
+                if (j0 + width) % UNIT == 0:
+                    store_scores(j0 // UNIT)
             if step in (0, 1):
-                pending[step] = round_wa(step, 1)
+                wa_rounded[step, 1] = round_wa(step, 1)
             if step in (1, 2):
-                wa_w[step - 1, 1], wa_sc[step - 1, 1] = quantise("wa%d1" % (step - 1), pending[step - 1])
-            if step in (LIB0, LIB1):
-                library(1, 0 if step == LIB0 else 1)
-            if step == LIB1:
-                w8_w = keep.tile([P, 2, N], U32, name="w8_w", tag="v2_w0", align_bytes=64)
-                nc.sync.dma_start(out=w8_w[:].bitcast(I32),
-                                  in_=w8_words.rearrange("b p n i -> p b (n i)").bitcast(I32))
-                w8_sc = keep.tile([P, 2 * N], U8, name="w8_sc", tag="v2_sc", align_bytes=64)
-                nc.vector.memset(w8_sc[:].bitcast(I32), 0)
-                for d in range(4):
-                    nc.sync.dma_start(
-                        out=w8_sc[:].bitcast(I32).rearrange("p (a n) -> p a n", a=2)[32 * d : 32 * d + 4],
-                        in_=w8_scales.bitcast(I32)[:, 4 * d : 4 * d + 4, :].rearrange("a r n -> r a n"))
-            if step in (2, 4):
-                pending[step + 1] = prepare_wr(step // 2 - 1)
-            if step in (3, 5):
-                wr_w[step // 2 - 1], wr_sc[step // 2 - 1] = quantise("wr%d" % (step // 2 - 1), pending[step])
+                wa_q[step - 1, 1] = quantise("wa%d1" % (step - 1), wa_rounded[step - 1, 1][:], PASS)
+            if step == 2:
+                library_logs(1, 0)
+                wr_rounded[0] = round_wr(0, None)
+                wr_raw.append(load_rows("wr_raw1", wr[PASS : 2 * PASS, :], "rows0"))
+            if step == 3:
+                library_logs(1, 1)
+                w8_w = kept("w8_w", [P, 2, N], U32, "v2_w0")
+                nc.sync.dma_start(out=as_words(w8_w[:]), in_=as_words(w8_words.rearrange("b p n i -> p b (n i)")))
+                w8_sc = kept("w8_sc", [P, 2 * N], U8, "v2_sc")
+                nc.vector.memset(as_words(w8_sc[:]), 0)
+                load_plane(nc.sync, as_words(w8_sc[:]).rearrange("p (b n) -> p b n", b=2),
+                           lambda q: as_words(w8_scales)[:, q, :].rearrange("b r n -> r b n"))
+                wr_q[0] = quantise("wr0", wr_rounded[0][:], N)
+            if step == 4:
+                wr_rounded[1] = round_wr(1, "rows1")
+            if step == 5:
+                wr_q[1] = quantise("wr1", wr_rounded[1][:], N)

@@ -1,6 +1,7 @@
 from contextlib import ExitStack
 
 import concourse.mybir as mybir
+from concourse.masks import make_identity
 
 K, M, H, N, T, S = 1024, 512, 1024, 512, 2048, 1024
 FLOPS = 2 * S * (K * H + M * H + 2 * H * N)
@@ -20,10 +21,8 @@ P = 128
 SLOTS = 4
 PASS = P * SLOTS
 QUADRANT = 32
-HALF = 512
-UNIT = 256
+GROUP = 256
 LINE = 4
-GAIN_ON_VECTOR = 2
 
 
 def tile_list_metabolite_annotation_scores_kernel(
@@ -33,9 +32,9 @@ def tile_list_metabolite_annotation_scores_kernel(
     nc = tc.nc
     with ExitStack() as ctx:
         keep = ctx.enter_context(tc.tile_pool(name="keep", bufs=1))
-        stage = ctx.enter_context(tc.tile_pool(name="stage", bufs=3))
+        stage = ctx.enter_context(tc.tile_pool(name="stage", bufs=2))
         work = ctx.enter_context(tc.tile_pool(name="work", bufs=2))
-        psum = ctx.enter_context(tc.psum_pool(name="psum", bufs=4))
+        psum = ctx.enter_context(tc.psum_pool(name="psum", bufs=2))
 
         def kept(name, shape, dtype, buffer=None):
             return keep.tile(shape, dtype, name=name, tag=buffer or name, align_bytes=64)
@@ -45,69 +44,73 @@ def tile_list_metabolite_annotation_scores_kernel(
 
         list8 = keep.tile([P, S // 16], U16, name="list8")
         list1 = keep.tile([P, S // 16], U16, name="list1")
-        tab2_sc = kept("tab2_sc", [P, T], U8)
-        w4_sc_raw = kept("w4_sc_raw", [P, H], U8)
         tab_sc = kept("tab_sc", [P, T], U8)
-        w4_raw = kept("w4_raw", [P, 2 * H], U8)
+        tab2_sc = kept("tab2_sc", [P, T], U8)
+        w4_sc = kept("w4_sc", [P, H], U8)
+        w8_sc = kept("w8_sc", [P, 2 * N], U8)
+        w4_w = kept("w4_w", [P, 2 * H], U8)
         one = kept("one", [P, 1], F32)
         warm = kept("warm", [P, 1], F32)
+        identity = kept("identity", [P, P], F32)
 
-        nc.gpsimd.memset(as_words(tab2_sc[:]), 0)
-        nc.vector.memset(as_words(tab_sc[:]), 0)
-        nc.vector.memset(as_words(w4_sc_raw[:]), 0)
+        nc.gpsimd.memset(as_words(tab_sc[:]), 0)
+        nc.vector.memset(as_words(tab2_sc[:]), 0)
+        nc.vector.memset(as_words(w4_sc[:]), 0)
         nc.vector.memset(one[:], 1.0)
+        nc.vector.memset(as_words(w8_sc[:]), 0)
+        make_identity(nc, identity[:])
+        nc.scalar.activation(out=warm[:], in_=one[:], func=ACT.Ln, bias=1.0)
 
-        def load_plane(queue, plane, rows):
+        def load_plane(plane, rows):
             for d in range(4):
-                queue.dma_start(out=plane[QUADRANT * d : QUADRANT * d + 4], in_=rows(slice(4 * d, 4 * d + 4)))
+                nc.sync.dma_start(out=plane[QUADRANT * d : QUADRANT * d + 4], in_=rows(slice(4 * d, 4 * d + 4)))
 
-        def load_table(name, words, buffer):
-            tile = kept(name, [P, T], U32, buffer)
+        def load_table(name, words):
+            tile = kept(name, [P, T], U32)
             nc.sync.dma_start(out=as_words(tile[:]), in_=as_words(words.rearrange("p t i -> p (t i)")))
             return tile
 
-        def load_rows(name, rows, buffer):
+        def load_rows(name, rows, buffer=None):
             tile = kept(name, [P, SLOTS, PASS], F32, buffer)
             nc.sync.dma_start(out=tile[:], in_=rows.rearrange("(p j) c -> p j c", j=SLOTS))
             return tile
 
-        def load_wa(kp, rb, buffer):
+        def load_wa(kp, rb, buffer=None):
             return load_rows("wa_raw%d%d" % (kp, rb), wa[kp * PASS : (kp + 1) * PASS, rb * PASS : (rb + 1) * PASS], buffer)
 
-        def gather_words(name, table, offsets, h):
-            tile = kept(name, [P, HALF], U32)
-            nc.vector.tensor_copy(tile[:], table[:].indirect(offsets[:, h * HALF // 16 : (h + 1) * HALF // 16]))
+        def gather_words(name, table, offsets, g):
+            tile = kept(name, [P, GROUP], U32)
+            nc.vector.tensor_copy(tile[:], table[:].indirect(offsets[:, g * GROUP // 16 : (g + 1) * GROUP // 16]))
             return tile
 
-        for kp in range(2):
-            nc.scalar.dma_start(out=as_words(tab_sc[:])[4 * kp : P : 8, :], in_=as_words(tab_scales[kp]))
-        nc.scalar.activation(out=warm[:], in_=one[:], func=ACT.Ln, bias=1.0)
+        def rounded(name, raw):
+            tile = stage.tile([P, SLOTS * PASS], BF16, name="rounded", align_bytes=64)
+            nc.scalar.copy(out=tile[:].rearrange("p (c i j) -> p c j i", i=LINE, j=SLOTS),
+                           in_=raw[:].rearrange("p j (c i) -> p c j i", i=LINE))
+            return tile
+
+        def quantise(name, values, columns, buffer=None):
+            words = kept(name + "_w", [P, columns], U32, buffer)
+            plane = kept(name + "_sc", [P, columns], U8)
+            nc.vector.quantize_mx(out=words[:].bitcast(FP8X4), scales=plane[:], in_=values)
+            return words, plane
 
         wa_raw = {}
-        nc.sync.dma_start(list1[:], offs2)
-        nc.sync.dma_start(out=as_words(w4_raw[:]), in_=as_words(w4_words[0]))
-        load_plane(nc.sync, as_words(tab2_sc[:]), lambda q: as_words(tab2_scales[0])[q, :])
-        tab2_w = load_table("tab2_w", tab2_words[0], None)
-        load_plane(nc.sync, as_words(w4_sc_raw[:]), lambda q: as_words(w4_scales[0])[q, :])
-        wa_raw[0, 0] = load_wa(0, 0, "rows0")
         nc.sync.dma_start(list8[:], offs)
-        wa_raw[1, 0] = load_wa(1, 0, "rows1")
-        tab_w = [load_table("tab_w%d" % kp, tab_words[kp], "table%d" % kp) for kp in range(2)]
+        nc.sync.dma_start(list1[:], offs2)
+        for kp in range(2):
+            nc.sync.dma_start(out=as_words(tab_sc[:])[4 * kp : P : 8, :], in_=as_words(tab_scales[kp]))
+        wa_raw[0, 0] = load_wa(0, 0)
+        load_plane(as_words(tab2_sc[:]), lambda q: as_words(tab2_scales[0])[q, :])
+        wa_raw[1, 0] = load_wa(1, 0)
+        load_plane(as_words(w4_sc[:]), lambda q: as_words(w4_scales[0])[q, :])
+        nc.sync.dma_start(out=as_words(w4_w[:]), in_=as_words(w4_words[0]))
+        tab2_w = load_table("tab2_w", tab2_words[0])
         gains = kept("gains", [P, 2, SLOTS], F32)
         nc.gpsimd.dma_start(out=gains[:], in_=gain.rearrange("(b p t) -> p b t", b=2, t=SLOTS))
 
-        v2_sc = kept("v2_sc", [P, S], U8)
-        nc.vector.tensor_copy(v2_sc[:], tab2_sc[:].indirect(list1[:]))
-        v2_w = [gather_words("v2_w0", tab2_w, list1, 0)]
-        by_slot, by_channel = "p (b t m) -> p b m t", "p (b m t) -> p b m t"
-        w4_w = kept("w4_w", [P, 2 * H], U8)
-        nc.vector.tensor_copy(out=w4_w[:].bitcast(U16).rearrange(by_slot, b=2, t=SLOTS),
-                              in_=w4_raw[:].bitcast(U16).rearrange(by_channel, b=2, t=SLOTS))
-        w4_sc = kept("w4_sc", [P, H], U8)
-        nc.vector.tensor_copy(out=w4_sc[:].rearrange(by_slot, b=2, t=SLOTS),
-                              in_=w4_sc_raw[:].rearrange(by_channel, b=2, t=SLOTS))
-
-        picked_sc = kept("picked_sc", [P, S], U8, "rows2")
+        tab_w = [load_table("tab_w0", tab_words[0])]
+        picked_sc = kept("picked_sc", [P, S], U8)
         nc.vector.tensor_copy(picked_sc[:], tab_sc[:].indirect(list8[:]))
         v_sc = kept("v_sc", [P, S], U8)
         nc.vector.tensor_copy(as_words(v_sc[:]), as_words(picked_sc[:]))
@@ -115,164 +118,157 @@ def tile_list_metabolite_annotation_scores_kernel(
             for r in range(1, 4):
                 nc.sync.dma_start(out=as_words(v_sc[:])[4 * kp + r : P : QUADRANT, :],
                                   in_=as_words(picked_sc[:])[4 * kp + 8 * r : P : QUADRANT, :])
-        v2_w.append(gather_words("v2_w1", tab2_w, list1, 1))
+        tab_w.append(load_table("tab_w1", tab_words[1]))
+        for kp in range(2):
+            wa_raw[kp, 1] = load_wa(kp, 1)
+        wr_raw = [load_rows("wr_raw0", wr[0:PASS, :])]
+        w8_w = kept("w8_w", [P, 2, N], U32)
+        nc.sync.dma_start(out=as_words(w8_w[:]), in_=as_words(w8_words.rearrange("b p n i -> p b (n i)")))
+        load_plane(as_words(w8_sc[:]).rearrange("p (b n) -> p b n", b=2),
+                   lambda q: as_words(w8_scales)[:, q, :].rearrange("b r n -> r b n"))
+        wr_raw.append(load_rows("wr_raw1", wr[PASS : 2 * PASS, :]))
+        v2_sc = kept("v2_sc", [P, S], U8)
+        nc.vector.tensor_copy(v2_sc[:], tab2_sc[:].indirect(list1[:]))
 
-        def round_wa(kp, rb):
-            rounded = stage.tile([P, SLOTS * PASS], BF16, name="wa_rounded", align_bytes=64)
-            nc.scalar.copy(out=rounded[:].rearrange("p (t m j) -> p m j t", t=SLOTS, j=SLOTS),
-                           in_=wa_raw[kp, rb][:].rearrange("p j (m t) -> p m j t", t=SLOTS))
-            return rounded
+        wa_q, wr_q, v_w, v2_w = {}, {}, {}, {}
+        for kp in range(2):
+            wa_q[kp, 0] = quantise("wa%d0" % kp, rounded("wa", wa_raw[kp, 0])[:], PASS, "tab2_sc" if kp == 0 else None)
 
-        def round_wr(rb, buffer):
-            rounded = kept("wr_rounded%d" % rb, [P, SLOTS * N], BF16, buffer)
-            nc.vector.tensor_copy(out=rounded[:].rearrange("p (c i j) -> p c j i", i=LINE, j=SLOTS),
-                                  in_=wr_raw[rb][:].rearrange("p j (c i) -> p c j i", i=LINE))
-            return rounded
+        minus_log_b, log_a, diff, scaled, both, both_q, banks = {}, {}, {}, {}, {}, {}, {}
+        by_slot = "p (m t) -> p t m"
 
-        def quantise(name, rounded, columns):
-            words = kept(name + "_w", [P, columns], U32)
-            plane = kept(name + "_sc", [P, columns], U8)
-            nc.vector.quantize_mx(out=words[:].bitcast(FP8X4), scales=plane[:], in_=rounded)
-            return words, plane
+        def library_logs(rb, g):
+            logs = work.tile([P, 2, SLOTS, P], F32, name="log_b")
+            for u in range(2):
+                j0 = g * GROUP + u * P
+                bank = psum.tile([P, PASS], F32, name="first")
+                nc.tensor.matmul_mx(out=bank[:], lhsT=v2_w[g][:, u * P : (u + 1) * P].bitcast(FP8X4),
+                                    lhsT_scale=v2_sc[:, j0 : j0 + P],
+                                    rhs=w4_w[:, 2 * rb * PASS : 2 * (rb + 1) * PASS].bitcast(FP4X4),
+                                    rhs_scale=w4_sc[:, rb * PASS : (rb + 1) * PASS], start=True, stop=True)
+                nc.scalar.activation(out=logs[:, u], in_=bank[:].rearrange(by_slot, t=SLOTS), func=ACT.Ln, bias=1.0)
+            minus_log_b[rb, g] = kept("minus_log_b%d%d" % (rb, g), [P, 2, SLOTS, P], F32)
+            flat = "p u t m -> p (u t m)"
+            nc.gpsimd.tensor_scalar(out=minus_log_b[rb, g][:].rearrange(flat), in0=logs[:].rearrange(flat),
+                                    scalar1=-1.0, scalar2=0.0, op0=ALU.mult, op1=ALU.add)
 
-        log_b = {}
+        def sample_logs(rb, g, u):
+            j0 = g * GROUP + u * P
+            bank = psum.tile([P, PASS], F32, name="first")
+            for kp in range(2):
+                words, plane = wa_q[kp, rb]
+                nc.tensor.matmul_mx(out=bank[:], lhsT=v_w[kp, g][:, u * P : (u + 1) * P].bitcast(FP8X4),
+                                    lhsT_scale=v_sc[4 * kp : P, j0 : j0 + P], rhs=words[:].bitcast(FP8X4),
+                                    rhs_scale=plane[:], start=(kp == 0), stop=(kp == 1))
+            log_a[rb, g, u] = work.tile([P, SLOTS, P], F32, name="log_a", bufs=4)
+            nc.scalar.activation(out=log_a[rb, g, u][:], in_=bank[:].rearrange(by_slot, t=SLOTS), func=ACT.Ln, bias=1.0)
 
-        def library_logs(rb, h, buffer=None, banks_of="other"):
-            log_b[rb, h] = kept("log_b%d%d" % (rb, h), [P, SLOTS, HALF], F32, buffer)
+        def differences(rb, g, u):
+            d = diff[rb, g, u] = psum.tile([P, SLOTS, P], F32, name="diff", bufs=4)
             for t in range(SLOTS):
-                c = (SLOTS * rb + t) * P
-                bank = psum.tile([P, HALF], F32, name=banks_of)
-                nc.tensor.matmul_mx(out=bank[:], lhsT=w4_w[:, 2 * c : 2 * (c + P)].bitcast(FP4X4),
-                                    lhsT_scale=w4_sc[:, c : c + P], rhs=v2_w[h][:].bitcast(FP8X4),
-                                    rhs_scale=v2_sc[:, h * HALF : (h + 1) * HALF], start=True, stop=True)
-                nc.scalar.activation(out=log_b[rb, h][:, t, :], in_=bank[:], func=ACT.Ln, bias=1.0)
-
-        wa_rounded = {(kp, 0): round_wa(kp, 0) for kp in range(2)}
-        library_logs(0, 0, "rows0")
-        wr_raw = [load_rows("wr_raw0", wr[0:PASS, :], "rows2")]
-
-        wa_q, wr_q, v_w = {}, {}, {}
-        for kp in range(2):
-            v_w[kp, 0] = gather_words("v_w%d0" % kp, tab_w[kp], list8, 0)
-            wa_q[kp, 0] = quantise("wa%d0" % kp, wa_rounded[kp, 0][:], PASS)
-        library_logs(0, 1, "rows1", "sample")
-        for kp in range(2):
-            v_w[kp, 1] = gather_words("v_w%d1" % kp, tab_w[kp], list8, 1)
-        for kp in range(2):
-            wa_raw[kp, 1] = load_wa(kp, 1, "table%d" % kp)
-
-        diff, scaled, both, both_q, banks = {}, {}, {}, {}, {}
-
-        def sample_logs(rb, j0, width):
-            h, off = divmod(j0, HALF)
-            per_bank = HALF // width
-            diff[rb, j0] = work.tile([P, SLOTS, width], F32, name="diff", bufs=4)
-            for t0 in range(0, SLOTS, per_bank):
-                bank = psum.tile([P, per_bank, width], F32, name="sample")
-                for u in range(per_bank):
-                    cols = slice((t0 + u) * P, (t0 + u + 1) * P)
-                    for kp in range(2):
-                        words, plane = wa_q[kp, rb]
-                        nc.tensor.matmul_mx(out=bank[:, u, :], lhsT=words[:, cols].bitcast(FP8X4),
-                                            lhsT_scale=plane[:, cols],
-                                            rhs=v_w[kp, h][:, off : off + width].bitcast(FP8X4),
-                                            rhs_scale=v_sc[4 * kp : P, j0 : j0 + width],
-                                            start=(kp == 0), stop=(kp == 1))
-                nc.scalar.activation(out=diff[rb, j0][:, t0 : t0 + per_bank, :], in_=bank[:], func=ACT.Ln, bias=1.0)
-
-        def differences(rb, j0, width):
-            h, off = divmod(j0, HALF)
-            d = diff[rb, j0]
-            nc.vector.tensor_tensor(out=d[:], in0=d[:], in1=log_b[rb, h][:, :, off : off + width], op=ALU.subtract)
-            e = work.tile([P, SLOTS, width], F32, name="scaled", bufs=3)
+                nc.tensor.matmul(out=d[:, t, :], lhsT=minus_log_b[rb, g][:, u, t, :], rhs=identity[:],
+                                 is_transpose=True, start=(t == 0), stop=False)
             for t in range(SLOTS):
-                if rb == 0 and j0 < GAIN_ON_VECTOR * UNIT:
-                    nc.vector.tensor_scalar(out=e[:, t, :], in0=d[:, t, :], scalar1=gains[:, rb, t : t + 1],
-                                            scalar2=None, op0=ALU.mult)
-                else:
-                    nc.scalar.activation(out=e[:, t, :], in_=d[:, t, :], func=ACT.Copy, scale=gains[:, rb, t : t + 1])
-            scaled[rb, j0] = e
+                nc.tensor.matmul(out=d[:, t, :], lhsT=log_a[rb, g, u][:, t, :], rhs=identity[:],
+                                 is_transpose=True, start=False, stop=(t == SLOTS - 1))
 
-        def products(rb, j0, width):
-            both[rb, j0] = work.tile([P, 2, width * SLOTS], BF16, name="both", align_bytes=64)
-            woven, apart = "p (c i t) -> p c t i", "p t (c i) -> p c t i"
-            e = scaled[rb, j0][:].rearrange(apart, i=LINE)
-            nc.vector.tensor_tensor(out=both[rb, j0][:, 1, :].rearrange(woven, i=LINE, t=SLOTS), in0=e,
-                                    in1=diff[rb, j0][:].rearrange(apart, i=LINE), op=ALU.mult)
-            copy = nc.scalar.copy if rb == 1 and width == UNIT else nc.vector.tensor_copy
-            copy(out=both[rb, j0][:, 0, :].rearrange(woven, i=LINE, t=SLOTS), in_=e)
+        def scale(rb, g, u):
+            if u == 0:
+                scaled[rb, g] = work.tile([P, 2, P, SLOTS], F32, name="scaled")
+                both[rb, g] = work.tile([P, 2, GROUP * SLOTS], BF16, name="both", align_bytes=64)
+            nc.vector.tensor_tensor(out=scaled[rb, g][:, u], in0=diff[rb, g, u][:].rearrange("p t j -> p j t"),
+                                    in1=gains[:, rb : rb + 1, :].to_broadcast([P, P, SLOTS]), op=ALU.mult)
+            if u == 1:
+                nc.gpsimd.tensor_scalar(out=both[rb, g][:, 0, :], in0=scaled[rb, g][:].rearrange("p u j t -> p (u j t)"),
+                                        scalar1=1.0, scalar2=0.0, op0=ALU.mult, op1=ALU.add)
 
-        def quantise_unit(rb, j0, width):
-            both_q[rb, j0] = quantise("both%d_%d" % (rb, j0), both[rb, j0][:].rearrange("p s c -> p (s c)"), 2 * width)
+        def square(rb, g, u):
+            nc.vector.tensor_tensor(out=both[rb, g][:, 1, u * PASS : (u + 1) * PASS].rearrange("p (j t) -> p j t", t=SLOTS),
+                                    in0=diff[rb, g, u][:].rearrange("p t j -> p j t"), in1=scaled[rb, g][:, u], op=ALU.mult)
 
-        def score_passes(rb, j0, width):
-            q, off = divmod(j0, UNIT)
-            words, plane = both_q[rb, j0]
+        def quantise_group(rb, g):
+            both_q[rb, g] = quantise("both%d%d" % (rb, g), both[rb, g][:].rearrange("p s c -> p (s c)"), 2 * GROUP)
+
+        def score_passes(rb, g):
+            words, plane = both_q[rb, g]
             for pair in range(2):
                 if rb == 0:
-                    banks[q, pair] = psum.tile([P, 2, UNIT], F32, name="sample" if j0 + UNIT == S else "other")
+                    banks[g, pair] = psum.tile([P, 2, GROUP], F32, name="scores")
                 for u in range(2):
                     n0 = (2 * pair + u) * P
                     cols = slice(n0, n0 + P)
-                    dst = banks[q, pair][:, u, off : off + width]
+                    dst = banks[g, pair][:, u, :]
                     nc.tensor.matmul_mx(out=dst, lhsT=wr_q[rb][0][:, cols].bitcast(FP8X4), lhsT_scale=wr_q[rb][1][:, cols],
-                                        rhs=words[:, 0:width].bitcast(FP8X4), rhs_scale=plane[:, 0:width],
+                                        rhs=words[:, 0:GROUP].bitcast(FP8X4), rhs_scale=plane[:, 0:GROUP],
                                         start=(rb == 0 and u == 0), stop=False)
                     nc.tensor.matmul_mx(out=dst, lhsT=w8_w[:, rb, cols].bitcast(FP8X4),
                                         lhsT_scale=w8_sc[:, rb * N + n0 : rb * N + n0 + P],
-                                        rhs=words[:, width : 2 * width].bitcast(FP8X4),
-                                        rhs_scale=plane[:, width : 2 * width],
-                                        start=False, stop=(rb == 1 and off + width == UNIT and u == 1))
+                                        rhs=words[:, GROUP : 2 * GROUP].bitcast(FP8X4),
+                                        rhs_scale=plane[:, GROUP : 2 * GROUP],
+                                        start=False, stop=(rb == 1 and u == 1))
 
-        def store_scores(q):
-            rows = out.rearrange("(nt p) j -> p nt j", p=P)[:, :, q * UNIT : (q + 1) * UNIT]
-            staged = [work.tile([P, 2, UNIT], F32, name="staged%d" % pair) for pair in range(2)]
-            nc.scalar.copy(out=staged[0][:], in_=banks[q, 0][:])
-            copy = nc.vector.tensor_copy if (q + 1) * UNIT == S else nc.scalar.copy
-            copy(out=staged[1][:], in_=banks[q, 1][:])
+        def store_scores(g):
+            rows = out.rearrange("(nt p) j -> p nt j", p=P)[:, :, g * GROUP : (g + 1) * GROUP]
+            staged = [work.tile([P, 2, GROUP], F32, name="staged%d" % pair) for pair in range(2)]
+            nc.scalar.copy(out=staged[0][:], in_=banks[g, 0][:])
+            copy = nc.vector.tensor_copy if (g + 1) * GROUP == S else nc.scalar.copy
+            copy(out=staged[1][:], in_=banks[g, 1][:])
             for pair in range(2):
                 nc.sync.dma_start(out=rows[:, 2 * pair : 2 * pair + 2, :], in_=staged[pair][:])
 
-        units = [(rb, j0, UNIT) for rb in range(2) for j0 in range(0, S, UNIT)]
-        units = units[:-1] + [(1, S - UNIT, UNIT // 2), (1, S - UNIT // 2, UNIT // 2)]
-        wr_rounded = {}
+        groups = S // GROUP
+        for g in range(groups):
+            v2_w[g] = gather_words("v2_w%d" % g, tab2_w, list1, g)
+            library_logs(0, g)
+        for g in range(groups):
+            v_w[0, g] = gather_words("v_w0%d" % g, tab_w[0], list8, g)
+        v_w[1, 0] = gather_words("v_w10", tab_w[1], list8, 0)
 
-        sample_logs(*units[0])
-        for step in range(len(units) + 2):
-            if step + 1 < len(units):
-                sample_logs(*units[step + 1])
-            if step < len(units):
-                differences(*units[step])
-            if step >= 2:
-                quantise_unit(*units[step - 2])
-            if 1 <= step <= len(units):
-                rb, j0, width = units[step - 1]
-                products(rb, j0, width)
-                if rb == 1 and j0 % UNIT == 0:
-                    score_passes(0, j0, UNIT)
-            if step >= 2 and units[step - 2][0] == 1:
-                rb, j0, width = units[step - 2]
-                score_passes(rb, j0, width)
-                if (j0 + width) % UNIT == 0:
-                    store_scores(j0 // UNIT)
-            if step in (0, 1):
-                wa_rounded[step, 1] = round_wa(step, 1)
-            if step in (1, 2):
-                wa_q[step - 1, 1] = quantise("wa%d1" % (step - 1), wa_rounded[step - 1, 1][:], PASS)
-            if step == 2:
-                library_logs(1, 0)
-                wr_rounded[0] = round_wr(0, None)
-                wr_raw.append(load_rows("wr_raw1", wr[PASS : 2 * PASS, :], "rows0"))
-            if step == 3:
+        steps = [(0, 0), (0, 1), (1, 0), (0, 2), (1, 1), (0, 3), (1, 2), (1, 3)]
+        for u in range(2):
+            sample_logs(*steps[0], u)
+        v_w[1, 1] = gather_words("v_w11", tab_w[1], list8, 1)
+        library_logs(1, 0)
+        for u in range(2):
+            differences(*steps[0], u)
+        for u in range(2):
+            sample_logs(*steps[1], u)
+        scale(*steps[0], 0)
+        for s, (rb, g) in enumerate(steps):
+            if s + 1 < len(steps):
+                for u in range(2):
+                    differences(*steps[s + 1], u)
+            scale(rb, g, 1)
+            if s == 0:
+                for kp in range(2):
+                    wa_q[kp, 1] = quantise("wa%d1" % kp, rounded("wa", wa_raw[kp, 1])[:], PASS)
+            if s >= 1:
+                quantise_group(*steps[s - 1])
+            if s + 2 < len(steps):
+                for u in range(2):
+                    sample_logs(*steps[s + 2], u)
+            if s >= 1 and steps[s - 1][0] == 1:
+                if s - 1 < len(steps) - 2:
+                    score_passes(0, steps[s - 1][1])
+                score_passes(*steps[s - 1])
+                store_scores(steps[s - 1][1])
+            square(rb, g, 0)
+            if s + 1 < len(steps):
+                scale(*steps[s + 1], 0)
+            square(rb, g, 1)
+            if s == 0:
+                v_w[1, 2] = gather_words("v_w12", tab_w[1], list8, 2)
                 library_logs(1, 1)
-                w8_w = kept("w8_w", [P, 2, N], U32, "v2_w0")
-                nc.sync.dma_start(out=as_words(w8_w[:]), in_=as_words(w8_words.rearrange("b p n i -> p b (n i)")))
-                w8_sc = kept("w8_sc", [P, 2 * N], U8, "v2_sc")
-                nc.vector.memset(as_words(w8_sc[:]), 0)
-                load_plane(nc.sync, as_words(w8_sc[:]).rearrange("p (b n) -> p b n", b=2),
-                           lambda q: as_words(w8_scales)[:, q, :].rearrange("b r n -> r b n"))
-                wr_q[0] = quantise("wr0", wr_rounded[0][:], N)
-            if step == 4:
-                wr_rounded[1] = round_wr(1, "rows1")
-            if step == 5:
-                wr_q[1] = quantise("wr1", wr_rounded[1][:], N)
+            if s == 1:
+                v_w[1, 3] = gather_words("v_w13", tab_w[1], list8, 3)
+                wr_q[0] = quantise("wr0", rounded("wr", wr_raw[0])[:], N)
+            if s == 2:
+                wr_q[1] = quantise("wr1", rounded("wr", wr_raw[1])[:], N)
+            if s in (3, 4):
+                library_logs(1, s - 1)
+            if s == len(steps) - 2:
+                score_passes(0, g)
+        score_passes(0, groups - 1)
+        quantise_group(*steps[-1])
+        score_passes(*steps[-1])
+        store_scores(groups - 1)

@@ -23,6 +23,7 @@ PASS = P * SLOTS
 QUADRANT = 32
 GROUP = 256
 LINE = 4
+ADDED_IN_PSUM = 5
 
 
 def tile_list_metabolite_annotation_scores_kernel(
@@ -61,9 +62,9 @@ def tile_list_metabolite_annotation_scores_kernel(
         make_identity(nc, identity[:])
         nc.scalar.activation(out=warm[:], in_=one[:], func=ACT.Ln, bias=1.0)
 
-        def load_plane(plane, rows):
+        def load_plane(queue, plane, rows):
             for d in range(4):
-                nc.sync.dma_start(out=plane[QUADRANT * d : QUADRANT * d + 4], in_=rows(slice(4 * d, 4 * d + 4)))
+                queue.dma_start(out=plane[QUADRANT * d : QUADRANT * d + 4], in_=rows(slice(4 * d, 4 * d + 4)))
 
         def load_table(name, words):
             tile = kept(name, [P, T], U32)
@@ -83,10 +84,10 @@ def tile_list_metabolite_annotation_scores_kernel(
             nc.vector.tensor_copy(tile[:], table[:].indirect(offsets[:, g * GROUP // 16 : (g + 1) * GROUP // 16]))
             return tile
 
-        def rounded(name, raw):
-            tile = stage.tile([P, SLOTS * PASS], BF16, name="rounded", align_bytes=64)
-            nc.scalar.copy(out=tile[:].rearrange("p (c i j) -> p c j i", i=LINE, j=SLOTS),
-                           in_=raw[:].rearrange("p j (c i) -> p c j i", i=LINE))
+        def rounded(copy, raw, buffer):
+            tile = kept("rounded", [P, SLOTS * PASS], BF16, buffer)
+            copy(out=tile[:].rearrange("p (c i j) -> p c j i", i=LINE, j=SLOTS),
+                 in_=raw[:].rearrange("p j (c i) -> p c j i", i=LINE))
             return tile
 
         def quantise(name, values, columns, buffer=None):
@@ -101,11 +102,11 @@ def tile_list_metabolite_annotation_scores_kernel(
         for kp in range(2):
             nc.sync.dma_start(out=as_words(tab_sc[:])[4 * kp : P : 8, :], in_=as_words(tab_scales[kp]))
         wa_raw[0, 0] = load_wa(0, 0)
-        load_plane(as_words(tab2_sc[:]), lambda q: as_words(tab2_scales[0])[q, :])
-        wa_raw[1, 0] = load_wa(1, 0)
-        load_plane(as_words(w4_sc[:]), lambda q: as_words(w4_scales[0])[q, :])
-        nc.sync.dma_start(out=as_words(w4_w[:]), in_=as_words(w4_words[0]))
+        load_plane(nc.sync, as_words(tab2_sc[:]), lambda q: as_words(tab2_scales[0])[q, :])
         tab2_w = load_table("tab2_w", tab2_words[0])
+        load_plane(nc.sync, as_words(w4_sc[:]), lambda q: as_words(w4_scales[0])[q, :])
+        nc.sync.dma_start(out=as_words(w4_w[:]), in_=as_words(w4_words[0]))
+        wa_raw[1, 0] = load_wa(1, 0)
         gains = kept("gains", [P, 2, SLOTS], F32)
         nc.gpsimd.dma_start(out=gains[:], in_=gain.rearrange("(b p t) -> p b t", b=2, t=SLOTS))
 
@@ -114,6 +115,7 @@ def tile_list_metabolite_annotation_scores_kernel(
         nc.vector.tensor_copy(picked_sc[:], tab_sc[:].indirect(list8[:]))
         v_sc = kept("v_sc", [P, S], U8)
         nc.vector.tensor_copy(as_words(v_sc[:]), as_words(picked_sc[:]))
+        wa_rounded = rounded(nc.scalar.copy, wa_raw[0, 0], "stage0")
         for kp in range(2):
             for r in range(1, 4):
                 nc.sync.dma_start(out=as_words(v_sc[:])[4 * kp + r : P : QUADRANT, :],
@@ -122,78 +124,89 @@ def tile_list_metabolite_annotation_scores_kernel(
         for kp in range(2):
             wa_raw[kp, 1] = load_wa(kp, 1)
         wr_raw = [load_rows("wr_raw0", wr[0:PASS, :])]
+        load_plane(nc.sync, as_words(w8_sc[:]).rearrange("p (b n) -> p b n", b=2),
+                   lambda q: as_words(w8_scales)[:, q, :].rearrange("b r n -> r b n"))
         w8_w = kept("w8_w", [P, 2, N], U32)
         nc.sync.dma_start(out=as_words(w8_w[:]), in_=as_words(w8_words.rearrange("b p n i -> p b (n i)")))
-        load_plane(as_words(w8_sc[:]).rearrange("p (b n) -> p b n", b=2),
-                   lambda q: as_words(w8_scales)[:, q, :].rearrange("b r n -> r b n"))
         wr_raw.append(load_rows("wr_raw1", wr[PASS : 2 * PASS, :]))
         v2_sc = kept("v2_sc", [P, S], U8)
         nc.vector.tensor_copy(v2_sc[:], tab2_sc[:].indirect(list1[:]))
 
         wa_q, wr_q, v_w, v2_w = {}, {}, {}, {}
-        for kp in range(2):
-            wa_q[kp, 0] = quantise("wa%d0" % kp, rounded("wa", wa_raw[kp, 0])[:], PASS, "tab2_sc" if kp == 0 else None)
+        wa_q[0, 0] = quantise("wa00", wa_rounded[:], PASS, "tab2_sc")
 
-        minus_log_b, log_a, diff, scaled, both, both_q, banks = {}, {}, {}, {}, {}, {}, {}
+        log_b, log_a, diff, scaled, both, both_q, banks = {}, {}, {}, {}, {}, {}, {}
         by_slot = "p (m t) -> p t m"
+        groups = S // GROUP
+        steps = [(0, 0), (0, 1), (0, 2), (1, 0), (0, 3), (1, 1), (1, 2), (1, 3)]
 
-        def library_logs(rb, g):
-            logs = work.tile([P, 2, SLOTS, P], F32, name="log_b")
+        def library_logs(s, pair, buffer=None):
+            rb, g = steps[s]
+            logs = log_b[s] = kept("log_b%d" % s, [P, 2, SLOTS, P], F32, buffer)
             for u in range(2):
                 j0 = g * GROUP + u * P
-                bank = psum.tile([P, PASS], F32, name="first")
+                bank = psum.tile([P, PASS], F32, name=pair)
                 nc.tensor.matmul_mx(out=bank[:], lhsT=v2_w[g][:, u * P : (u + 1) * P].bitcast(FP8X4),
                                     lhsT_scale=v2_sc[:, j0 : j0 + P],
                                     rhs=w4_w[:, 2 * rb * PASS : 2 * (rb + 1) * PASS].bitcast(FP4X4),
                                     rhs_scale=w4_sc[:, rb * PASS : (rb + 1) * PASS], start=True, stop=True)
                 nc.scalar.activation(out=logs[:, u], in_=bank[:].rearrange(by_slot, t=SLOTS), func=ACT.Ln, bias=1.0)
-            minus_log_b[rb, g] = kept("minus_log_b%d%d" % (rb, g), [P, 2, SLOTS, P], F32)
+
+        def negate(s, buffer=None):
             flat = "p u t m -> p (u t m)"
-            nc.gpsimd.tensor_scalar(out=minus_log_b[rb, g][:].rearrange(flat), in0=logs[:].rearrange(flat),
+            negated = kept("negated%d" % s, [P, 2, SLOTS, P], F32, buffer)
+            nc.gpsimd.tensor_scalar(out=negated[:].rearrange(flat), in0=log_b[s][:].rearrange(flat),
                                     scalar1=-1.0, scalar2=0.0, op0=ALU.mult, op1=ALU.add)
+            log_b[s] = negated
 
-        def sample_logs(rb, g, u):
-            j0 = g * GROUP + u * P
-            bank = psum.tile([P, PASS], F32, name="first")
-            for kp in range(2):
-                words, plane = wa_q[kp, rb]
-                nc.tensor.matmul_mx(out=bank[:], lhsT=v_w[kp, g][:, u * P : (u + 1) * P].bitcast(FP8X4),
-                                    lhsT_scale=v_sc[4 * kp : P, j0 : j0 + P], rhs=words[:].bitcast(FP8X4),
-                                    rhs_scale=plane[:], start=(kp == 0), stop=(kp == 1))
-            log_a[rb, g, u] = work.tile([P, SLOTS, P], F32, name="log_a", bufs=4)
-            nc.scalar.activation(out=log_a[rb, g, u][:], in_=bank[:].rearrange(by_slot, t=SLOTS), func=ACT.Ln, bias=1.0)
+        def sample_logs(s, pair="x"):
+            rb, g = steps[s]
+            log_a[s] = work.tile([P, 2, SLOTS, P], F32, name="log_a", bufs=4)
+            for u in range(2):
+                j0 = g * GROUP + u * P
+                bank = psum.tile([P, PASS], F32, name=pair)
+                for kp in (0, 1) if s == 0 else (1, 0):
+                    words, plane = wa_q[kp, rb]
+                    nc.tensor.matmul_mx(out=bank[:], lhsT=v_w[kp, g][:, u * P : (u + 1) * P].bitcast(FP8X4),
+                                        lhsT_scale=v_sc[4 * kp : P, j0 : j0 + P], rhs=words[:].bitcast(FP8X4),
+                                        rhs_scale=plane[:], start=(kp == (0 if s == 0 else 1)), stop=(kp == (1 if s == 0 else 0)))
+                nc.scalar.activation(out=log_a[s][:, u], in_=bank[:].rearrange(by_slot, t=SLOTS), func=ACT.Ln, bias=1.0)
 
-        def differences(rb, g, u):
-            d = diff[rb, g, u] = psum.tile([P, SLOTS, P], F32, name="diff", bufs=4)
-            for t in range(SLOTS):
-                nc.tensor.matmul(out=d[:, t, :], lhsT=minus_log_b[rb, g][:, u, t, :], rhs=identity[:],
-                                 is_transpose=True, start=(t == 0), stop=False)
-            for t in range(SLOTS):
-                nc.tensor.matmul(out=d[:, t, :], lhsT=log_a[rb, g, u][:, t, :], rhs=identity[:],
-                                 is_transpose=True, start=False, stop=(t == SLOTS - 1))
+        def subtract(s):
+            nc.vector.tensor_tensor(out=log_a[s][:], in0=log_a[s][:], in1=log_b[s][:], op=ALU.subtract)
 
-        def scale(rb, g, u):
+        def differences(s):
+            for u in range(2):
+                d = diff[s, u] = psum.tile([P, SLOTS, P], F32, name="diff", bufs=4)
+                terms = [log_a[s], log_b[s]] if s < ADDED_IN_PSUM else [log_a[s]]
+                for i, term in enumerate(terms):
+                    for t in range(SLOTS):
+                        nc.tensor.matmul(out=d[:, t, :], lhsT=term[:, u, t, :], rhs=identity[:], is_transpose=True,
+                                         start=(i == 0 and t == 0), stop=(i == len(terms) - 1 and t == SLOTS - 1))
+
+        def scale(s, u):
+            rb = steps[s][0]
             if u == 0:
-                scaled[rb, g] = work.tile([P, 2, P, SLOTS], F32, name="scaled")
-                both[rb, g] = work.tile([P, 2, GROUP * SLOTS], BF16, name="both", align_bytes=64)
-            nc.vector.tensor_tensor(out=scaled[rb, g][:, u], in0=diff[rb, g, u][:].rearrange("p t j -> p j t"),
+                scaled[s] = work.tile([P, 2, P, SLOTS], F32, name="scaled")
+                both[s] = work.tile([P, 2, GROUP * SLOTS], BF16, name="both", align_bytes=64)
+            nc.vector.tensor_tensor(out=scaled[s][:, u], in0=diff[s, u][:].rearrange("p t j -> p j t"),
                                     in1=gains[:, rb : rb + 1, :].to_broadcast([P, P, SLOTS]), op=ALU.mult)
             if u == 1:
-                nc.gpsimd.tensor_scalar(out=both[rb, g][:, 0, :], in0=scaled[rb, g][:].rearrange("p u j t -> p (u j t)"),
+                nc.gpsimd.tensor_scalar(out=both[s][:, 0, :], in0=scaled[s][:].rearrange("p u j t -> p (u j t)"),
                                         scalar1=1.0, scalar2=0.0, op0=ALU.mult, op1=ALU.add)
 
-        def square(rb, g, u):
-            nc.vector.tensor_tensor(out=both[rb, g][:, 1, u * PASS : (u + 1) * PASS].rearrange("p (j t) -> p j t", t=SLOTS),
-                                    in0=diff[rb, g, u][:].rearrange("p t j -> p j t"), in1=scaled[rb, g][:, u], op=ALU.mult)
+        def square(s, u):
+            nc.vector.tensor_tensor(out=both[s][:, 1, u * PASS : (u + 1) * PASS].rearrange("p (j t) -> p j t", t=SLOTS),
+                                    in0=diff[s, u][:].rearrange("p t j -> p j t"), in1=scaled[s][:, u], op=ALU.mult)
 
-        def quantise_group(rb, g):
-            both_q[rb, g] = quantise("both%d%d" % (rb, g), both[rb, g][:].rearrange("p s c -> p (s c)"), 2 * GROUP)
+        def quantise_group(s):
+            both_q[steps[s]] = quantise("both%d" % s, both[s][:].rearrange("p s c -> p (s c)"), 2 * GROUP)
 
         def score_passes(rb, g):
             words, plane = both_q[rb, g]
             for pair in range(2):
                 if rb == 0:
-                    banks[g, pair] = psum.tile([P, 2, GROUP], F32, name="scores")
+                    banks[g, pair] = psum.tile([P, 2, GROUP], F32, name="x" if g == groups - 1 else "y")
                 for u in range(2):
                     n0 = (2 * pair + u) * P
                     cols = slice(n0, n0 + P)
@@ -216,59 +229,56 @@ def tile_list_metabolite_annotation_scores_kernel(
             for pair in range(2):
                 nc.sync.dma_start(out=rows[:, 2 * pair : 2 * pair + 2, :], in_=staged[pair][:])
 
-        groups = S // GROUP
         for g in range(groups):
             v2_w[g] = gather_words("v2_w%d" % g, tab2_w, list1, g)
-            library_logs(0, g)
-        for g in range(groups):
-            v_w[0, g] = gather_words("v_w0%d" % g, tab_w[0], list8, g)
-        v_w[1, 0] = gather_words("v_w10", tab_w[1], list8, 0)
-
-        steps = [(0, 0), (0, 1), (1, 0), (0, 2), (1, 1), (0, 3), (1, 2), (1, 3)]
-        for u in range(2):
-            sample_logs(*steps[0], u)
-        v_w[1, 1] = gather_words("v_w11", tab_w[1], list8, 1)
-        library_logs(1, 0)
-        for u in range(2):
-            differences(*steps[0], u)
-        for u in range(2):
-            sample_logs(*steps[1], u)
-        scale(*steps[0], 0)
+        wa_q[1, 0] = quantise("wa10", rounded(nc.vector.tensor_copy, wa_raw[1, 0], "stage1")[:], PASS)
+        for s in range(ADDED_IN_PSUM):
+            library_logs(s, "xy"[s % 2])
+            negate(s, "stage1" if s == 0 else None)
+        for kp in range(2):
+            for g in range(groups):
+                v_w[kp, g] = gather_words("v_w%d%d" % (kp, g), tab_w[kp], list8, g)
+        sample_logs(0, "y")
+        sample_logs(1, "x")
+        differences(0)
+        sample_logs(2, "y")
+        wa_rounded = [rounded(nc.scalar.copy, wa_raw[kp, 1], "stage%d" % (2 + kp)) for kp in range(2)]
+        scale(0, 0)
+        last = len(steps) - 1
         for s, (rb, g) in enumerate(steps):
-            if s + 1 < len(steps):
-                for u in range(2):
-                    differences(*steps[s + 1], u)
-            scale(rb, g, 1)
-            if s == 0:
-                for kp in range(2):
-                    wa_q[kp, 1] = quantise("wa%d1" % kp, rounded("wa", wa_raw[kp, 1])[:], PASS)
+            if 2 <= s and s + 2 <= last:
+                sample_logs(s + 2, "y" if s == 2 else "x")
+            if s < last:
+                differences(s + 1)
+            scale(s, 1)
             if s >= 1:
-                quantise_group(*steps[s - 1])
-            if s + 2 < len(steps):
-                for u in range(2):
-                    sample_logs(*steps[s + 2], u)
+                quantise_group(s - 1)
+            if s == 2:
+                for late in range(ADDED_IN_PSUM, last + 1):
+                    library_logs(late, "y", "log_b%d" % (late - ADDED_IN_PSUM))
+            if s == 3:
+                score_passes(0, 0)
             if s >= 1 and steps[s - 1][0] == 1:
-                if s - 1 < len(steps) - 2:
-                    score_passes(0, steps[s - 1][1])
                 score_passes(*steps[s - 1])
                 store_scores(steps[s - 1][1])
-            square(rb, g, 0)
-            if s + 1 < len(steps):
-                scale(*steps[s + 1], 0)
-            square(rb, g, 1)
-            if s == 0:
-                v_w[1, 2] = gather_words("v_w12", tab_w[1], list8, 2)
-                library_logs(1, 1)
+            if s == 4:
+                score_passes(0, 1)
+            if s == 6:
+                score_passes(0, 2)
+                score_passes(0, 3)
+            square(s, 0)
+            if s < last:
+                scale(s + 1, 0)
+            square(s, 1)
+            if s < 2:
+                wa_q[s, 1] = quantise("wa%d1" % s, wa_rounded[s][:], PASS)
             if s == 1:
-                v_w[1, 3] = gather_words("v_w13", tab_w[1], list8, 3)
-                wr_q[0] = quantise("wr0", rounded("wr", wr_raw[0])[:], N)
-            if s == 2:
-                wr_q[1] = quantise("wr1", rounded("wr", wr_raw[1])[:], N)
-            if s in (3, 4):
-                library_logs(1, s - 1)
-            if s == len(steps) - 2:
-                score_passes(0, g)
-        score_passes(0, groups - 1)
-        quantise_group(*steps[-1])
-        score_passes(*steps[-1])
+                sample_logs(3)
+                wr_rounded = [rounded(nc.scalar.copy, wr_raw[rb], "stage%d" % (2 * rb)) for rb in range(2)]
+            if s in (2, 3):
+                wr_q[s - 2] = quantise("wr%d" % (s - 2), wr_rounded[s - 2][:], N)
+            if ADDED_IN_PSUM <= s + 2 <= last:
+                subtract(s + 2)
+        quantise_group(last)
+        score_passes(*steps[last])
         store_scores(groups - 1)

@@ -23,7 +23,7 @@ PASS = P * SLOTS
 QUADRANT = 32
 GROUP = 256
 LINE = 4
-ADDED_IN_PSUM = 5
+EARLY = 4
 
 
 def tile_list_metabolite_annotation_scores_kernel(
@@ -54,8 +54,8 @@ def tile_list_metabolite_annotation_scores_kernel(
         warm = kept("warm", [P, 1], F32)
         identity = kept("identity", [P, P], F32)
 
-        nc.gpsimd.memset(as_words(tab_sc[:]), 0)
-        nc.vector.memset(as_words(tab2_sc[:]), 0)
+        nc.gpsimd.memset(as_words(tab2_sc[:]), 0)
+        nc.vector.memset(as_words(tab_sc[:]), 0)
         nc.vector.memset(as_words(w4_sc[:]), 0)
         nc.vector.memset(one[:], 1.0)
         nc.vector.memset(as_words(w8_sc[:]), 0)
@@ -63,8 +63,8 @@ def tile_list_metabolite_annotation_scores_kernel(
         nc.scalar.activation(out=warm[:], in_=one[:], func=ACT.Ln, bias=1.0)
 
         def load_plane(queue, plane, rows):
-            for d in range(4):
-                queue.dma_start(out=plane[QUADRANT * d : QUADRANT * d + 4], in_=rows(slice(4 * d, 4 * d + 4)))
+            for r in range(4):
+                queue.dma_start(out=plane[r:P:QUADRANT], in_=rows(slice(r, 16, 4)))
 
         def load_table(name, words):
             tile = kept(name, [P, T], U32)
@@ -97,25 +97,30 @@ def tile_list_metabolite_annotation_scores_kernel(
             return words, plane
 
         wa_raw = {}
-        nc.sync.dma_start(list8[:], offs)
         nc.sync.dma_start(list1[:], offs2)
-        for kp in range(2):
-            nc.sync.dma_start(out=as_words(tab_sc[:])[4 * kp : P : 8, :], in_=as_words(tab_scales[kp]))
-        wa_raw[0, 0] = load_wa(0, 0)
+        nc.sync.dma_start(list8[:], offs)
         load_plane(nc.sync, as_words(tab2_sc[:]), lambda q: as_words(tab2_scales[0])[q, :])
         tab2_w = load_table("tab2_w", tab2_words[0])
-        load_plane(nc.sync, as_words(w4_sc[:]), lambda q: as_words(w4_scales[0])[q, :])
         nc.sync.dma_start(out=as_words(w4_w[:]), in_=as_words(w4_words[0]))
-        wa_raw[1, 0] = load_wa(1, 0)
+        load_plane(nc.sync, as_words(w4_sc[:]), lambda q: as_words(w4_scales[0])[q, :])
+        for kp in range(2):
+            nc.sync.dma_start(out=as_words(tab_sc[:])[4 * kp : P : 8, :], in_=as_words(tab_scales[kp]))
+        for kp in range(2):
+            wa_raw[kp, 0] = load_wa(kp, 0)
         gains = kept("gains", [P, 2, SLOTS], F32)
         nc.gpsimd.dma_start(out=gains[:], in_=gain.rearrange("(b p t) -> p b t", b=2, t=SLOTS))
-
         tab_w = [load_table("tab_w0", tab_words[0])]
+
+        wa_q, wr_q, v_w, v2_w = {}, {}, {}, {}
+        groups = S // GROUP
+        v2_sc = kept("v2_sc", [P, S], U8)
+        nc.vector.tensor_copy(v2_sc[:], tab2_sc[:].indirect(list1[:]))
+        for g in range(groups):
+            v2_w[g] = gather_words("v2_w%d" % g, tab2_w, list1, g)
         picked_sc = kept("picked_sc", [P, S], U8)
         nc.vector.tensor_copy(picked_sc[:], tab_sc[:].indirect(list8[:]))
         v_sc = kept("v_sc", [P, S], U8)
         nc.vector.tensor_copy(as_words(v_sc[:]), as_words(picked_sc[:]))
-        wa_rounded = rounded(nc.scalar.copy, wa_raw[0, 0], "stage0")
         for kp in range(2):
             for r in range(1, 4):
                 nc.sync.dma_start(out=as_words(v_sc[:])[4 * kp + r : P : QUADRANT, :],
@@ -129,16 +134,12 @@ def tile_list_metabolite_annotation_scores_kernel(
         w8_w = kept("w8_w", [P, 2, N], U32)
         nc.sync.dma_start(out=as_words(w8_w[:]), in_=as_words(w8_words.rearrange("b p n i -> p b (n i)")))
         wr_raw.append(load_rows("wr_raw1", wr[PASS : 2 * PASS, :]))
-        v2_sc = kept("v2_sc", [P, S], U8)
-        nc.vector.tensor_copy(v2_sc[:], tab2_sc[:].indirect(list1[:]))
-
-        wa_q, wr_q, v_w, v2_w = {}, {}, {}, {}
-        wa_q[0, 0] = quantise("wa00", wa_rounded[:], PASS, "tab2_sc")
+        for kp in range(2):
+            wa_q[kp, 0] = quantise("wa%d0" % kp, rounded(nc.vector.tensor_copy, wa_raw[kp, 0], "stage%d" % kp)[:], PASS)
 
         log_b, log_a, diff, scaled, both, both_q, banks = {}, {}, {}, {}, {}, {}, {}
         by_slot = "p (m t) -> p t m"
-        groups = S // GROUP
-        steps = [(0, 0), (0, 1), (0, 2), (1, 0), (0, 3), (1, 1), (1, 2), (1, 3)]
+        steps = [(rb, g) for rb in range(2) for g in range(groups)]
 
         def library_logs(s, pair, buffer=None):
             rb, g = steps[s]
@@ -155,8 +156,11 @@ def tile_list_metabolite_annotation_scores_kernel(
         def negate(s, buffer=None):
             flat = "p u t m -> p (u t m)"
             negated = kept("negated%d" % s, [P, 2, SLOTS, P], F32, buffer)
-            nc.gpsimd.tensor_scalar(out=negated[:].rearrange(flat), in0=log_b[s][:].rearrange(flat),
-                                    scalar1=-1.0, scalar2=0.0, op0=ALU.mult, op1=ALU.add)
+            if s < EARLY:
+                nc.gpsimd.tensor_scalar(out=negated[:].rearrange(flat), in0=log_b[s][:].rearrange(flat),
+                                        scalar1=-1.0, scalar2=0.0, op0=ALU.mult, op1=ALU.add)
+            else:
+                nc.scalar.activation(out=negated[:], in_=log_b[s][:], func=ACT.Copy, scale=-1.0)
             log_b[s] = negated
 
         def sample_logs(s, pair="x"):
@@ -172,13 +176,10 @@ def tile_list_metabolite_annotation_scores_kernel(
                                         rhs_scale=plane[:], start=(kp == (0 if s == 0 else 1)), stop=(kp == (1 if s == 0 else 0)))
                 nc.scalar.activation(out=log_a[s][:, u], in_=bank[:].rearrange(by_slot, t=SLOTS), func=ACT.Ln, bias=1.0)
 
-        def subtract(s):
-            nc.vector.tensor_tensor(out=log_a[s][:], in0=log_a[s][:], in1=log_b[s][:], op=ALU.subtract)
-
         def differences(s):
             for u in range(2):
                 d = diff[s, u] = psum.tile([P, SLOTS, P], F32, name="diff", bufs=4)
-                terms = [log_a[s], log_b[s]] if s < ADDED_IN_PSUM else [log_a[s]]
+                terms = [log_a[s], log_b[s]]
                 for i, term in enumerate(terms):
                     for t in range(SLOTS):
                         nc.tensor.matmul(out=d[:, t, :], lhsT=term[:, u, t, :], rhs=identity[:], is_transpose=True,
@@ -188,97 +189,117 @@ def tile_list_metabolite_annotation_scores_kernel(
             rb = steps[s][0]
             if u == 0:
                 scaled[s] = work.tile([P, 2, P, SLOTS], F32, name="scaled")
-                both[s] = work.tile([P, 2, GROUP * SLOTS], BF16, name="both", align_bytes=64)
+                both[s] = work.tile([P, 2, 2, PASS], BF16, name="both", align_bytes=64)
             nc.vector.tensor_tensor(out=scaled[s][:, u], in0=diff[s, u][:].rearrange("p t j -> p j t"),
                                     in1=gains[:, rb : rb + 1, :].to_broadcast([P, P, SLOTS]), op=ALU.mult)
-            if u == 1:
-                nc.gpsimd.tensor_scalar(out=both[s][:, 0, :], in0=scaled[s][:].rearrange("p u j t -> p (u j t)"),
+            if s == last:
+                nc.scalar.copy(out=both[s][:, u, 0, :], in_=scaled[s][:, u].rearrange("p j t -> p (j t)"))
+            elif u == 1:
+                nc.gpsimd.tensor_scalar(out=both[s][:, 0].rearrange("p u c -> p (u c)"),
+                                        in0=scaled[s][:].rearrange("p u j t -> p (u j t)"),
                                         scalar1=1.0, scalar2=0.0, op0=ALU.mult, op1=ALU.add)
 
         def square(s, u):
-            nc.vector.tensor_tensor(out=both[s][:, 1, u * PASS : (u + 1) * PASS].rearrange("p (j t) -> p j t", t=SLOTS),
+            dst = both[s][:, u, 1, :] if s == last else both[s][:, 1, u, :]
+            nc.vector.tensor_tensor(out=dst.rearrange("p (j t) -> p j t", t=SLOTS),
                                     in0=diff[s, u][:].rearrange("p t j -> p j t"), in1=scaled[s][:, u], op=ALU.mult)
 
         def quantise_group(s):
-            both_q[steps[s]] = quantise("both%d" % s, both[s][:].rearrange("p s c -> p (s c)"), 2 * GROUP)
+            both_q[steps[s]] = quantise("both%d" % s, both[s][:].rearrange("p s u c -> p (s u c)"), 2 * GROUP)
+
+        def passes(dst, rb, nt, quantised, first, width, half, start, stop):
+            words, plane = quantised
+            cols = slice(nt * P, (nt + 1) * P)
+            nc.tensor.matmul_mx(out=dst, lhsT=wr_q[rb][0][:, cols].bitcast(FP8X4), lhsT_scale=wr_q[rb][1][:, cols],
+                                rhs=words[:, first : first + width].bitcast(FP8X4), rhs_scale=plane[:, first : first + width],
+                                start=start, stop=False)
+            first = first + half
+            nc.tensor.matmul_mx(out=dst, lhsT=w8_w[:, rb, cols].bitcast(FP8X4),
+                                lhsT_scale=w8_sc[:, rb * N + nt * P : rb * N + (nt + 1) * P],
+                                rhs=words[:, first : first + width].bitcast(FP8X4), rhs_scale=plane[:, first : first + width],
+                                start=False, stop=stop)
 
         def score_passes(rb, g):
-            words, plane = both_q[rb, g]
             for pair in range(2):
                 if rb == 0:
-                    banks[g, pair] = psum.tile([P, 2, GROUP], F32, name="x" if g == groups - 1 else "y")
+                    banks[g, pair] = psum.tile([P, 2, GROUP], F32, name="yx"[g % 2])
                 for u in range(2):
-                    n0 = (2 * pair + u) * P
-                    cols = slice(n0, n0 + P)
-                    dst = banks[g, pair][:, u, :]
-                    nc.tensor.matmul_mx(out=dst, lhsT=wr_q[rb][0][:, cols].bitcast(FP8X4), lhsT_scale=wr_q[rb][1][:, cols],
-                                        rhs=words[:, 0:GROUP].bitcast(FP8X4), rhs_scale=plane[:, 0:GROUP],
-                                        start=(rb == 0 and u == 0), stop=False)
-                    nc.tensor.matmul_mx(out=dst, lhsT=w8_w[:, rb, cols].bitcast(FP8X4),
-                                        lhsT_scale=w8_sc[:, rb * N + n0 : rb * N + n0 + P],
-                                        rhs=words[:, GROUP : 2 * GROUP].bitcast(FP8X4),
-                                        rhs_scale=plane[:, GROUP : 2 * GROUP],
-                                        start=False, stop=(rb == 1 and u == 1))
+                    passes(banks[g, pair][:, u, :], rb, 2 * pair + u, both_q[rb, g], 0, GROUP, GROUP,
+                           rb == 0 and u == 0, rb == 1 and u == 1)
+
+        rows = out.rearrange("(nt p) j -> p nt j", p=P)
 
         def store_scores(g):
-            rows = out.rearrange("(nt p) j -> p nt j", p=P)[:, :, g * GROUP : (g + 1) * GROUP]
-            staged = [work.tile([P, 2, GROUP], F32, name="staged%d" % pair) for pair in range(2)]
-            nc.scalar.copy(out=staged[0][:], in_=banks[g, 0][:])
-            copy = nc.vector.tensor_copy if (g + 1) * GROUP == S else nc.scalar.copy
-            copy(out=staged[1][:], in_=banks[g, 1][:])
             for pair in range(2):
-                nc.sync.dma_start(out=rows[:, 2 * pair : 2 * pair + 2, :], in_=staged[pair][:])
+                staged = work.tile([P, 2, GROUP], F32, name="staged%d" % pair)
+                nc.scalar.copy(out=staged[:], in_=banks[g, pair][:])
+                nc.sync.dma_start(out=rows[:, 2 * pair : 2 * pair + 2, g * GROUP : (g + 1) * GROUP], in_=staged[:])
 
-        for g in range(groups):
-            v2_w[g] = gather_words("v2_w%d" % g, tab2_w, list1, g)
-        wa_q[1, 0] = quantise("wa10", rounded(nc.vector.tensor_copy, wa_raw[1, 0], "stage1")[:], PASS)
-        for s in range(ADDED_IN_PSUM):
+        def last_passes(rb, u):
+            if rb == 0:
+                banks["last", u] = psum.tile([P, SLOTS, P], F32, name="diff", bufs=4)
+                quantised, first, half = both_q[0, groups - 1], u * P, GROUP
+            else:
+                quantised = quantise("both_last%d" % u, both[last][:, u].rearrange("p s c -> p (s c)"), 2 * P)
+                first, half = 0, P
+            for nt in range(4):
+                passes(banks["last", u][:, nt, :], rb, nt, quantised, first, P, half, rb == 0 and nt == 0, rb == 1 and nt == 3)
+            if rb == 1:
+                staged = work.tile([P, SLOTS, P], F32, name="staged%d" % u)
+                (nc.scalar.copy if u == 0 else nc.vector.tensor_copy)(out=staged[:], in_=banks["last", u][:])
+                j0 = S - GROUP + u * P
+                nc.sync.dma_start(out=rows[:, :, j0 : j0 + P], in_=staged[:])
+
+        last = len(steps) - 1
+        for s in range(len(steps)):
             library_logs(s, "xy"[s % 2])
-            negate(s, "stage1" if s == 0 else None)
+            if s < EARLY:
+                negate(s, "stage1" if s == 1 else "log_b%d" % (s - 1) if s > 1 else None)
         for kp in range(2):
             for g in range(groups):
                 v_w[kp, g] = gather_words("v_w%d%d" % (kp, g), tab_w[kp], list8, g)
-        sample_logs(0, "y")
-        sample_logs(1, "x")
+        negate(4)
+        sample_logs(0, "x")
+        sample_logs(1, "y")
         differences(0)
-        sample_logs(2, "y")
-        wa_rounded = [rounded(nc.scalar.copy, wa_raw[kp, 1], "stage%d" % (2 + kp)) for kp in range(2)]
+        wa_q[0, 1] = quantise("wa01", rounded(nc.vector.tensor_copy, wa_raw[0, 1], "stage2")[:], PASS)
+        wa_rounded = rounded(nc.scalar.copy, wa_raw[1, 1], "stage3")
+        negate(5, "negated0")
         scale(0, 0)
-        last = len(steps) - 1
-        for s, (rb, g) in enumerate(steps):
-            if 2 <= s and s + 2 <= last:
-                sample_logs(s + 2, "y" if s == 2 else "x")
+        for s in range(len(steps)):
+            if s + 2 <= last:
+                sample_logs(s + 2, "y" if s + 2 in (3, 5) else "x")
+            if s in (5, 6):
+                negate(s + 1, "log_b%d" % (s - 4))
             if s < last:
                 differences(s + 1)
             scale(s, 1)
             if s >= 1:
                 quantise_group(s - 1)
-            if s == 2:
-                for late in range(ADDED_IN_PSUM, last + 1):
-                    library_logs(late, "y", "log_b%d" % (late - ADDED_IN_PSUM))
-            if s == 3:
+            if s == 5:
                 score_passes(0, 0)
-            if s >= 1 and steps[s - 1][0] == 1:
-                score_passes(*steps[s - 1])
-                store_scores(steps[s - 1][1])
-            if s == 4:
-                score_passes(0, 1)
-            if s == 6:
-                score_passes(0, 2)
-                score_passes(0, 3)
+            if s >= 6:
+                score_passes(1, s - 6)
+                store_scores(s - 6)
+                score_passes(0, s - 5)
+            if s == last:
+                for u in range(2):
+                    last_passes(0, u)
             square(s, 0)
             if s < last:
                 scale(s + 1, 0)
+            else:
+                score_passes(1, 2)
+                last_passes(1, 0)
             square(s, 1)
-            if s < 2:
-                wa_q[s, 1] = quantise("wa%d1" % s, wa_rounded[s][:], PASS)
             if s == 1:
-                sample_logs(3)
-                wr_rounded = [rounded(nc.scalar.copy, wr_raw[rb], "stage%d" % (2 * rb)) for rb in range(2)]
-            if s in (2, 3):
-                wr_q[s - 2] = quantise("wr%d" % (s - 2), wr_rounded[s - 2][:], N)
-            if ADDED_IN_PSUM <= s + 2 <= last:
-                subtract(s + 2)
-        quantise_group(last)
-        score_passes(*steps[last])
-        store_scores(groups - 1)
+                wa_q[1, 1] = quantise("wa11", wa_rounded[:], PASS)
+                wr_rounded = [rounded(nc.scalar.copy, wr_raw[0], "stage0")]
+            if s == 2:
+                wr_q[0] = quantise("wr0", wr_rounded[0][:], N)
+            if s == 3:
+                wr_rounded.append(rounded(nc.scalar.copy, wr_raw[1], "negated4"))
+            if s == 4:
+                wr_q[1] = quantise("wr1", wr_rounded[1][:], N)
+        last_passes(1, 1)
+        store_scores(2)

@@ -84,9 +84,9 @@ def tile_list_metabolite_annotation_scores_kernel(
             nc.vector.tensor_copy(tile[:], table[:].indirect(offsets[:, g * GROUP // 16 : (g + 1) * GROUP // 16]))
             return tile
 
-        def rounded(copy, raw, buffer):
+        def rounded(copy, raw, buffer, order="p (i c j) -> p c j i"):
             tile = kept("rounded", [P, SLOTS * PASS], BF16, buffer)
-            copy(out=tile[:].rearrange("p (c i j) -> p c j i", i=LINE, j=SLOTS),
+            copy(out=tile[:].rearrange(order, i=LINE, j=SLOTS),
                  in_=raw[:].rearrange("p j (c i) -> p c j i", i=LINE))
             return tile
 
@@ -138,7 +138,6 @@ def tile_list_metabolite_annotation_scores_kernel(
             wa_q[kp, 0] = quantise("wa%d0" % kp, rounded(nc.vector.tensor_copy, wa_raw[kp, 0], "stage%d" % kp)[:], PASS)
 
         log_b, log_a, diff, scaled, both, both_q, banks = {}, {}, {}, {}, {}, {}, {}
-        by_slot = "p (m t) -> p t m"
         steps = [(rb, g) for rb in range(2) for g in range(groups)]
 
         def library_logs(s, pair, buffer=None):
@@ -151,7 +150,8 @@ def tile_list_metabolite_annotation_scores_kernel(
                                     lhsT_scale=v2_sc[:, j0 : j0 + P],
                                     rhs=w4_w[:, 2 * rb * PASS : 2 * (rb + 1) * PASS].bitcast(FP4X4),
                                     rhs_scale=w4_sc[:, rb * PASS : (rb + 1) * PASS], start=True, stop=True)
-                nc.scalar.activation(out=logs[:, u], in_=bank[:].rearrange(by_slot, t=SLOTS), func=ACT.Ln, bias=1.0)
+                nc.scalar.activation(out=logs[:, u].rearrange("p t m -> p m t"), in_=bank[:].rearrange("p (m t) -> p m t", t=SLOTS),
+                                     func=ACT.Ln, bias=1.0)
 
         def negate(s, buffer=None):
             flat = "p u t m -> p (u t m)"
@@ -174,7 +174,7 @@ def tile_list_metabolite_annotation_scores_kernel(
                     nc.tensor.matmul_mx(out=bank[:], lhsT=v_w[kp, g][:, u * P : (u + 1) * P].bitcast(FP8X4),
                                         lhsT_scale=v_sc[4 * kp : P, j0 : j0 + P], rhs=words[:].bitcast(FP8X4),
                                         rhs_scale=plane[:], start=(kp == (0 if s == 0 else 1)), stop=(kp == (1 if s == 0 else 0)))
-                nc.scalar.activation(out=log_a[s][:, u], in_=bank[:].rearrange(by_slot, t=SLOTS), func=ACT.Ln, bias=1.0)
+                nc.scalar.activation(out=log_a[s][:, u].rearrange("p t m -> p (t m)"), in_=bank[:], func=ACT.Ln, bias=1.0)
 
         def differences(s):
             for u in range(2):
@@ -294,11 +294,11 @@ def tile_list_metabolite_annotation_scores_kernel(
             square(s, 1)
             if s == 1:
                 wa_q[1, 1] = quantise("wa11", wa_rounded[:], PASS)
-                wr_rounded = [rounded(nc.scalar.copy, wr_raw[0], "stage0")]
+                wr_rounded = [rounded(nc.scalar.copy, wr_raw[0], "stage0", "p (c i j) -> p c j i")]
             if s == 2:
                 wr_q[0] = quantise("wr0", wr_rounded[0][:], N)
             if s == 3:
-                wr_rounded.append(rounded(nc.scalar.copy, wr_raw[1], "negated4"))
+                wr_rounded.append(rounded(nc.scalar.copy, wr_raw[1], "negated4", "p (c i j) -> p c j i"))
             if s == 4:
                 wr_q[1] = quantise("wr1", wr_rounded[1][:], N)
         last_passes(1, 1)

@@ -50,17 +50,13 @@ def tile_list_metabolite_annotation_scores_kernel(
         w4_sc = kept("w4_sc", [P, H], U8)
         w8_sc = kept("w8_sc", [P, 2 * N], U8)
         w4_w = kept("w4_w", [P, 2 * H], U8)
-        one = kept("one", [P, 1], F32)
-        warm = kept("warm", [P, 1], F32)
         identity = kept("identity", [P, P], F32)
 
         nc.gpsimd.memset(as_words(tab2_sc[:]), 0)
         nc.vector.memset(as_words(tab_sc[:]), 0)
         nc.vector.memset(as_words(w4_sc[:]), 0)
-        nc.vector.memset(one[:], 1.0)
         nc.vector.memset(as_words(w8_sc[:]), 0)
         make_identity(nc, identity[:])
-        nc.scalar.activation(out=warm[:], in_=one[:], func=ACT.Ln, bias=1.0)
 
         def load_plane(queue, plane, rows):
             for r in range(4):
@@ -79,10 +75,14 @@ def tile_list_metabolite_annotation_scores_kernel(
         def load_wa(kp, rb, buffer=None):
             return load_rows("wa_raw%d%d" % (kp, rb), wa[kp * PASS : (kp + 1) * PASS, rb * PASS : (rb + 1) * PASS], buffer)
 
-        def gather_words(name, table, offsets, g):
-            tile = kept(name, [P, GROUP], U32)
-            nc.vector.tensor_copy(tile[:], table[:].indirect(offsets[:, g * GROUP // 16 : (g + 1) * GROUP // 16]))
-            return tile
+        def gather_words(name, table, offsets, cuts):
+            pieces = []
+            for first, end in zip([0] + cuts, cuts):
+                tile = kept("%s_%d" % (name, first), [P, end - first, GROUP], U32)
+                nc.vector.tensor_copy(tile[:].rearrange("p g c -> p (g c)"),
+                                      table[:].indirect(offsets[:, first * GROUP // 16 : end * GROUP // 16]))
+                pieces.extend(tile[:, g] for g in range(end - first))
+            return pieces
 
         def rounded(copy, raw, buffer, order="p (i c j) -> p c j i"):
             tile = kept("rounded", [P, SLOTS * PASS], BF16, buffer)
@@ -111,12 +111,11 @@ def tile_list_metabolite_annotation_scores_kernel(
         nc.gpsimd.dma_start(out=gains[:], in_=gain.rearrange("(b p t) -> p b t", b=2, t=SLOTS))
         tab_w = [load_table("tab_w0", tab_words[0])]
 
-        wa_q, wr_q, v_w, v2_w = {}, {}, {}, {}
+        wa_q, wr_q = {}, {}
         groups = S // GROUP
         v2_sc = kept("v2_sc", [P, S], U8)
         nc.vector.tensor_copy(v2_sc[:], tab2_sc[:].indirect(list1[:]))
-        for g in range(groups):
-            v2_w[g] = gather_words("v2_w%d" % g, tab2_w, list1, g)
+        v2_w = gather_words("v2_w", tab2_w, list1, [1, 2, groups])
         picked_sc = kept("picked_sc", [P, S], U8)
         nc.vector.tensor_copy(picked_sc[:], tab_sc[:].indirect(list8[:]))
         v_sc = kept("v_sc", [P, S], U8)
@@ -126,8 +125,12 @@ def tile_list_metabolite_annotation_scores_kernel(
                 nc.sync.dma_start(out=as_words(v_sc[:])[4 * kp + r : P : QUADRANT, :],
                                   in_=as_words(picked_sc[:])[4 * kp + 8 * r : P : QUADRANT, :])
         tab_w.append(load_table("tab_w1", tab_words[1]))
-        for kp in range(2):
-            wa_raw[kp, 1] = load_wa(kp, 1)
+        wa_raw[0, 1] = load_wa(0, 1)
+        wa_halves = []
+        for h in range(2):
+            wa_halves.append(kept("wa_half%d" % h, [P, SLOTS, PASS // 2], F32))
+            c0 = PASS + h * PASS // 2
+            nc.sync.dma_start(out=wa_halves[h][:], in_=wa[PASS:K, c0 : c0 + PASS // 2].rearrange("(p j) c -> p j c", j=SLOTS))
         wr_raw = [load_rows("wr_raw0", wr[0:PASS, :])]
         load_plane(nc.sync, as_words(w8_sc[:]).rearrange("p (b n) -> p b n", b=2),
                    lambda q: as_words(w8_scales)[:, q, :].rearrange("b r n -> r b n"))
@@ -137,6 +140,7 @@ def tile_list_metabolite_annotation_scores_kernel(
         for kp in range(2):
             wa_q[kp, 0] = quantise("wa%d0" % kp, rounded(nc.vector.tensor_copy, wa_raw[kp, 0], "stage%d" % kp)[:], PASS)
 
+        minus = {}
         log_b, log_a, diff, scaled, both, both_q, banks = {}, {}, {}, {}, {}, {}, {}
         steps = [(rb, g) for rb in range(2) for g in range(groups)]
 
@@ -161,51 +165,64 @@ def tile_list_metabolite_annotation_scores_kernel(
                                         scalar1=-1.0, scalar2=0.0, op0=ALU.mult, op1=ALU.add)
             else:
                 nc.scalar.activation(out=negated[:], in_=log_b[s][:], func=ACT.Copy, scale=-1.0)
-            log_b[s] = negated
+            for u in range(2):
+                minus[s, u] = negated[:, u]
 
         def sample_logs(s, pair="x"):
             rb, g = steps[s]
-            log_a[s] = work.tile([P, 2, SLOTS, P], F32, name="log_a", bufs=4)
+            if s == 2:
+                log_a[s] = kept("log_a2", [P, 2, SLOTS, P], F32, "wa_half0")
+            else:
+                log_a[s] = work.tile([P, 2, SLOTS, P], F32, name="log_a", bufs=4)
             for u in range(2):
                 j0 = g * GROUP + u * P
                 bank = psum.tile([P, PASS], F32, name=pair)
-                for kp in (0, 1) if s == 0 else (1, 0):
+                for kp in range(2):
                     words, plane = wa_q[kp, rb]
-                    nc.tensor.matmul_mx(out=bank[:], lhsT=v_w[kp, g][:, u * P : (u + 1) * P].bitcast(FP8X4),
-                                        lhsT_scale=v_sc[4 * kp : P, j0 : j0 + P], rhs=words[:].bitcast(FP8X4),
-                                        rhs_scale=plane[:], start=(kp == (0 if s == 0 else 1)), stop=(kp == (1 if s == 0 else 0)))
+                    nc.tensor.matmul_mx(out=bank[:], lhsT=v_w[kp][g][:, u * P : (u + 1) * P].bitcast(FP8X4),
+                                        lhsT_scale=v_sc[4 * kp : P, j0 : j0 + P], rhs=words[:, 0:PASS].bitcast(FP8X4),
+                                        rhs_scale=plane[:, 0:PASS], start=(kp == 0), stop=(kp == 1))
                 nc.scalar.activation(out=log_a[s][:, u].rearrange("p t m -> p (t m)"), in_=bank[:], func=ACT.Ln, bias=1.0)
 
         def differences(s):
             for u in range(2):
-                d = diff[s, u] = psum.tile([P, SLOTS, P], F32, name="diff", bufs=4)
-                terms = [log_a[s], log_b[s]]
+                d = diff[s, u] = psum.tile([P, SLOTS, P], F32, name="diff", bufs=4)[:]
+                terms = [log_a[s][:, u], minus[s, u]]
                 for i, term in enumerate(terms):
                     for t in range(SLOTS):
-                        nc.tensor.matmul(out=d[:, t, :], lhsT=term[:, u, t, :], rhs=identity[:], is_transpose=True,
+                        nc.tensor.matmul(out=d[:, t, :], lhsT=term[:, t, :], rhs=identity[:], is_transpose=True,
                                          start=(i == 0 and t == 0), stop=(i == len(terms) - 1 and t == SLOTS - 1))
 
         def scale(s, u):
             rb = steps[s][0]
             if u == 0:
-                scaled[s] = work.tile([P, 2, P, SLOTS], F32, name="scaled")
-                both[s] = work.tile([P, 2, 2, PASS], BF16, name="both", align_bytes=64)
-            nc.vector.tensor_tensor(out=scaled[s][:, u], in0=diff[s, u][:].rearrange("p t j -> p j t"),
+                if s == 0:
+                    scaled[s] = kept("scaled0", [P, 2, P, SLOTS], F32, "wa_raw01")
+                else:
+                    scaled[s] = work.tile([P, 2, P, SLOTS], F32, name="scaled")
+            nc.vector.tensor_tensor(out=scaled[s][:, u], in0=diff[s, u].rearrange("p t j -> p j t"),
                                     in1=gains[:, rb : rb + 1, :].to_broadcast([P, P, SLOTS]), op=ALU.mult)
-            if s == last:
-                nc.scalar.copy(out=both[s][:, u, 0, :], in_=scaled[s][:, u].rearrange("p j t -> p (j t)"))
+            if s == last and u == 1:
+                nc.scalar.copy(out=both[s][:, u, 0], in_=scaled[s][:, u].rearrange("p j t -> p (j t)"))
+            elif s == last:
+                nc.gpsimd.tensor_scalar(out=both[s][:, u, 0], in0=scaled[s][:, u].rearrange("p j t -> p (j t)"),
+                                        scalar1=1.0, scalar2=0.0, op0=ALU.mult, op1=ALU.add)
             elif u == 1:
                 nc.gpsimd.tensor_scalar(out=both[s][:, 0].rearrange("p u c -> p (u c)"),
                                         in0=scaled[s][:].rearrange("p u j t -> p (u j t)"),
                                         scalar1=1.0, scalar2=0.0, op0=ALU.mult, op1=ALU.add)
 
         def square(s, u):
-            dst = both[s][:, u, 1, :] if s == last else both[s][:, 1, u, :]
+            dst = both[s][:, u, 1] if s == last else both[s][:, 1, u]
             nc.vector.tensor_tensor(out=dst.rearrange("p (j t) -> p j t", t=SLOTS),
-                                    in0=diff[s, u][:].rearrange("p t j -> p j t"), in1=scaled[s][:, u], op=ALU.mult)
+                                    in0=diff[s, u].rearrange("p t j -> p j t"), in1=scaled[s][:, u], op=ALU.mult)
 
         def quantise_group(s):
-            both_q[steps[s]] = quantise("both%d" % s, both[s][:].rearrange("p s u c -> p (s u c)"), 2 * GROUP)
+            columns = 2 * GROUP + (PASS if s in riders else 0)
+            words, plane = quantise("both%d" % s, staged_values[s][:, 0 : SLOTS * columns], columns)
+            both_q[steps[s]] = words, plane
+            if s in riders:
+                return words[:, 2 * GROUP : columns], plane[:, 2 * GROUP : columns]
 
         def passes(dst, rb, nt, quantised, first, width, half, start, stop):
             words, plane = quantised
@@ -232,50 +249,74 @@ def tile_list_metabolite_annotation_scores_kernel(
         def store_scores(g):
             for pair in range(2):
                 staged = work.tile([P, 2, GROUP], F32, name="staged%d" % pair)
-                nc.scalar.copy(out=staged[:], in_=banks[g, pair][:])
+                copy = nc.vector.tensor_copy if g == groups - 2 and pair == 1 else nc.scalar.copy
+                copy(out=staged[:], in_=banks[g, pair][:])
                 nc.sync.dma_start(out=rows[:, 2 * pair : 2 * pair + 2, g * GROUP : (g + 1) * GROUP], in_=staged[:])
+
+        def store_last(u):
+            staged = work.tile([P, SLOTS, P], F32, name="staged_last")
+            (nc.scalar.copy if u == 0 else nc.vector.tensor_copy)(out=staged[:], in_=banks["last", u])
+            j0 = S - GROUP + u * P
+            nc.sync.dma_start(out=rows[:, :, j0 : j0 + P], in_=staged[:])
 
         def last_passes(rb, u):
             if rb == 0:
-                banks["last", u] = psum.tile([P, SLOTS, P], F32, name="diff", bufs=4)
+                banks["last", u] = psum.tile([P, SLOTS, P], F32, name="diff", bufs=4)[:]
                 quantised, first, half = both_q[0, groups - 1], u * P, GROUP
             else:
                 quantised = quantise("both_last%d" % u, both[last][:, u].rearrange("p s c -> p (s c)"), 2 * P)
                 first, half = 0, P
             for nt in range(4):
                 passes(banks["last", u][:, nt, :], rb, nt, quantised, first, P, half, rb == 0 and nt == 0, rb == 1 and nt == 3)
-            if rb == 1:
-                staged = work.tile([P, SLOTS, P], F32, name="staged%d" % u)
-                (nc.scalar.copy if u == 0 else nc.vector.tensor_copy)(out=staged[:], in_=banks["last", u][:])
-                j0 = S - GROUP + u * P
-                nc.sync.dma_start(out=rows[:, :, j0 : j0 + P], in_=staged[:])
 
         last = len(steps) - 1
+        riders = (0, 2, 3)
+        homes = ["tab2_w", "tab_w0", "wa_raw00", "wa_raw10", "tab_w1", "wa_raw01", "log_b5", "log_b6"]
+        staged_values = {}
+
+        def stage_values(s):
+            staged_values[s] = kept("values%d" % s, [P, SLOTS * (2 * GROUP + (PASS if s in riders else 0))], BF16, homes[s])
+            both[s] = staged_values[s][:, 0 : SLOTS * 2 * GROUP].rearrange("p (x y c) -> p x y c", x=2, y=2)
+
+        def negate_tile(s, u, buffer):
+            flat = "p t m -> p (t m)"
+            negated = kept("negated%d%d" % (s, u), [P, SLOTS, P], F32, buffer)
+            nc.gpsimd.tensor_scalar(out=negated[:].rearrange(flat), in0=log_b[s][:, u].rearrange(flat),
+                                    scalar1=-1.0, scalar2=0.0, op0=ALU.mult, op1=ALU.add)
+            minus[s, u] = negated[:]
+
         for s in range(len(steps)):
             library_logs(s, "xy"[s % 2])
             if s < EARLY:
                 negate(s, "stage1" if s == 1 else "log_b%d" % (s - 1) if s > 1 else None)
-        for kp in range(2):
-            for g in range(groups):
-                v_w[kp, g] = gather_words("v_w%d%d" % (kp, g), tab_w[kp], list8, g)
+        v_w = [gather_words("v_w0", tab_w[0], list8, [2, groups]), gather_words("v_w1", tab_w[1], list8, [1, 2, groups])]
         negate(4)
         sample_logs(0, "x")
         sample_logs(1, "y")
         differences(0)
         wa_q[0, 1] = quantise("wa01", rounded(nc.vector.tensor_copy, wa_raw[0, 1], "stage2")[:], PASS)
-        wa_rounded = rounded(nc.scalar.copy, wa_raw[1, 1], "stage3")
-        negate(5, "negated0")
+        stage_values(0)
+        rider = staged_values[0][:, SLOTS * 2 * GROUP :].rearrange("p (i h c j) -> p h c j i", i=LINE, h=2, j=SLOTS)
+        for h in range(2):
+            nc.scalar.copy(out=rider[:, h], in_=wa_halves[h][:].rearrange("p j (c i) -> p c j i", i=LINE))
         scale(0, 0)
+        late = [(s, u) for s in range(EARLY + 1, last + 1) for u in range(2)]
         for s in range(len(steps)):
-            if s + 2 <= last:
+            if s + 2 <= last and s != 2:
                 sample_logs(s + 2, "y" if s + 2 in (3, 5) else "x")
-            if s in (5, 6):
-                negate(s + 1, "log_b%d" % (s - 4))
             if s < last:
                 differences(s + 1)
+                stage_values(s + 1)
             scale(s, 1)
             if s >= 1:
-                quantise_group(s - 1)
+                carried = quantise_group(s - 1)
+                if s == 1:
+                    wa_q[1, 1] = carried
+                    sample_logs(4)
+                if s in (3, 4):
+                    wr_q[s - 3] = carried
+            if s < len(late):
+                negate_tile(*late[s], homes[s - 1] if s else "stage2")
             if s == 5:
                 score_passes(0, 0)
             if s >= 6:
@@ -292,14 +333,10 @@ def tile_list_metabolite_annotation_scores_kernel(
                 score_passes(1, 2)
                 last_passes(1, 0)
             square(s, 1)
-            if s == 1:
-                wa_q[1, 1] = quantise("wa11", wa_rounded[:], PASS)
-                wr_rounded = [rounded(nc.scalar.copy, wr_raw[0], "stage0", "p (c i j) -> p c j i")]
-            if s == 2:
-                wr_q[0] = quantise("wr0", wr_rounded[0][:], N)
-            if s == 3:
-                wr_rounded.append(rounded(nc.scalar.copy, wr_raw[1], "negated4", "p (c i j) -> p c j i"))
-            if s == 4:
-                wr_q[1] = quantise("wr1", wr_rounded[1][:], N)
+            if s in (1, 2):
+                nc.scalar.copy(out=staged_values[s + 1][:, SLOTS * 2 * GROUP :].rearrange("p (c i j) -> p c j i", i=LINE, j=SLOTS),
+                               in_=wr_raw[s - 1][:].rearrange("p j (c i) -> p c j i", i=LINE))
         last_passes(1, 1)
         store_scores(2)
+        for u in range(2):
+            store_last(u)

@@ -23,7 +23,15 @@ PASS = P * SLOTS
 QUADRANT = 32
 GROUP = 256
 LINE = 4
-EARLY = 4
+EARLY = 3
+TURNED = 5
+WR1 = 4
+HEAD = 8
+AHEAD = 3
+ON_SCALAR = [5]
+LAST_S = 1
+DBUF = 3
+PIECES = 2
 
 
 def tile_list_metabolite_annotation_scores_kernel(
@@ -75,10 +83,10 @@ def tile_list_metabolite_annotation_scores_kernel(
         def load_wa(kp, rb, buffer=None):
             return load_rows("wa_raw%d%d" % (kp, rb), wa[kp * PASS : (kp + 1) * PASS, rb * PASS : (rb + 1) * PASS], buffer)
 
-        def gather_words(name, table, offsets, cuts):
+        def gather_words(name, table, offsets, cuts, buffers={}):
             pieces = []
             for first, end in zip([0] + cuts, cuts):
-                tile = kept("%s_%d" % (name, first), [P, end - first, GROUP], U32)
+                tile = kept("%s_%d" % (name, first), [P, end - first, GROUP], U32, buffers.get(first))
                 nc.vector.tensor_copy(tile[:].rearrange("p g c -> p (g c)"),
                                       table[:].indirect(offsets[:, first * GROUP // 16 : end * GROUP // 16]))
                 pieces.extend(tile[:, g] for g in range(end - first))
@@ -116,6 +124,13 @@ def tile_list_metabolite_annotation_scores_kernel(
         v2_sc = kept("v2_sc", [P, S], U8)
         nc.vector.tensor_copy(v2_sc[:], tab2_sc[:].indirect(list1[:]))
         v2_w = gather_words("v2_w", tab2_w, list1, [1, 2, groups])
+        if TURNED < 8:
+            w4_slot_w = kept("w4_slot_w", [P, 2 * PASS], U8)
+            nc.vector.tensor_copy(out=w4_slot_w[:].bitcast(U16).rearrange("p (t m) -> p m t", t=SLOTS),
+                                  in_=w4_w[:, 2 * PASS : 4 * PASS].bitcast(U16).rearrange("p (m t) -> p m t", t=SLOTS))
+            w4_slot_sc = kept("w4_slot_sc", [P, PASS], U8)
+            nc.vector.tensor_copy(out=w4_slot_sc[:].rearrange("p (t m) -> p m t", t=SLOTS),
+                                  in_=w4_sc[:, PASS : 2 * PASS].rearrange("p (m t) -> p m t", t=SLOTS))
         picked_sc = kept("picked_sc", [P, S], U8)
         nc.vector.tensor_copy(picked_sc[:], tab_sc[:].indirect(list8[:]))
         v_sc = kept("v_sc", [P, S], U8)
@@ -146,10 +161,21 @@ def tile_list_metabolite_annotation_scores_kernel(
 
         def library_logs(s, pair, buffer=None):
             rb, g = steps[s]
+            if s >= TURNED:
+                logs = log_b[s] = kept("log_b%d" % s, [P, SLOTS, GROUP], F32, buffer)
+                for half in range(2):
+                    bank = psum.tile([P, 2, GROUP], F32, name="diff", bufs=4)
+                    for u in range(2):
+                        c = (2 * half + u) * P
+                        nc.tensor.matmul_mx(out=bank[:, u, :], lhsT=w4_slot_w[:, 2 * c : 2 * (c + P)].bitcast(FP4X4),
+                                            lhsT_scale=w4_slot_sc[:, c : c + P], rhs=v2_w[g].bitcast(FP8X4),
+                                            rhs_scale=v2_sc[:, g * GROUP : (g + 1) * GROUP], start=True, stop=True)
+                    nc.scalar.activation(out=logs[:, 2 * half : 2 * half + 2, :], in_=bank[:], func=ACT.Ln, bias=1.0)
+                return
             logs = log_b[s] = kept("log_b%d" % s, [P, 2, SLOTS, P], F32, buffer)
             for u in range(2):
                 j0 = g * GROUP + u * P
-                bank = psum.tile([P, PASS], F32, name=pair)
+                bank = psum.tile([P, PASS], F32, name="diff", bufs=4)
                 nc.tensor.matmul_mx(out=bank[:], lhsT=v2_w[g][:, u * P : (u + 1) * P].bitcast(FP8X4),
                                     lhsT_scale=v2_sc[:, j0 : j0 + P],
                                     rhs=w4_w[:, 2 * rb * PASS : 2 * (rb + 1) * PASS].bitcast(FP4X4),
@@ -170,10 +196,20 @@ def tile_list_metabolite_annotation_scores_kernel(
 
         def sample_logs(s, pair="x"):
             rb, g = steps[s]
-            if s == 2:
-                log_a[s] = kept("log_a2", [P, 2, SLOTS, P], F32, "wa_half0")
-            else:
-                log_a[s] = work.tile([P, 2, SLOTS, P], F32, name="log_a", bufs=4)
+            if s >= TURNED:
+                log_a[s] = work.tile([P, SLOTS, GROUP], F32, name="log_a_direct", bufs=DBUF)
+                for half in range(2):
+                    bank = psum.tile([P, 2, GROUP], F32, name=pair)
+                    for u in range(2):
+                        cols = slice((2 * half + u) * P, (2 * half + u + 1) * P)
+                        for kp in range(2):
+                            words, plane = wa_q[kp, rb]
+                            nc.tensor.matmul_mx(out=bank[:, u, :], lhsT=words[:, cols].bitcast(FP8X4), lhsT_scale=plane[:, cols],
+                                                rhs=v_w[kp][g].bitcast(FP8X4),
+                                                rhs_scale=v_sc[4 * kp : P, g * GROUP : (g + 1) * GROUP],
+                                                start=(kp == 0), stop=(kp == 1))
+                    nc.scalar.activation(out=log_a[s][:, 2 * half : 2 * half + 2, :], in_=bank[:], func=ACT.Ln, bias=1.0)
+                return
             for u in range(2):
                 j0 = g * GROUP + u * P
                 bank = psum.tile([P, PASS], F32, name=pair)
@@ -182,12 +218,16 @@ def tile_list_metabolite_annotation_scores_kernel(
                     nc.tensor.matmul_mx(out=bank[:], lhsT=v_w[kp][g][:, u * P : (u + 1) * P].bitcast(FP8X4),
                                         lhsT_scale=v_sc[4 * kp : P, j0 : j0 + P], rhs=words[:, 0:PASS].bitcast(FP8X4),
                                         rhs_scale=plane[:, 0:PASS], start=(kp == 0), stop=(kp == 1))
-                nc.scalar.activation(out=log_a[s][:, u].rearrange("p t m -> p (t m)"), in_=bank[:], func=ACT.Ln, bias=1.0)
+                if s == 2:
+                    log_a[s, u] = kept("log_a2%d" % u, [P, SLOTS, P], F32, "wa_half%d" % u)
+                else:
+                    log_a[s, u] = work.tile([P, SLOTS, P], F32, name="log_a", bufs=AHEAD)
+                nc.scalar.activation(out=log_a[s, u][:].rearrange("p t m -> p (t m)"), in_=bank[:], func=ACT.Ln, bias=1.0)
 
         def differences(s):
             for u in range(2):
                 d = diff[s, u] = psum.tile([P, SLOTS, P], F32, name="diff", bufs=4)[:]
-                terms = [log_a[s][:, u], minus[s, u]]
+                terms = [log_a[s, u][:], minus[s, u]]
                 for i, term in enumerate(terms):
                     for t in range(SLOTS):
                         nc.tensor.matmul(out=d[:, t, :], lhsT=term[:, t, :], rhs=identity[:], is_transpose=True,
@@ -216,6 +256,21 @@ def tile_list_metabolite_annotation_scores_kernel(
             dst = both[s][:, u, 1] if s == last else both[s][:, 1, u]
             nc.vector.tensor_tensor(out=dst.rearrange("p (j t) -> p j t", t=SLOTS),
                                     in0=diff[s, u].rearrange("p t j -> p j t"), in1=scaled[s][:, u], op=ALU.mult)
+
+        def subtract(s, part):
+            d = log_a[s][:, :, part]
+            nc.vector.tensor_tensor(out=d, in0=d, in1=log_b[s][:, :, part], op=ALU.subtract)
+            if part.start == 0:
+                scaled[s] = work.tile([P, SLOTS, GROUP], F32, name="scaled")
+            for t in range(SLOTS):
+                nc.scalar.activation(out=scaled[s][:, t, part], in_=d[:, t, :], func=ACT.Copy, scale=gains[:, 1, t : t + 1])
+
+        def products(s, part, e_dst, sq_dst, copy):
+            woven, apart = "p (c i t) -> p c t i", "p t (c i) -> p c t i"
+            e = scaled[s][:, :, part].rearrange(apart, i=LINE)
+            nc.vector.tensor_tensor(out=sq_dst.rearrange(woven, i=LINE, t=SLOTS), in0=e,
+                                    in1=log_a[s][:, :, part].rearrange(apart, i=LINE), op=ALU.mult)
+            copy(out=e_dst.rearrange(woven, i=LINE, t=SLOTS), in_=e)
 
         def quantise_group(s):
             columns = 2 * GROUP + (PASS if s in riders else 0)
@@ -270,8 +325,17 @@ def tile_list_metabolite_annotation_scores_kernel(
                 passes(banks["last", u][:, nt, :], rb, nt, quantised, first, P, half, rb == 0 and nt == 0, rb == 1 and nt == 3)
 
         last = len(steps) - 1
-        riders = (0, 2, 3)
-        homes = ["tab2_w", "tab_w0", "wa_raw00", "wa_raw10", "tab_w1", "wa_raw01", "log_b5", "log_b6"]
+        riders = (0, 2, WR1)
+        homes = ["tab2_w", "tab_w0", "wa_raw00", "wa_raw10", "tab_w1", "wa_raw01", "stage0", "log_b3"]
+
+        def round_rider(s):
+            raw, order = wr_raw[0 if s == 2 else 1], "p (c i j) -> p c j i"
+            dst = staged_values[s][:, SLOTS * 2 * GROUP :].rearrange(order, i=LINE, j=SLOTS)
+            src = raw[:].rearrange("p j (c i) -> p c j i", i=LINE)
+            for h in range(PIECES):
+                part = slice(h * P // PIECES, (h + 1) * P // PIECES)
+                nc.scalar.copy(out=dst[:, part], in_=src[:, part])
+
         staged_values = {}
 
         def stage_values(s):
@@ -285,14 +349,15 @@ def tile_list_metabolite_annotation_scores_kernel(
                                     scalar1=-1.0, scalar2=0.0, op0=ALU.mult, op1=ALU.add)
             minus[s, u] = negated[:]
 
-        for s in range(len(steps)):
+        for s in range(HEAD):
             library_logs(s, "xy"[s % 2])
             if s < EARLY:
                 negate(s, "stage1" if s == 1 else "log_b%d" % (s - 1) if s > 1 else None)
+        for s in range(EARLY, min(TURNED, 5)):
+            negate(s)
         v_w = [gather_words("v_w0", tab_w[0], list8, [2, groups]), gather_words("v_w1", tab_w[1], list8, [1, 2, groups])]
-        negate(4)
-        sample_logs(0, "x")
-        sample_logs(1, "y")
+        sample_logs(0, "xy"[HEAD % 2])
+        sample_logs(1, "yx"[HEAD % 2])
         differences(0)
         wa_q[0, 1] = quantise("wa01", rounded(nc.vector.tensor_copy, wa_raw[0, 1], "stage2")[:], PASS)
         stage_values(0)
@@ -300,23 +365,32 @@ def tile_list_metabolite_annotation_scores_kernel(
         for h in range(2):
             nc.scalar.copy(out=rider[:, h], in_=wa_halves[h][:].rearrange("p j (c i) -> p c j i", i=LINE))
         scale(0, 0)
-        late = [(s, u) for s in range(EARLY + 1, last + 1) for u in range(2)]
+        late = [(s, u) for s in range(5, TURNED) for u in range(2)]
+        whole, flat = slice(0, GROUP), "p u c -> p (u c)"
         for s in range(len(steps)):
             if s + 2 <= last and s != 2:
-                sample_logs(s + 2, "y" if s + 2 in (3, 5) else "x")
-            if s < last:
+                sample_logs(s + 2)
+            if s + 1 < TURNED:
                 differences(s + 1)
+            if s < last:
                 stage_values(s + 1)
-            scale(s, 1)
+            if s < TURNED:
+                scale(s, 1)
+            elif s < last:
+                subtract(s + 1, whole if s + 1 < last else slice(0, P))
+            else:
+                subtract(last, slice(P, GROUP))
             if s >= 1:
                 carried = quantise_group(s - 1)
                 if s == 1:
                     wa_q[1, 1] = carried
                     sample_logs(4)
-                if s in (3, 4):
-                    wr_q[s - 3] = carried
+                if s in (3, WR1 + 1):
+                    wr_q[0 if s == 3 else 1] = carried
             if s < len(late):
                 negate_tile(*late[s], homes[s - 1] if s else "stage2")
+            if HEAD + s <= last:
+                library_logs(HEAD + s, "y", "stage0" if s == 0 else "log_b1")
             if s == 5:
                 score_passes(0, 0)
             if s >= 6:
@@ -326,16 +400,27 @@ def tile_list_metabolite_annotation_scores_kernel(
             if s == last:
                 for u in range(2):
                     last_passes(0, u)
-            square(s, 0)
-            if s < last:
-                scale(s + 1, 0)
-            else:
                 score_passes(1, 2)
-                last_passes(1, 0)
-            square(s, 1)
-            if s in (1, 2):
-                nc.scalar.copy(out=staged_values[s + 1][:, SLOTS * 2 * GROUP :].rearrange("p (c i j) -> p c j i", i=LINE, j=SLOTS),
-                               in_=wr_raw[s - 1][:].rearrange("p j (c i) -> p c j i", i=LINE))
+            if s < TURNED:
+                square(s, 0)
+                if s + 1 < TURNED:
+                    scale(s + 1, 0)
+                elif s < last:
+                    subtract(s + 1, whole if s + 1 < last else slice(0, P))
+                else:
+                    last_passes(1, 0)
+                square(s, 1)
+            elif s < last:
+                products(s, whole, both[s][:, 0].rearrange(flat), both[s][:, 1].rearrange(flat),
+                         nc.scalar.copy if s in ON_SCALAR else nc.vector.tensor_copy)
+            else:
+                for u in range(2):
+                    products(last, slice(u * P, (u + 1) * P), both[last][:, u, 0], both[last][:, u, 1],
+                             nc.scalar.copy if u < LAST_S else nc.vector.tensor_copy)
+                    if u == 0:
+                        last_passes(1, 0)
+            if s + 1 in (2, WR1):
+                round_rider(s + 1)
         last_passes(1, 1)
         store_scores(2)
         for u in range(2):

@@ -25,12 +25,15 @@ GROUP = 256
 LINE = 4
 EARLY = 3
 TURNED = 5
+WR0 = 2
+SHARE = 256
+ALT = 0
 WR1 = 4
 HEAD = 8
 AHEAD = 3
-ON_SCALAR = [5]
-LAST_S = 1
-DBUF = 3
+ON_SCALAR = [6]
+LAST_S = 0
+DBUF = 2
 PIECES = 2
 
 
@@ -164,7 +167,7 @@ def tile_list_metabolite_annotation_scores_kernel(
             if s >= TURNED:
                 logs = log_b[s] = kept("log_b%d" % s, [P, SLOTS, GROUP], F32, buffer)
                 for half in range(2):
-                    bank = psum.tile([P, 2, GROUP], F32, name="diff", bufs=4)
+                    bank = psum.tile([P, 2, GROUP], F32, name="diff" if s < HEAD else "y", bufs=4 if s < HEAD else 2)
                     for u in range(2):
                         c = (2 * half + u) * P
                         nc.tensor.matmul_mx(out=bank[:, u, :], lhsT=w4_slot_w[:, 2 * c : 2 * (c + P)].bitcast(FP4X4),
@@ -194,7 +197,7 @@ def tile_list_metabolite_annotation_scores_kernel(
             for u in range(2):
                 minus[s, u] = negated[:, u]
 
-        def sample_logs(s, pair="x"):
+        def sample_logs(s, pair="x", tiles=(0, 1)):
             rb, g = steps[s]
             if s >= TURNED:
                 log_a[s] = work.tile([P, SLOTS, GROUP], F32, name="log_a_direct", bufs=DBUF)
@@ -210,7 +213,7 @@ def tile_list_metabolite_annotation_scores_kernel(
                                                 start=(kp == 0), stop=(kp == 1))
                     nc.scalar.activation(out=log_a[s][:, 2 * half : 2 * half + 2, :], in_=bank[:], func=ACT.Ln, bias=1.0)
                 return
-            for u in range(2):
+            for u in tiles:
                 j0 = g * GROUP + u * P
                 bank = psum.tile([P, PASS], F32, name=pair)
                 for kp in range(2):
@@ -224,8 +227,8 @@ def tile_list_metabolite_annotation_scores_kernel(
                     log_a[s, u] = work.tile([P, SLOTS, P], F32, name="log_a", bufs=AHEAD)
                 nc.scalar.activation(out=log_a[s, u][:].rearrange("p t m -> p (t m)"), in_=bank[:], func=ACT.Ln, bias=1.0)
 
-        def differences(s):
-            for u in range(2):
+        def differences(s, tiles=(0, 1)):
+            for u in tiles:
                 d = diff[s, u] = psum.tile([P, SLOTS, P], F32, name="diff", bufs=4)[:]
                 terms = [log_a[s, u][:], minus[s, u]]
                 for i, term in enumerate(terms):
@@ -248,9 +251,11 @@ def tile_list_metabolite_annotation_scores_kernel(
                 nc.gpsimd.tensor_scalar(out=both[s][:, u, 0], in0=scaled[s][:, u].rearrange("p j t -> p (j t)"),
                                         scalar1=1.0, scalar2=0.0, op0=ALU.mult, op1=ALU.add)
             elif u == 1:
-                nc.gpsimd.tensor_scalar(out=both[s][:, 0].rearrange("p u c -> p (u c)"),
-                                        in0=scaled[s][:].rearrange("p u j t -> p (u j t)"),
-                                        scalar1=1.0, scalar2=0.0, op0=ALU.mult, op1=ALU.add)
+                dst, src = both[s][:, 0].rearrange("p u c -> p (u c)"), scaled[s][:].rearrange("p u j t -> p (u j t)")
+                nc.gpsimd.tensor_scalar(out=dst[:, SHARE:], in0=src[:, SHARE:], scalar1=1.0, scalar2=0.0,
+                                        op0=ALU.mult, op1=ALU.add)
+                if SHARE:
+                    nc.scalar.copy(out=dst[:, 0:SHARE], in_=src[:, 0:SHARE])
 
         def square(s, u):
             dst = both[s][:, u, 1] if s == last else both[s][:, 1, u]
@@ -304,32 +309,36 @@ def tile_list_metabolite_annotation_scores_kernel(
         def store_scores(g):
             for pair in range(2):
                 staged = work.tile([P, 2, GROUP], F32, name="staged%d" % pair)
-                copy = nc.vector.tensor_copy if g == groups - 2 and pair == 1 else nc.scalar.copy
-                copy(out=staged[:], in_=banks[g, pair][:])
+                nc.scalar.copy(out=staged[:], in_=banks[g, pair][:])
                 nc.sync.dma_start(out=rows[:, 2 * pair : 2 * pair + 2, g * GROUP : (g + 1) * GROUP], in_=staged[:])
 
         def store_last(u):
-            staged = work.tile([P, SLOTS, P], F32, name="staged_last")
-            (nc.scalar.copy if u == 0 else nc.vector.tensor_copy)(out=staged[:], in_=banks["last", u])
             j0 = S - GROUP + u * P
-            nc.sync.dma_start(out=rows[:, :, j0 : j0 + P], in_=staged[:])
+            for i, bank in enumerate(banks["last", u]):
+                count = 4 // len(banks["last", u])
+                staged = kept("staged_last%d%d" % (u, i), [P, count, P], F32, None if u else homes[last])
+                (nc.scalar.copy if (u, i) == (1, 0) else nc.vector.tensor_copy)(out=staged[:], in_=bank[:, 0:count, :])
+                nc.sync.dma_start(out=rows[:, i * count : (i + 1) * count, j0 : j0 + P], in_=staged[:])
 
         def last_passes(rb, u):
+            count = 4 // (u + 1)
             if rb == 0:
-                banks["last", u] = psum.tile([P, SLOTS, P], F32, name="diff", bufs=4)[:]
+                banks["last", u] = [psum.tile([P, SLOTS, P], F32, name="diff", bufs=4) for i in range(u + 1)]
                 quantised, first, half = both_q[0, groups - 1], u * P, GROUP
             else:
                 quantised = quantise("both_last%d" % u, both[last][:, u].rearrange("p s c -> p (s c)"), 2 * P)
                 first, half = 0, P
             for nt in range(4):
-                passes(banks["last", u][:, nt, :], rb, nt, quantised, first, P, half, rb == 0 and nt == 0, rb == 1 and nt == 3)
+                i, k = divmod(nt, count)
+                passes(banks["last", u][i][:, k, :], rb, nt, quantised, first, P, half,
+                       rb == 0 and k == 0, rb == 1 and k == count - 1)
 
         last = len(steps) - 1
-        riders = (0, 2, WR1)
-        homes = ["tab2_w", "tab_w0", "wa_raw00", "wa_raw10", "tab_w1", "wa_raw01", "stage0", "log_b3"]
+        riders = (0, WR0, WR1)
+        homes = ["tab2_w", "tab_w0", "wa_raw00", "wa_raw10", "tab_w1", "wa_raw01", "log_b2", "log_b3"]
 
         def round_rider(s):
-            raw, order = wr_raw[0 if s == 2 else 1], "p (c i j) -> p c j i"
+            raw, order = wr_raw[0 if s == WR0 else 1], "p (c i j) -> p c j i"
             dst = staged_values[s][:, SLOTS * 2 * GROUP :].rearrange(order, i=LINE, j=SLOTS)
             src = raw[:].rearrange("p j (c i) -> p c j i", i=LINE)
             for h in range(PIECES):
@@ -353,24 +362,34 @@ def tile_list_metabolite_annotation_scores_kernel(
             library_logs(s, "xy"[s % 2])
             if s < EARLY:
                 negate(s, "stage1" if s == 1 else "log_b%d" % (s - 1) if s > 1 else None)
-        for s in range(EARLY, min(TURNED, 5)):
+        for s in range(EARLY, TURNED):
             negate(s)
         v_w = [gather_words("v_w0", tab_w[0], list8, [2, groups]), gather_words("v_w1", tab_w[1], list8, [1, 2, groups])]
         sample_logs(0, "xy"[HEAD % 2])
         sample_logs(1, "yx"[HEAD % 2])
-        differences(0)
-        wa_q[0, 1] = quantise("wa01", rounded(nc.vector.tensor_copy, wa_raw[0, 1], "stage2")[:], PASS)
+        differences(0, [0])
+        wa_rounded = rounded(nc.vector.tensor_copy, wa_raw[0, 1], "stage2")
+        scale(0, 0)
+        wa_q[0, 1] = quantise("wa01", wa_rounded[:], PASS)
         stage_values(0)
         rider = staged_values[0][:, SLOTS * 2 * GROUP :].rearrange("p (i h c j) -> p h c j i", i=LINE, h=2, j=SLOTS)
         for h in range(2):
             nc.scalar.copy(out=rider[:, h], in_=wa_halves[h][:].rearrange("p j (c i) -> p c j i", i=LINE))
-        scale(0, 0)
-        late = [(s, u) for s in range(5, TURNED) for u in range(2)]
+        sample_logs(2, "x", [0])
+        differences(0, [1])
+        differences(1, [0])
+        sample_logs(2, "x", [1])
+        differences(1, [1])
         whole, flat = slice(0, GROUP), "p u c -> p (u c)"
         for s in range(len(steps)):
-            if s + 2 <= last and s != 2:
-                sample_logs(s + 2)
-            if s + 1 < TURNED:
+            if s + 2 <= last and s not in (0, 2):
+                if s == 1 and ALT:
+                    for u in range(2):
+                        differences(2, [u])
+                        sample_logs(3, "x", [u])
+                else:
+                    sample_logs(s + 2)
+            if 1 < s + 1 < TURNED and not (s == 1 and ALT):
                 differences(s + 1)
             if s < last:
                 stage_values(s + 1)
@@ -385,12 +404,8 @@ def tile_list_metabolite_annotation_scores_kernel(
                 if s == 1:
                     wa_q[1, 1] = carried
                     sample_logs(4)
-                if s in (3, WR1 + 1):
-                    wr_q[0 if s == 3 else 1] = carried
-            if s < len(late):
-                negate_tile(*late[s], homes[s - 1] if s else "stage2")
-            if HEAD + s <= last:
-                library_logs(HEAD + s, "y", "stage0" if s == 0 else "log_b1")
+                if s in (WR0 + 1, WR1 + 1):
+                    wr_q[0 if s == WR0 + 1 else 1] = carried
             if s == 5:
                 score_passes(0, 0)
             if s >= 6:
@@ -419,7 +434,7 @@ def tile_list_metabolite_annotation_scores_kernel(
                              nc.scalar.copy if u < LAST_S else nc.vector.tensor_copy)
                     if u == 0:
                         last_passes(1, 0)
-            if s + 1 in (2, WR1):
+            if s + 1 in (WR0, WR1):
                 round_rider(s + 1)
         last_passes(1, 1)
         store_scores(2)

@@ -23,13 +23,16 @@ PASS = P * SLOTS
 QUADRANT = 32
 GROUP = 256
 LINE = 4
-EARLY = 3
+EARLY = 4
+BAT = 2
+GATE = ["log_b0", "wa_half0"]
+NGATE = None
 TURNED = 5
 WR0 = 2
 SHARE = 256
 ALT = 0
 WR1 = 4
-HEAD = 8
+HEAD = 7
 AHEAD = 3
 ON_SCALAR = [6]
 LAST_S = 0
@@ -155,8 +158,14 @@ def tile_list_metabolite_annotation_scores_kernel(
         w8_w = kept("w8_w", [P, 2, N], U32)
         nc.sync.dma_start(out=as_words(w8_w[:]), in_=as_words(w8_words.rearrange("b p n i -> p b (n i)")))
         wr_raw.append(load_rows("wr_raw1", wr[PASS : 2 * PASS, :]))
+        first_values = kept("first_values", [P, 2, SLOTS * PASS], BF16, "stage1")
         for kp in range(2):
-            wa_q[kp, 0] = quantise("wa%d0" % kp, rounded(nc.vector.tensor_copy, wa_raw[kp, 0], "stage%d" % kp)[:], PASS)
+            copy = nc.vector.tensor_copy if kp else nc.scalar.copy
+            copy(out=first_values[:, kp].rearrange("p (i c j) -> p c j i", i=LINE, j=SLOTS),
+                 in_=wa_raw[kp, 0][:].rearrange("p j (c i) -> p c j i", i=LINE))
+        words, plane = quantise("wa_first", first_values[:].rearrange("p k c -> p (k c)"), 2 * PASS)
+        for kp in range(2):
+            wa_q[kp, 0] = words[:, kp * PASS : (kp + 1) * PASS], plane[:, kp * PASS : (kp + 1) * PASS]
 
         minus = {}
         log_b, log_a, diff, scaled, both, both_q, banks = {}, {}, {}, {}, {}, {}, {}
@@ -363,7 +372,7 @@ def tile_list_metabolite_annotation_scores_kernel(
             if s < EARLY:
                 negate(s, "stage1" if s == 1 else "log_b%d" % (s - 1) if s > 1 else None)
         for s in range(EARLY, TURNED):
-            negate(s)
+            negate(s, NGATE)
         v_w = [gather_words("v_w0", tab_w[0], list8, [2, groups]), gather_words("v_w1", tab_w[1], list8, [1, 2, groups])]
         sample_logs(0, "xy"[HEAD % 2])
         sample_logs(1, "yx"[HEAD % 2])
@@ -406,6 +415,9 @@ def tile_list_metabolite_annotation_scores_kernel(
                     sample_logs(4)
                 if s in (WR0 + 1, WR1 + 1):
                     wr_q[0 if s == WR0 + 1 else 1] = carried
+            if s == BAT:
+                for late in range(HEAD, last + 1):
+                    library_logs(late, "y", GATE[late - HEAD])
             if s == 5:
                 score_passes(0, 0)
             if s >= 6:

@@ -22,22 +22,11 @@ SLOTS = 4
 PASS = P * SLOTS
 QUADRANT = 32
 GROUP = 256
+GROUPS = S // GROUP
 LINE = 4
-EARLY = 4
-BAT = 2
-GATE = ["log_b0", "wa_half0"]
-NGATE = None
 TURNED = 5
-WR0 = 2
-SHARE = 256
-ALT = 0
-WR1 = 4
-HEAD = 7
-AHEAD = 3
-ON_SCALAR = [6]
-LAST_S = 0
-DBUF = 2
-PIECES = 2
+STEP = SLOTS * GROUP
+BLOCK = SLOTS * PASS
 
 
 def tile_list_metabolite_annotation_scores_kernel(
@@ -47,12 +36,14 @@ def tile_list_metabolite_annotation_scores_kernel(
     nc = tc.nc
     with ExitStack() as ctx:
         keep = ctx.enter_context(tc.tile_pool(name="keep", bufs=1))
-        stage = ctx.enter_context(tc.tile_pool(name="stage", bufs=2))
         work = ctx.enter_context(tc.tile_pool(name="work", bufs=2))
-        psum = ctx.enter_context(tc.psum_pool(name="psum", bufs=2))
+        psum = ctx.enter_context(tc.psum_pool(name="psum", bufs=1))
 
         def kept(name, shape, dtype, buffer=None):
             return keep.tile(shape, dtype, name=name, tag=buffer or name, align_bytes=64)
+
+        def bank(i, shape):
+            return psum.tile(shape, F32, name="bank%d" % i)
 
         def as_words(ap):
             return ap.bitcast(I32)
@@ -65,252 +56,228 @@ def tile_list_metabolite_annotation_scores_kernel(
         w8_sc = kept("w8_sc", [P, 2 * N], U8)
         w4_w = kept("w4_w", [P, 2 * H], U8)
         identity = kept("identity", [P, P], F32)
-
-        nc.gpsimd.memset(as_words(tab2_sc[:]), 0)
-        nc.vector.memset(as_words(tab_sc[:]), 0)
-        nc.vector.memset(as_words(w4_sc[:]), 0)
-        nc.vector.memset(as_words(w8_sc[:]), 0)
+        v_sc = kept("v_sc", [P, 2 * S], U8)
+        for plane in (tab2_sc, w4_sc, tab_sc, w8_sc, v_sc):
+            nc.vector.memset(as_words(plane[:]), 0)
         make_identity(nc, identity[:])
+        gains = kept("gains", [P, 2, SLOTS], F32)
+        nc.gpsimd.dma_start(out=gains[:], in_=gain.rearrange("(b p t) -> p b t", b=2, t=SLOTS))
 
-        def load_plane(queue, plane, rows):
+        def load_plane(plane, rows):
             for r in range(4):
-                queue.dma_start(out=plane[r:P:QUADRANT], in_=rows(slice(r, 16, 4)))
+                nc.sync.dma_start(out=plane[r:P:QUADRANT], in_=rows(slice(r, 16, 4)))
 
         def load_table(name, words):
             tile = kept(name, [P, T], U32)
             nc.sync.dma_start(out=as_words(tile[:]), in_=as_words(words.rearrange("p t i -> p (t i)")))
             return tile
 
-        def load_rows(name, rows, buffer=None):
-            tile = kept(name, [P, SLOTS, PASS], F32, buffer)
+        def load_rows(name, rows):
+            tile = kept(name, [P, SLOTS, PASS], F32)
             nc.sync.dma_start(out=tile[:], in_=rows.rearrange("(p j) c -> p j c", j=SLOTS))
             return tile
 
-        def load_wa(kp, rb, buffer=None):
-            return load_rows("wa_raw%d%d" % (kp, rb), wa[kp * PASS : (kp + 1) * PASS, rb * PASS : (rb + 1) * PASS], buffer)
+        def load_wa(kp, rb):
+            return load_rows("wa_raw%d%d" % (kp, rb), wa[kp * PASS : (kp + 1) * PASS, rb * PASS : (rb + 1) * PASS])
 
-        def gather_words(name, table, offsets, cuts, buffers={}):
-            pieces = []
+        def gather(tile, table, offsets, cuts):
             for first, end in zip([0] + cuts, cuts):
-                tile = kept("%s_%d" % (name, first), [P, end - first, GROUP], U32, buffers.get(first))
-                nc.vector.tensor_copy(tile[:].rearrange("p g c -> p (g c)"),
-                                      table[:].indirect(offsets[:, first * GROUP // 16 : end * GROUP // 16]))
-                pieces.extend(tile[:, g] for g in range(end - first))
-            return pieces
+                nc.vector.tensor_copy(tile[:, first:end], table[:].indirect(offsets[:, first // 16 : end // 16]))
 
-        def rounded(copy, raw, buffer, order="p (i c j) -> p c j i"):
-            tile = kept("rounded", [P, SLOTS * PASS], BF16, buffer)
-            copy(out=tile[:].rearrange(order, i=LINE, j=SLOTS),
-                 in_=raw[:].rearrange("p j (c i) -> p c j i", i=LINE))
-            return tile
+        def pool_copy(out, in_, factor=1.0):
+            nc.gpsimd.tensor_scalar(out=out, in0=in_, scalar1=factor, scalar2=0.0, op0=ALU.mult, op1=ALU.add)
 
-        def quantise(name, values, columns, buffer=None):
-            words = kept(name + "_w", [P, columns], U32, buffer)
+        def quantise(name, values, columns):
+            words = kept(name + "_w", [P, columns], U32)
             plane = kept(name + "_sc", [P, columns], U8)
             nc.vector.quantize_mx(out=words[:].bitcast(FP8X4), scales=plane[:], in_=values)
             return words, plane
 
+        def window(pair, first, width):
+            return pair[0][:, first : first + width], pair[1][:, first : first + width]
+
         wa_raw = {}
         nc.sync.dma_start(list1[:], offs2)
         nc.sync.dma_start(list8[:], offs)
-        load_plane(nc.sync, as_words(tab2_sc[:]), lambda q: as_words(tab2_scales[0])[q, :])
+        load_plane(as_words(tab2_sc[:]), lambda q: as_words(tab2_scales[0])[q, :])
         tab2_w = load_table("tab2_w", tab2_words[0])
         nc.sync.dma_start(out=as_words(w4_w[:]), in_=as_words(w4_words[0]))
-        load_plane(nc.sync, as_words(w4_sc[:]), lambda q: as_words(w4_scales[0])[q, :])
-        for kp in range(2):
-            nc.sync.dma_start(out=as_words(tab_sc[:])[4 * kp : P : 8, :], in_=as_words(tab_scales[kp]))
-        for kp in range(2):
-            wa_raw[kp, 0] = load_wa(kp, 0)
-        gains = kept("gains", [P, 2, SLOTS], F32)
-        nc.gpsimd.dma_start(out=gains[:], in_=gain.rearrange("(b p t) -> p b t", b=2, t=SLOTS))
+        load_plane(as_words(w4_sc[:]), lambda q: as_words(w4_scales[0])[q, :])
+        wa_raw[0, 0] = load_wa(0, 0)
+        nc.sync.dma_start(out=as_words(tab_sc[:])[0:P:4, :], in_=as_words(tab_scales).rearrange("a q c -> q a c"))
         tab_w = [load_table("tab_w0", tab_words[0])]
-
-        wa_q, wr_q = {}, {}
-        groups = S // GROUP
-        v2_sc = kept("v2_sc", [P, S], U8)
-        nc.vector.tensor_copy(v2_sc[:], tab2_sc[:].indirect(list1[:]))
-        v2_w = gather_words("v2_w", tab2_w, list1, [1, 2, groups])
-        if TURNED < 8:
-            w4_slot_w = kept("w4_slot_w", [P, 2 * PASS], U8)
-            nc.vector.tensor_copy(out=w4_slot_w[:].bitcast(U16).rearrange("p (t m) -> p m t", t=SLOTS),
-                                  in_=w4_w[:, 2 * PASS : 4 * PASS].bitcast(U16).rearrange("p (m t) -> p m t", t=SLOTS))
-            w4_slot_sc = kept("w4_slot_sc", [P, PASS], U8)
-            nc.vector.tensor_copy(out=w4_slot_sc[:].rearrange("p (t m) -> p m t", t=SLOTS),
-                                  in_=w4_sc[:, PASS : 2 * PASS].rearrange("p (m t) -> p m t", t=SLOTS))
-        picked_sc = kept("picked_sc", [P, S], U8)
-        nc.vector.tensor_copy(picked_sc[:], tab_sc[:].indirect(list8[:]))
-        v_sc = kept("v_sc", [P, S], U8)
-        nc.vector.tensor_copy(as_words(v_sc[:]), as_words(picked_sc[:]))
-        for kp in range(2):
-            for r in range(1, 4):
-                nc.sync.dma_start(out=as_words(v_sc[:])[4 * kp + r : P : QUADRANT, :],
-                                  in_=as_words(picked_sc[:])[4 * kp + 8 * r : P : QUADRANT, :])
+        wa_raw[1, 0] = load_wa(1, 0)
         tab_w.append(load_table("tab_w1", tab_words[1]))
+
+        v2_sc = kept("v2_sc", [P, S], U8)
+        gather(v2_sc, tab2_sc, list1, [S])
+        v2_w = kept("v2_w", [P, S], U32)
+        gather(v2_w, tab2_w, list1, [GROUP, 2 * GROUP, S])
+        w4_slot_w = kept("w4_slot_w", [P, 2 * PASS], U8)
+        nc.gpsimd.tensor_copy(out=w4_slot_w[:].rearrange("p (t m b) -> p t m b", t=SLOTS, b=2),
+                              in_=w4_w[:, 2 * PASS : 4 * PASS].rearrange("p (m t b) -> p t m b", t=SLOTS, b=2))
+        picked_sc = kept("picked_sc", [P, S], U8)
+        gather(picked_sc, tab_sc, list8, [S])
+        for d in range(0, P, QUADRANT):
+            nc.sync.dma_start(out=as_words(v_sc[:])[d : d + 4, :], in_=as_words(picked_sc[:])[d : d + QUADRANT : 4, :])
+        w4_slot_sc = kept("w4_slot_sc", [P, PASS], U8)
+        nc.gpsimd.tensor_copy(out=w4_slot_sc[:].rearrange("p (t m) -> p t m", t=SLOTS),
+                              in_=w4_sc[:, PASS : 2 * PASS].rearrange("p (m t) -> p t m", t=SLOTS))
         wa_raw[0, 1] = load_wa(0, 1)
-        wa_halves = []
-        for h in range(2):
-            wa_halves.append(kept("wa_half%d" % h, [P, SLOTS, PASS // 2], F32))
-            c0 = PASS + h * PASS // 2
-            nc.sync.dma_start(out=wa_halves[h][:], in_=wa[PASS:K, c0 : c0 + PASS // 2].rearrange("(p j) c -> p j c", j=SLOTS))
-        wr_raw = [load_rows("wr_raw0", wr[0:PASS, :])]
-        load_plane(nc.sync, as_words(w8_sc[:]).rearrange("p (b n) -> p b n", b=2),
+        wa_raw[1, 1] = load_wa(1, 1)
+        wr_raw = [load_rows("wr_raw%d" % rb, wr[rb * PASS : (rb + 1) * PASS, :]) for rb in range(2)]
+        load_plane(as_words(w8_sc[:]).rearrange("p (b n) -> p b n", b=2),
                    lambda q: as_words(w8_scales)[:, q, :].rearrange("b r n -> r b n"))
         w8_w = kept("w8_w", [P, 2, N], U32)
         nc.sync.dma_start(out=as_words(w8_w[:]), in_=as_words(w8_words.rearrange("b p n i -> p b (n i)")))
-        wr_raw.append(load_rows("wr_raw1", wr[PASS : 2 * PASS, :]))
-        first_values = kept("first_values", [P, 2, SLOTS * PASS], BF16, "stage1")
-        for kp in range(2):
-            copy = nc.vector.tensor_copy if kp else nc.scalar.copy
-            copy(out=first_values[:, kp].rearrange("p (i c j) -> p c j i", i=LINE, j=SLOTS),
-                 in_=wa_raw[kp, 0][:].rearrange("p j (c i) -> p c j i", i=LINE))
-        words, plane = quantise("wa_first", first_values[:].rearrange("p k c -> p (k c)"), 2 * PASS)
-        for kp in range(2):
-            wa_q[kp, 0] = words[:, kp * PASS : (kp + 1) * PASS], plane[:, kp * PASS : (kp + 1) * PASS]
 
-        minus = {}
-        log_b, log_a, diff, scaled, both, both_q, banks = {}, {}, {}, {}, {}, {}, {}
-        steps = [(rb, g) for rb in range(2) for g in range(groups)]
+        steps = [(rb, g) for rb in range(2) for g in range(GROUPS)]
+        last = len(steps) - 1
+        log_b, log_a, minus, diff, scaled, made, banks, wa_q, wr_q = {}, {}, {}, {}, {}, {}, {}, {}, {}
 
-        def library_logs(s, pair, buffer=None):
+        def library_logs(s, first_bank, logs):
             rb, g = steps[s]
-            if s >= TURNED:
-                logs = log_b[s] = kept("log_b%d" % s, [P, SLOTS, GROUP], F32, buffer)
-                for half in range(2):
-                    bank = psum.tile([P, 2, GROUP], F32, name="diff" if s < HEAD else "y", bufs=4 if s < HEAD else 2)
-                    for u in range(2):
-                        c = (2 * half + u) * P
-                        nc.tensor.matmul_mx(out=bank[:, u, :], lhsT=w4_slot_w[:, 2 * c : 2 * (c + P)].bitcast(FP4X4),
-                                            lhsT_scale=w4_slot_sc[:, c : c + P], rhs=v2_w[g].bitcast(FP8X4),
-                                            rhs_scale=v2_sc[:, g * GROUP : (g + 1) * GROUP], start=True, stop=True)
-                    nc.scalar.activation(out=logs[:, 2 * half : 2 * half + 2, :], in_=bank[:], func=ACT.Ln, bias=1.0)
-                return
-            logs = log_b[s] = kept("log_b%d" % s, [P, 2, SLOTS, P], F32, buffer)
+            log_b[s] = logs
             for u in range(2):
-                j0 = g * GROUP + u * P
-                bank = psum.tile([P, PASS], F32, name="diff", bufs=4)
-                nc.tensor.matmul_mx(out=bank[:], lhsT=v2_w[g][:, u * P : (u + 1) * P].bitcast(FP8X4),
-                                    lhsT_scale=v2_sc[:, j0 : j0 + P],
-                                    rhs=w4_w[:, 2 * rb * PASS : 2 * (rb + 1) * PASS].bitcast(FP4X4),
-                                    rhs_scale=w4_sc[:, rb * PASS : (rb + 1) * PASS], start=True, stop=True)
-                nc.scalar.activation(out=logs[:, u].rearrange("p t m -> p m t"), in_=bank[:].rearrange("p (m t) -> p m t", t=SLOTS),
-                                     func=ACT.Ln, bias=1.0)
+                if s < TURNED:
+                    j0 = g * GROUP + u * P
+                    sums = bank(first_bank + u, [P, PASS])
+                    nc.tensor.matmul_mx(out=sums[:], lhsT=v2_w[:, j0 : j0 + P].bitcast(FP8X4), lhsT_scale=v2_sc[:, j0 : j0 + P],
+                                        rhs=w4_w[:, 2 * rb * PASS : 2 * (rb + 1) * PASS].bitcast(FP4X4),
+                                        rhs_scale=w4_sc[:, rb * PASS : (rb + 1) * PASS], start=True, stop=True)
+                    nc.scalar.activation(out=logs[:, u * PASS : (u + 1) * PASS].rearrange("p (t m) -> p t m", t=SLOTS),
+                                         in_=sums[:].rearrange("p (m t) -> p t m", t=SLOTS), func=ACT.Ln, bias=1.0)
+                else:
+                    sums = bank(first_bank + u, [P, 2, GROUP])
+                    entries = slice(g * GROUP, (g + 1) * GROUP)
+                    for i in range(2):
+                        c = (2 * u + i) * P
+                        nc.tensor.matmul_mx(out=sums[:, i, :], lhsT=w4_slot_w[:, 2 * c : 2 * (c + P)].bitcast(FP4X4),
+                                            lhsT_scale=w4_slot_sc[:, c : c + P], rhs=v2_w[:, entries].bitcast(FP8X4),
+                                            rhs_scale=v2_sc[:, entries], start=True, stop=True)
+                    nc.scalar.activation(out=logs[:, u * PASS : (u + 1) * PASS], in_=sums[:].rearrange("p i c -> p (i c)"),
+                                         func=ACT.Ln, bias=1.0)
 
-        def negate(s, buffer=None):
-            flat = "p u t m -> p (u t m)"
-            negated = kept("negated%d" % s, [P, 2, SLOTS, P], F32, buffer)
-            if s < EARLY:
-                nc.gpsimd.tensor_scalar(out=negated[:].rearrange(flat), in0=log_b[s][:].rearrange(flat),
-                                        scalar1=-1.0, scalar2=0.0, op0=ALU.mult, op1=ALU.add)
-            else:
-                nc.scalar.activation(out=negated[:], in_=log_b[s][:], func=ACT.Copy, scale=-1.0)
-            for u in range(2):
-                minus[s, u] = negated[:, u]
-
-        def sample_logs(s, pair="x", tiles=(0, 1)):
+        def sample_logs(s, tiles=(0, 1)):
             rb, g = steps[s]
-            if s >= TURNED:
-                log_a[s] = work.tile([P, SLOTS, GROUP], F32, name="log_a_direct", bufs=DBUF)
-                for half in range(2):
-                    bank = psum.tile([P, 2, GROUP], F32, name=pair)
-                    for u in range(2):
-                        cols = slice((2 * half + u) * P, (2 * half + u + 1) * P)
+            for u in tiles:
+                if s < TURNED:
+                    j0 = g * GROUP + u * P
+                    sums = bank(u + 6 * (1 - s % 2), [P, PASS])
+                    for kp in range(2):
+                        words, plane = wa_q[kp, rb]
+                        nc.tensor.matmul_mx(out=sums[:], lhsT=v_w[kp][:, j0 : j0 + P].bitcast(FP8X4),
+                                            lhsT_scale=v_sc[:, kp * S + j0 : kp * S + j0 + P], rhs=words.bitcast(FP8X4),
+                                            rhs_scale=plane, start=(kp == 0), stop=(kp == 1))
+                    log_a[s, u] = work.tile([P, SLOTS, P], F32, name="log_a", bufs=4)
+                    order = "p (t m) -> p t m" if rb else "p (m t) -> p t m"
+                    nc.scalar.activation(out=log_a[s, u][:], in_=sums[:].rearrange(order, t=SLOTS), func=ACT.Ln, bias=1.0)
+                else:
+                    if u == 0:
+                        log_a[s] = work.tile([P, SLOTS, GROUP], F32, name="log_a_direct", bufs=3)
+                    sums = bank(u + 4 * (1 - s % 2), [P, 2, GROUP])
+                    entries = slice(g * GROUP, (g + 1) * GROUP)
+                    for i in range(2):
+                        cols = slice((2 * u + i) * P, (2 * u + i + 1) * P)
                         for kp in range(2):
                             words, plane = wa_q[kp, rb]
-                            nc.tensor.matmul_mx(out=bank[:, u, :], lhsT=words[:, cols].bitcast(FP8X4), lhsT_scale=plane[:, cols],
-                                                rhs=v_w[kp][g].bitcast(FP8X4),
-                                                rhs_scale=v_sc[4 * kp : P, g * GROUP : (g + 1) * GROUP],
+                            nc.tensor.matmul_mx(out=sums[:, i, :], lhsT=words[:, cols].bitcast(FP8X4), lhsT_scale=plane[:, cols],
+                                                rhs=v_w[kp][:, entries].bitcast(FP8X4), rhs_scale=v_sc[:, kp * S + g * GROUP : kp * S + (g + 1) * GROUP],
                                                 start=(kp == 0), stop=(kp == 1))
-                    nc.scalar.activation(out=log_a[s][:, 2 * half : 2 * half + 2, :], in_=bank[:], func=ACT.Ln, bias=1.0)
-                return
-            for u in tiles:
-                j0 = g * GROUP + u * P
-                bank = psum.tile([P, PASS], F32, name=pair)
-                for kp in range(2):
-                    words, plane = wa_q[kp, rb]
-                    nc.tensor.matmul_mx(out=bank[:], lhsT=v_w[kp][g][:, u * P : (u + 1) * P].bitcast(FP8X4),
-                                        lhsT_scale=v_sc[4 * kp : P, j0 : j0 + P], rhs=words[:, 0:PASS].bitcast(FP8X4),
-                                        rhs_scale=plane[:, 0:PASS], start=(kp == 0), stop=(kp == 1))
-                if s == 2:
-                    log_a[s, u] = kept("log_a2%d" % u, [P, SLOTS, P], F32, "wa_half%d" % u)
-                else:
-                    log_a[s, u] = work.tile([P, SLOTS, P], F32, name="log_a", bufs=AHEAD)
-                nc.scalar.activation(out=log_a[s, u][:].rearrange("p t m -> p (t m)"), in_=bank[:], func=ACT.Ln, bias=1.0)
+                    nc.scalar.activation(out=log_a[s][:, 2 * u : 2 * u + 2, :], in_=sums[:], func=ACT.Ln, bias=1.0)
+
+        def turn(s, u, term, start, stop):
+            if start:
+                diff[s, u] = bank(2 + (2 * s + u) % 4, [P, SLOTS, P])
+            for t in range(SLOTS):
+                nc.tensor.matmul(out=diff[s, u][:, t, :], lhsT=term[:, t, :], rhs=identity[:], is_transpose=True,
+                                 start=(start and t == 0), stop=(stop and t == SLOTS - 1))
+
+        def minus_tile(s, u):
+            return minus[s][:, u * PASS : (u + 1) * PASS].rearrange("p (t m) -> p t m", t=SLOTS)
 
         def differences(s, tiles=(0, 1)):
             for u in tiles:
-                d = diff[s, u] = psum.tile([P, SLOTS, P], F32, name="diff", bufs=4)[:]
-                terms = [log_a[s, u][:], minus[s, u]]
-                for i, term in enumerate(terms):
-                    for t in range(SLOTS):
-                        nc.tensor.matmul(out=d[:, t, :], lhsT=term[:, t, :], rhs=identity[:], is_transpose=True,
-                                         start=(i == 0 and t == 0), stop=(i == len(terms) - 1 and t == SLOTS - 1))
+                turn(s, u, log_a[s, u][:], True, False)
+                turn(s, u, minus_tile(s, u), False, True)
+
+        values = kept("values", [P, 2 * BLOCK + 3 * STEP], BF16)
+        e_values = values[:, BLOCK + STEP : BLOCK + 2 * STEP]
+
+        def sq_values(s):
+            first = BLOCK + 2 * STEP * (s % 2)
+            return values[:, first : first + STEP]
+
+        def rider_values(s):
+            first = (BLOCK + 3 * STEP) * (s % 2)
+            return values[:, first : first + BLOCK]
+
+        def weave(raw, dst, order, part=slice(0, P)):
+            return (dst.rearrange(order, i=LINE, j=SLOTS)[:, part], raw[:].rearrange("p j (c i) -> p c j i", i=LINE)[:, part])
+
+        natural, by_slot = "p (c i j) -> p c j i", "p (i c j) -> p c j i"
+
+        def round_rider(s, raw, order):
+            dst, src = weave(raw, rider_values(s), order)
+            nc.scalar.copy(out=dst, in_=src)
+
+        def quantise_step(s, rider=False):
+            extra = BLOCK if rider else 0
+            if s % 2:
+                first, places = BLOCK + STEP, (0, GROUP, 2 * GROUP)
+            else:
+                first, places = BLOCK - extra, (extra // SLOTS + GROUP, extra // SLOTS, 0)
+            pair = quantise("step%d" % s, values[:, first : first + 2 * STEP + extra], (2 * STEP + extra) // SLOTS)
+            made[steps[s]] = window(pair, places[0], GROUP), window(pair, places[1], GROUP)
+            return window(pair, places[2], PASS) if rider else None
 
         def scale(s, u):
             rb = steps[s][0]
             if u == 0:
-                if s == 0:
-                    scaled[s] = kept("scaled0", [P, 2, P, SLOTS], F32, "wa_raw01")
-                else:
-                    scaled[s] = work.tile([P, 2, P, SLOTS], F32, name="scaled")
-            nc.vector.tensor_tensor(out=scaled[s][:, u], in0=diff[s, u].rearrange("p t j -> p j t"),
+                scaled[s] = work.tile([P, 2, P, SLOTS], F32, name="scaled")
+            nc.vector.tensor_tensor(out=scaled[s][:, u], in0=diff[s, u][:].rearrange("p t j -> p j t"),
                                     in1=gains[:, rb : rb + 1, :].to_broadcast([P, P, SLOTS]), op=ALU.mult)
-            if s == last and u == 1:
-                nc.scalar.copy(out=both[s][:, u, 0], in_=scaled[s][:, u].rearrange("p j t -> p (j t)"))
-            elif s == last:
-                nc.gpsimd.tensor_scalar(out=both[s][:, u, 0], in0=scaled[s][:, u].rearrange("p j t -> p (j t)"),
-                                        scalar1=1.0, scalar2=0.0, op0=ALU.mult, op1=ALU.add)
-            elif u == 1:
-                dst, src = both[s][:, 0].rearrange("p u c -> p (u c)"), scaled[s][:].rearrange("p u j t -> p (u j t)")
-                nc.gpsimd.tensor_scalar(out=dst[:, SHARE:], in0=src[:, SHARE:], scalar1=1.0, scalar2=0.0,
-                                        op0=ALU.mult, op1=ALU.add)
-                if SHARE:
-                    nc.scalar.copy(out=dst[:, 0:SHARE], in_=src[:, 0:SHARE])
+
+        def round_e(s):
+            pool_copy(e_values, scaled[s][:].rearrange("p u j t -> p (u j t)"))
 
         def square(s, u):
-            dst = both[s][:, u, 1] if s == last else both[s][:, 1, u]
-            nc.vector.tensor_tensor(out=dst.rearrange("p (j t) -> p j t", t=SLOTS),
-                                    in0=diff[s, u].rearrange("p t j -> p j t"), in1=scaled[s][:, u], op=ALU.mult)
+            nc.vector.tensor_tensor(out=sq_values(s)[:, u * PASS : (u + 1) * PASS].rearrange("p (j t) -> p j t", t=SLOTS),
+                                    in0=diff[s, u][:].rearrange("p t j -> p j t"), in1=scaled[s][:, u], op=ALU.mult)
 
         def subtract(s, part):
             d = log_a[s][:, :, part]
-            nc.vector.tensor_tensor(out=d, in0=d, in1=log_b[s][:, :, part], op=ALU.subtract)
+            nc.vector.tensor_tensor(out=d, in0=d, in1=log_b[s].rearrange("p (t c) -> p t c", t=SLOTS)[:, :, part], op=ALU.subtract)
             if part.start == 0:
                 scaled[s] = work.tile([P, SLOTS, GROUP], F32, name="scaled")
             for t in range(SLOTS):
                 nc.scalar.activation(out=scaled[s][:, t, part], in_=d[:, t, :], func=ACT.Copy, scale=gains[:, 1, t : t + 1])
 
-        def products(s, part, e_dst, sq_dst, copy):
-            woven, apart = "p (c i t) -> p c t i", "p t (c i) -> p c t i"
-            e = scaled[s][:, :, part].rearrange(apart, i=LINE)
-            nc.vector.tensor_tensor(out=sq_dst.rearrange(woven, i=LINE, t=SLOTS), in0=e,
+        woven, apart = "p (c i t) -> p c t i", "p t (c i) -> p c t i"
+
+        def square_direct(s, part, dst):
+            nc.vector.tensor_tensor(out=dst.rearrange(woven, i=LINE, t=SLOTS), in0=scaled[s][:, :, part].rearrange(apart, i=LINE),
                                     in1=log_a[s][:, :, part].rearrange(apart, i=LINE), op=ALU.mult)
-            copy(out=e_dst.rearrange(woven, i=LINE, t=SLOTS), in_=e)
 
-        def quantise_group(s):
-            columns = 2 * GROUP + (PASS if s in riders else 0)
-            words, plane = quantise("both%d" % s, staged_values[s][:, 0 : SLOTS * columns], columns)
-            both_q[steps[s]] = words, plane
-            if s in riders:
-                return words[:, 2 * GROUP : columns], plane[:, 2 * GROUP : columns]
+        def round_direct(s, part, dst):
+            nc.vector.tensor_copy(out=dst.rearrange(woven, i=LINE, t=SLOTS), in_=scaled[s][:, :, part].rearrange(apart, i=LINE))
 
-        def passes(dst, rb, nt, quantised, first, width, half, start, stop):
-            words, plane = quantised
+        def passes(dst, rb, nt, e, sq, start, stop):
             cols = slice(nt * P, (nt + 1) * P)
             nc.tensor.matmul_mx(out=dst, lhsT=wr_q[rb][0][:, cols].bitcast(FP8X4), lhsT_scale=wr_q[rb][1][:, cols],
-                                rhs=words[:, first : first + width].bitcast(FP8X4), rhs_scale=plane[:, first : first + width],
-                                start=start, stop=False)
-            first = first + half
+                                rhs=e[0].bitcast(FP8X4), rhs_scale=e[1], start=start, stop=False)
             nc.tensor.matmul_mx(out=dst, lhsT=w8_w[:, rb, cols].bitcast(FP8X4),
                                 lhsT_scale=w8_sc[:, rb * N + nt * P : rb * N + (nt + 1) * P],
-                                rhs=words[:, first : first + width].bitcast(FP8X4), rhs_scale=plane[:, first : first + width],
-                                start=False, stop=stop)
+                                rhs=sq[0].bitcast(FP8X4), rhs_scale=sq[1], start=False, stop=stop)
+
+        score_banks = [6, 2, 4]
 
         def score_passes(rb, g):
             for pair in range(2):
                 if rb == 0:
-                    banks[g, pair] = psum.tile([P, 2, GROUP], F32, name="yx"[g % 2])
+                    banks[g, pair] = bank(score_banks[g] + pair, [P, 2, GROUP])
                 for u in range(2):
-                    passes(banks[g, pair][:, u, :], rb, 2 * pair + u, both_q[rb, g], 0, GROUP, GROUP,
+                    passes(banks[g, pair][:, u, :], rb, 2 * pair + u, made[rb, g][0], made[rb, g][1],
                            rb == 0 and u == 0, rb == 1 and u == 1)
 
         rows = out.rearrange("(nt p) j -> p nt j", p=P)
@@ -321,134 +288,122 @@ def tile_list_metabolite_annotation_scores_kernel(
                 nc.scalar.copy(out=staged[:], in_=banks[g, pair][:])
                 nc.sync.dma_start(out=rows[:, 2 * pair : 2 * pair + 2, g * GROUP : (g + 1) * GROUP], in_=staged[:])
 
-        def store_last(u):
-            j0 = S - GROUP + u * P
-            for i, bank in enumerate(banks["last", u]):
-                count = 4 // len(banks["last", u])
-                staged = kept("staged_last%d%d" % (u, i), [P, count, P], F32, None if u else homes[last])
-                (nc.scalar.copy if (u, i) == (1, 0) else nc.vector.tensor_copy)(out=staged[:], in_=bank[:, 0:count, :])
-                nc.sync.dma_start(out=rows[:, i * count : (i + 1) * count, j0 : j0 + P], in_=staged[:])
+        last_banks = [[6], [0, 1]]
 
-        def last_passes(rb, u):
+        def last_passes(rb, u, e, sq):
             count = 4 // (u + 1)
             if rb == 0:
-                banks["last", u] = [psum.tile([P, SLOTS, P], F32, name="diff", bufs=4) for i in range(u + 1)]
-                quantised, first, half = both_q[0, groups - 1], u * P, GROUP
-            else:
-                quantised = quantise("both_last%d" % u, both[last][:, u].rearrange("p s c -> p (s c)"), 2 * P)
-                first, half = 0, P
+                banks["last", u] = [bank(i, [P, count, P]) for i in last_banks[u]]
             for nt in range(4):
                 i, k = divmod(nt, count)
-                passes(banks["last", u][i][:, k, :], rb, nt, quantised, first, P, half,
-                       rb == 0 and k == 0, rb == 1 and k == count - 1)
+                passes(banks["last", u][i][:, k, :], rb, nt, e, sq, rb == 0 and k == 0, rb == 1 and k == count - 1)
 
-        last = len(steps) - 1
-        riders = (0, WR0, WR1)
-        homes = ["tab2_w", "tab_w0", "wa_raw00", "wa_raw10", "tab_w1", "wa_raw01", "log_b2", "log_b3"]
+        def store_last(u):
+            j0 = S - GROUP + u * P
+            count = 4 // (u + 1)
+            for i, sums in enumerate(banks["last", u]):
+                staged = kept("staged_last%d%d" % (u, i), [P, count, P], F32)
+                (nc.scalar.copy if i == 0 else nc.vector.tensor_copy)(out=staged[:], in_=sums[:])
+                nc.sync.dma_start(out=rows[:, i * count : (i + 1) * count, j0 : j0 + P], in_=staged[:])
 
-        def round_rider(s):
-            raw, order = wr_raw[0 if s == WR0 else 1], "p (c i j) -> p c j i"
-            dst = staged_values[s][:, SLOTS * 2 * GROUP :].rearrange(order, i=LINE, j=SLOTS)
-            src = raw[:].rearrange("p j (c i) -> p c j i", i=LINE)
-            for h in range(PIECES):
-                part = slice(h * P // PIECES, (h + 1) * P // PIECES)
-                nc.scalar.copy(out=dst[:, part], in_=src[:, part])
+        first_values = kept("first_values", [P, 2 * BLOCK], BF16)
+        def pool_round(raw, dst, part):
+            pool_copy(dst.rearrange("p (c j) -> p c j", j=SLOTS)[:, part], raw[:].rearrange("p j c -> p c j")[:, part])
 
-        staged_values = {}
+        def round_first(kp):
+            dst, src = weave(wa_raw[kp, 0], first_values[:, kp * BLOCK : (kp + 1) * BLOCK], natural, slice(0, P // 2))
+            nc.scalar.copy(out=dst, in_=src)
+            if kp == 0:
+                pool_round(wa_raw[0, 0], first_values[:, 0:BLOCK], slice(PASS // 2, PASS))
+            else:
+                dst, src = weave(wa_raw[1, 0], first_values[:, BLOCK:], natural, slice(P // 2, P))
+                nc.vector.tensor_copy(out=dst, in_=src)
 
-        def stage_values(s):
-            staged_values[s] = kept("values%d" % s, [P, SLOTS * (2 * GROUP + (PASS if s in riders else 0))], BF16, homes[s])
-            both[s] = staged_values[s][:, 0 : SLOTS * 2 * GROUP].rearrange("p (x y c) -> p x y c", x=2, y=2)
-
-        def negate_tile(s, u, buffer):
-            flat = "p t m -> p (t m)"
-            negated = kept("negated%d%d" % (s, u), [P, SLOTS, P], F32, buffer)
-            nc.gpsimd.tensor_scalar(out=negated[:].rearrange(flat), in0=log_b[s][:, u].rearrange(flat),
-                                    scalar1=-1.0, scalar2=0.0, op0=ALU.mult, op1=ALU.add)
-            minus[s, u] = negated[:]
-
-        for s in range(HEAD):
-            library_logs(s, "xy"[s % 2])
-            if s < EARLY:
-                negate(s, "stage1" if s == 1 else "log_b%d" % (s - 1) if s > 1 else None)
-        for s in range(EARLY, TURNED):
-            negate(s, NGATE)
-        v_w = [gather_words("v_w0", tab_w[0], list8, [2, groups]), gather_words("v_w1", tab_w[1], list8, [1, 2, groups])]
-        sample_logs(0, "xy"[HEAD % 2])
-        sample_logs(1, "yx"[HEAD % 2])
-        differences(0, [0])
-        wa_rounded = rounded(nc.vector.tensor_copy, wa_raw[0, 1], "stage2")
+        for s in range(2):
+            library_logs(s, 6 * s, kept("log_b%d" % s, [P, STEP], F32)[:])
+        round_first(0)
+        library_logs(2, 0, kept("log_b2", [P, STEP], F32)[:])
+        for s in range(2):
+            minus[s] = kept("minus%d" % s, [P, STEP], F32, None)[:]
+            pool_copy(minus[s], log_b[s], -1.0)
+        v_w = [kept("v_w%d" % kp, [P, S], U32) for kp in range(2)]
+        gather(v_w[0], tab_w[0], list8, [S])
+        round_first(1)
+        pair = quantise("wa_first", first_values[:], 2 * PASS)
+        for kp in range(2):
+            wa_q[kp, 0] = window(pair, kp * PASS, PASS)
+        late = kept("log_b34", [P, 2, STEP], F32, "wa_raw10")
+        library_logs(3, 0, late[:, 0])
+        library_logs(4, 0, late[:, 1])
+        held = kept("minus23", [P, 2, STEP], F32, "first_values")
+        for s in range(2, TURNED):
+            minus[s] = held[:, s - 2] if s < 4 else kept("minus4", [P, STEP], F32, "log_b2")[:]
+            pool_copy(minus[s], log_b[s], -1.0)
+        gather(v_w[1], tab_w[1], list8, [GROUP, 2 * GROUP, S])
+        for s in range(2):
+            for u in range(2):
+                turn(s, u, minus_tile(s, u), True, False)
+        for s in range(2):
+            sample_logs(s)
+            for u in range(2):
+                turn(s, u, log_a[s, u][:], False, True)
         scale(0, 0)
-        wa_q[0, 1] = quantise("wa01", wa_rounded[:], PASS)
-        stage_values(0)
-        rider = staged_values[0][:, SLOTS * 2 * GROUP :].rearrange("p (i h c j) -> p h c j i", i=LINE, h=2, j=SLOTS)
-        for h in range(2):
-            nc.scalar.copy(out=rider[:, h], in_=wa_halves[h][:].rearrange("p j (c i) -> p c j i", i=LINE))
-        sample_logs(2, "x", [0])
-        differences(0, [1])
-        differences(1, [0])
-        sample_logs(2, "x", [1])
-        differences(1, [1])
-        whole, flat = slice(0, GROUP), "p u c -> p (u c)"
-        for s in range(len(steps)):
-            if s + 2 <= last and s not in (0, 2):
-                if s == 1 and ALT:
-                    for u in range(2):
-                        differences(2, [u])
-                        sample_logs(3, "x", [u])
-                else:
-                    sample_logs(s + 2)
-            if 1 < s + 1 < TURNED and not (s == 1 and ALT):
-                differences(s + 1)
-            if s < last:
-                stage_values(s + 1)
-            if s < TURNED:
-                scale(s, 1)
-            elif s < last:
-                subtract(s + 1, whole if s + 1 < last else slice(0, P))
+        riders = {0: (wa_raw[0, 1], by_slot), 1: (wa_raw[1, 1], by_slot), 2: (wr_raw[0], natural), 4: (wr_raw[1], natural)}
+        whole, halves = slice(0, GROUP), [slice(0, P), slice(P, GROUP)]
+
+        def quantise_before(s):
+            carried = quantise_step(s - 1, s - 1 in riders)
+            if s - 1 < 2:
+                wa_q[s - 1, 1] = carried
+            elif carried:
+                wr_q[(s - 1) // 4] = carried
+
+        for s in range(TURNED):
+            if s in riders:
+                round_rider(s, *riders[s])
+            scale(s, 1)
+            if s:
+                quantise_before(s)
+            round_e(s)
+            sample_logs(s + 2)
+            if s + 3 >= TURNED:
+                library_logs(s + 3, 6, kept("log_b%d" % (s + 3), [P, STEP], F32, ["tab2_w", "tab_w0", "tab_w1"][s - 2])[:])
+            square(s, 0)
+            if s + 1 < TURNED:
+                scale(s + 1, 0)
             else:
-                subtract(last, slice(P, GROUP))
-            if s >= 1:
-                carried = quantise_group(s - 1)
-                if s == 1:
-                    wa_q[1, 1] = carried
-                    sample_logs(4)
-                if s in (WR0 + 1, WR1 + 1):
-                    wr_q[0 if s == WR0 + 1 else 1] = carried
-            if s == BAT:
-                for late in range(HEAD, last + 1):
-                    library_logs(late, "y", GATE[late - HEAD])
-            if s == 5:
+                subtract(s + 1, whole)
+            square(s, 1)
+            if s + 2 < TURNED:
+                differences(s + 2)
+            if s == TURNED - 1:
                 score_passes(0, 0)
-            if s >= 6:
-                score_passes(1, s - 6)
-                store_scores(s - 6)
-                score_passes(0, s - 5)
-            if s == last:
-                for u in range(2):
-                    last_passes(0, u)
-                score_passes(1, 2)
-            if s < TURNED:
-                square(s, 0)
-                if s + 1 < TURNED:
-                    scale(s + 1, 0)
-                elif s < last:
-                    subtract(s + 1, whole if s + 1 < last else slice(0, P))
-                else:
-                    last_passes(1, 0)
-                square(s, 1)
-            elif s < last:
-                products(s, whole, both[s][:, 0].rearrange(flat), both[s][:, 1].rearrange(flat),
-                         nc.scalar.copy if s in ON_SCALAR else nc.vector.tensor_copy)
-            else:
-                for u in range(2):
-                    products(last, slice(u * P, (u + 1) * P), both[last][:, u, 0], both[last][:, u, 1],
-                             nc.scalar.copy if u < LAST_S else nc.vector.tensor_copy)
-                    if u == 0:
-                        last_passes(1, 0)
-            if s + 1 in (WR0, WR1):
-                round_rider(s + 1)
-        last_passes(1, 1)
+        for s in range(TURNED, last):
+            subtract(s + 1, whole if s + 1 < last else halves[0])
+            quantise_before(s)
+            if s == TURNED:
+                sample_logs(last)
+                score_passes(0, 1)
+            score_passes(1, s - TURNED)
+            store_scores(s - TURNED)
+            square_direct(s, whole, sq_values(s))
+            round_direct(s, whole, e_values)
+            if s == TURNED:
+                score_passes(0, 2)
+        subtract(last, halves[1])
+        quantise_before(last)
+        for u in range(2):
+            last_passes(0, u, window(made[0, 3][0], u * P, P), window(made[0, 3][1], u * P, P))
+        score_passes(1, 2)
+        last_values = kept("last_values", [P, 2, 2, PASS], BF16)
+        square_direct(last, halves[0], last_values[:, 0, 1])
+        round_direct(last, halves[0], last_values[:, 0, 0])
+        square_direct(last, halves[1], last_values[:, 1, 1])
+        for u in range(2):
+            if u:
+                round_direct(last, halves[1], last_values[:, 1, 0])
+            pair = quantise("last%d" % u, last_values[:, u].rearrange("p s c -> p (s c)"), 2 * P)
+            last_passes(1, u, window(pair, 0, P), window(pair, P, P))
         store_scores(2)
         for u in range(2):
             store_last(u)

@@ -112,7 +112,7 @@ def tile_list_metabolite_annotation_scores_kernel(
         v2_sc = kept("v2_sc", [P, S], U8)
         gather(v2_sc, tab2_sc, list1, [S])
         v2_w = kept("v2_w", [P, S], U32)
-        gather(v2_w, tab2_w, list1, [GROUP, 2 * GROUP, S])
+        gather(v2_w, tab2_w, list1, [GROUP, S])
         w4_slot_w = kept("w4_slot_w", [P, 2 * PASS], U8)
         nc.gpsimd.tensor_copy(out=w4_slot_w[:].rearrange("p (t m b) -> p t m b", t=SLOTS, b=2),
                               in_=w4_w[:, 2 * PASS : 4 * PASS].rearrange("p (m t b) -> p t m b", t=SLOTS, b=2))
@@ -198,9 +198,10 @@ def tile_list_metabolite_annotation_scores_kernel(
 
         def differences(s, tiles=(0, 1)):
             for u in tiles:
-                turn(s, u, log_a[s, u][:], True, False)
-                turn(s, u, minus_tile(s, u), False, True)
+                turn(s, u, minus_tile(s, u), True, False)
+                turn(s, u, log_a[s, u][:], False, True)
 
+        direct_values = {}
         values = kept("values", [P, 2 * BLOCK + 3 * STEP], BF16)
         e_values = values[:, BLOCK + STEP : BLOCK + 2 * STEP]
 
@@ -222,6 +223,10 @@ def tile_list_metabolite_annotation_scores_kernel(
             nc.scalar.copy(out=dst, in_=src)
 
         def quantise_step(s, rider=False):
+            if s >= TURNED:
+                pair = quantise("step%d" % s, direct_values[s][:].rearrange("p x c -> p (x c)"), 2 * GROUP)
+                made[steps[s]] = window(pair, 0, GROUP), window(pair, GROUP, GROUP)
+                return None
             extra = BLOCK if rider else 0
             if s % 2:
                 first, places = BLOCK + STEP, (0, GROUP, 2 * GROUP)
@@ -252,6 +257,9 @@ def tile_list_metabolite_annotation_scores_kernel(
                 scaled[s] = work.tile([P, SLOTS, GROUP], F32, name="scaled")
             for t in range(SLOTS):
                 nc.scalar.activation(out=scaled[s][:, t, part], in_=d[:, t, :], func=ACT.Copy, scale=gains[:, 1, t : t + 1])
+            if s < last:
+                direct_values[s] = kept("direct_values%d" % s, [P, 2, STEP], BF16, "wa_raw%d1" % (s - TURNED))
+                round_direct(s, part, direct_values[s][:, 0], nc.scalar.copy)
 
         woven, apart = "p (c i t) -> p c t i", "p t (c i) -> p c t i"
 
@@ -259,8 +267,8 @@ def tile_list_metabolite_annotation_scores_kernel(
             nc.vector.tensor_tensor(out=dst.rearrange(woven, i=LINE, t=SLOTS), in0=scaled[s][:, :, part].rearrange(apart, i=LINE),
                                     in1=log_a[s][:, :, part].rearrange(apart, i=LINE), op=ALU.mult)
 
-        def round_direct(s, part, dst):
-            nc.vector.tensor_copy(out=dst.rearrange(woven, i=LINE, t=SLOTS), in_=scaled[s][:, :, part].rearrange(apart, i=LINE))
+        def round_direct(s, part, dst, copy=nc.vector.tensor_copy):
+            copy(out=dst.rearrange(woven, i=LINE, t=SLOTS), in_=scaled[s][:, :, part].rearrange(apart, i=LINE))
 
         def passes(dst, rb, nt, e, sq, start, stop):
             cols = slice(nt * P, (nt + 1) * P)
@@ -282,9 +290,9 @@ def tile_list_metabolite_annotation_scores_kernel(
 
         rows = out.rearrange("(nt p) j -> p nt j", p=P)
 
-        def store_scores(g):
-            for pair in range(2):
-                staged = work.tile([P, 2, GROUP], F32, name="staged%d" % pair)
+        def store_scores(g, pairs=(0, 1)):
+            for pair in pairs:
+                staged = kept("staged%d%d" % (g, pair), [P, 2, GROUP], F32, {(0, 0): "tab_w0", (1, 1): "tab_w1"}.get((g, pair)))
                 nc.scalar.copy(out=staged[:], in_=banks[g, pair][:])
                 nc.sync.dma_start(out=rows[:, 2 * pair : 2 * pair + 2, g * GROUP : (g + 1) * GROUP], in_=staged[:])
 
@@ -311,12 +319,12 @@ def tile_list_metabolite_annotation_scores_kernel(
             pool_copy(dst.rearrange("p (c j) -> p c j", j=SLOTS)[:, part], raw[:].rearrange("p j c -> p c j")[:, part])
 
         def round_first(kp):
-            dst, src = weave(wa_raw[kp, 0], first_values[:, kp * BLOCK : (kp + 1) * BLOCK], natural, slice(0, P // 2))
-            nc.scalar.copy(out=dst, in_=src)
             if kp == 0:
+                dst, src = weave(wa_raw[0, 0], first_values[:, 0:BLOCK], natural, slice(0, P // 2))
+                nc.scalar.copy(out=dst, in_=src)
                 pool_round(wa_raw[0, 0], first_values[:, 0:BLOCK], slice(PASS // 2, PASS))
             else:
-                dst, src = weave(wa_raw[1, 0], first_values[:, BLOCK:], natural, slice(P // 2, P))
+                dst, src = weave(wa_raw[1, 0], first_values[:, BLOCK:], natural)
                 nc.vector.tensor_copy(out=dst, in_=src)
 
         for s in range(2):
@@ -332,9 +340,8 @@ def tile_list_metabolite_annotation_scores_kernel(
         pair = quantise("wa_first", first_values[:], 2 * PASS)
         for kp in range(2):
             wa_q[kp, 0] = window(pair, kp * PASS, PASS)
-        late = kept("log_b34", [P, 2, STEP], F32, "wa_raw10")
-        library_logs(3, 0, late[:, 0])
-        library_logs(4, 0, late[:, 1])
+        for s in range(3, 6):
+            library_logs(s, 6 * (s % 2), kept("log_b%d" % s, [P, STEP], F32, "tab2_w" if s == 5 else None)[:])
         held = kept("minus23", [P, 2, STEP], F32, "first_values")
         for s in range(2, TURNED):
             minus[s] = held[:, s - 2] if s < 4 else kept("minus4", [P, STEP], F32, "log_b2")[:]
@@ -358,39 +365,43 @@ def tile_list_metabolite_annotation_scores_kernel(
             elif carried:
                 wr_q[(s - 1) // 4] = carried
 
-        for s in range(TURNED):
+        for s in range(last):
             if s in riders:
                 round_rider(s, *riders[s])
-            scale(s, 1)
+            if s < TURNED:
+                scale(s, 1)
+            else:
+                subtract(s + 1, whole if s + 1 < last else halves[0])
             if s:
                 quantise_before(s)
-            round_e(s)
-            sample_logs(s + 2)
-            if s + 3 >= TURNED:
+            if s < TURNED:
+                round_e(s)
+            if s + 2 <= last:
+                sample_logs(s + 2)
+            if 3 <= s <= 4:
                 library_logs(s + 3, 6, kept("log_b%d" % (s + 3), [P, STEP], F32, ["tab2_w", "tab_w0", "tab_w1"][s - 2])[:])
-            square(s, 0)
-            if s + 1 < TURNED:
-                scale(s + 1, 0)
-            else:
-                subtract(s + 1, whole)
-            square(s, 1)
-            if s + 2 < TURNED:
-                differences(s + 2)
-            if s == TURNED - 1:
-                score_passes(0, 0)
-        for s in range(TURNED, last):
-            subtract(s + 1, whole if s + 1 < last else halves[0])
-            quantise_before(s)
-            if s == TURNED:
-                sample_logs(last)
+            if s == GROUPS + 1:
                 score_passes(0, 1)
-            score_passes(1, s - TURNED)
-            store_scores(s - TURNED)
-            square_direct(s, whole, sq_values(s))
-            round_direct(s, whole, e_values)
-            if s == TURNED:
+            if s > GROUPS:
+                score_passes(1, s - GROUPS - 1)
+                store_scores(s - GROUPS - 1, (0, 1) if s == GROUPS + 1 else (0,))
+            if s < TURNED:
+                square(s, 0)
+                if s + 1 < TURNED:
+                    scale(s + 1, 0)
+                else:
+                    subtract(s + 1, whole)
+                square(s, 1)
+                if s + 2 < TURNED:
+                    differences(s + 2)
+            else:
+                square_direct(s, whole, direct_values[s][:, 1])
+            if s == GROUPS:
+                score_passes(0, 0)
+            if s == GROUPS + 1:
                 score_passes(0, 2)
         subtract(last, halves[1])
+        store_scores(1, (1,))
         quantise_before(last)
         for u in range(2):
             last_passes(0, u, window(made[0, 3][0], u * P, P), window(made[0, 3][1], u * P, P))

@@ -324,8 +324,9 @@ def tile_list_metabolite_annotation_scores_kernel(
                 nc.scalar.copy(out=dst, in_=src)
                 pool_round(wa_raw[0, 0], first_values[:, 0:BLOCK], slice(PASS // 2, PASS))
             else:
-                dst, src = weave(wa_raw[1, 0], first_values[:, BLOCK:], natural)
-                nc.vector.tensor_copy(out=dst, in_=src)
+                for h, copy in enumerate((nc.scalar.copy, nc.vector.tensor_copy)):
+                    dst, src = weave(wa_raw[1, 0], first_values[:, BLOCK:], natural, slice(h * P // 2, (h + 1) * P // 2))
+                    copy(out=dst, in_=src)
 
         for s in range(2):
             library_logs(s, 6 * s, kept("log_b%d" % s, [P, STEP], F32)[:])
@@ -340,8 +341,10 @@ def tile_list_metabolite_annotation_scores_kernel(
         pair = quantise("wa_first", first_values[:], 2 * PASS)
         for kp in range(2):
             wa_q[kp, 0] = window(pair, kp * PASS, PASS)
-        for s in range(3, 6):
-            library_logs(s, 6 * (s % 2), kept("log_b%d" % s, [P, STEP], F32, "tab2_w" if s == 5 else None)[:])
+        library_logs(3, 6, kept("log_b3", [P, STEP], F32)[:])
+        late = kept("log_b45", [P, 2, STEP], F32, "wa_raw10")
+        library_logs(4, 6, late[:, 0])
+        library_logs(5, 0, late[:, 1])
         held = kept("minus23", [P, 2, STEP], F32, "first_values")
         for s in range(2, TURNED):
             minus[s] = held[:, s - 2] if s < 4 else kept("minus4", [P, STEP], F32, "log_b2")[:]

@@ -24,9 +24,11 @@ QUADRANT = 32
 GROUP = 256
 GROUPS = S // GROUP
 LINE = 4
-TURNED = 5
 STEP = SLOTS * GROUP
 BLOCK = SLOTS * PASS
+STEPS = [(rb, g) for rb in range(2) for g in range(GROUPS)]
+TURNED = 6
+SHARES = {0: 64, 1: 32, 3: 32, 4: 0}
 
 
 def tile_list_metabolite_annotation_scores_kernel(
@@ -59,13 +61,14 @@ def tile_list_metabolite_annotation_scores_kernel(
         v_sc = kept("v_sc", [P, 2 * S], U8)
         for plane in (tab2_sc, w4_sc, tab_sc, w8_sc, v_sc):
             nc.vector.memset(as_words(plane[:]), 0)
-        make_identity(nc, identity[:])
-        gains = kept("gains", [P, 2, SLOTS], F32)
-        nc.gpsimd.dma_start(out=gains[:], in_=gain.rearrange("(b p t) -> p b t", b=2, t=SLOTS))
 
         def load_plane(plane, rows):
             for r in range(4):
                 nc.sync.dma_start(out=plane[r:P:QUADRANT], in_=rows(slice(r, 16, 4)))
+
+        gains = kept("gains", [P, 2, SLOTS], F32)
+        nc.gpsimd.dma_start(out=gains[:], in_=gain.rearrange("(b p t) -> p b t", b=2, t=SLOTS))
+        make_identity(nc, identity[:])
 
         def load_table(name, words):
             tile = kept(name, [P, T], U32)
@@ -80,9 +83,8 @@ def tile_list_metabolite_annotation_scores_kernel(
         def load_wa(kp, rb):
             return load_rows("wa_raw%d%d" % (kp, rb), wa[kp * PASS : (kp + 1) * PASS, rb * PASS : (rb + 1) * PASS])
 
-        def gather(tile, table, offsets, cuts):
-            for first, end in zip([0] + cuts, cuts):
-                nc.vector.tensor_copy(tile[:, first:end], table[:].indirect(offsets[:, first // 16 : end // 16]))
+        def gather(tile, table, offsets, first, end):
+            nc.vector.tensor_copy(tile[:, first:end], table[:].indirect(offsets[:, first // 16 : end // 16]))
 
         def pool_copy(out, in_, factor=1.0):
             nc.gpsimd.tensor_scalar(out=out, in0=in_, scalar1=factor, scalar2=0.0, op0=ALU.mult, op1=ALU.add)
@@ -103,26 +105,26 @@ def tile_list_metabolite_annotation_scores_kernel(
         tab2_w = load_table("tab2_w", tab2_words[0])
         nc.sync.dma_start(out=as_words(w4_w[:]), in_=as_words(w4_words[0]))
         load_plane(as_words(w4_sc[:]), lambda q: as_words(w4_scales[0])[q, :])
-        wa_raw[0, 0] = load_wa(0, 0)
         nc.sync.dma_start(out=as_words(tab_sc[:])[0:P:4, :], in_=as_words(tab_scales).rearrange("a q c -> q a c"))
-        tab_w = [load_table("tab_w0", tab_words[0])]
-        wa_raw[1, 0] = load_wa(1, 0)
-        tab_w.append(load_table("tab_w1", tab_words[1]))
+        for kp in range(2):
+            wa_raw[kp, 0] = load_wa(kp, 0)
+        tab_w = [load_table("tab_w%d" % kp, tab_words[kp]) for kp in range(2)]
 
         v2_sc = kept("v2_sc", [P, S], U8)
-        gather(v2_sc, tab2_sc, list1, [S])
         v2_w = kept("v2_w", [P, S], U32)
-        gather(v2_w, tab2_w, list1, [GROUP, S])
+        picked_sc = kept("picked_sc", [P, S], U8)
+        gather(v2_sc, tab2_sc, list1, 0, S)
+        gather(v2_w, tab2_w, list1, 0, GROUP)
+        gather(v2_w, tab2_w, list1, GROUP, S)
+        gather(picked_sc, tab_sc, list8, 0, S)
         w4_slot_w = kept("w4_slot_w", [P, 2 * PASS], U8)
         nc.gpsimd.tensor_copy(out=w4_slot_w[:].rearrange("p (t m b) -> p t m b", t=SLOTS, b=2),
                               in_=w4_w[:, 2 * PASS : 4 * PASS].rearrange("p (m t b) -> p t m b", t=SLOTS, b=2))
-        picked_sc = kept("picked_sc", [P, S], U8)
-        gather(picked_sc, tab_sc, list8, [S])
-        for d in range(0, P, QUADRANT):
-            nc.sync.dma_start(out=as_words(v_sc[:])[d : d + 4, :], in_=as_words(picked_sc[:])[d : d + QUADRANT : 4, :])
         w4_slot_sc = kept("w4_slot_sc", [P, PASS], U8)
         nc.gpsimd.tensor_copy(out=w4_slot_sc[:].rearrange("p (t m) -> p t m", t=SLOTS),
                               in_=w4_sc[:, PASS : 2 * PASS].rearrange("p (m t) -> p t m", t=SLOTS))
+        for d in range(0, P, QUADRANT):
+            nc.sync.dma_start(out=as_words(v_sc[:])[d : d + 4, :], in_=as_words(picked_sc[:])[d : d + QUADRANT : 4, :])
         wa_raw[0, 1] = load_wa(0, 1)
         wa_raw[1, 1] = load_wa(1, 1)
         wr_raw = [load_rows("wr_raw%d" % rb, wr[rb * PASS : (rb + 1) * PASS, :]) for rb in range(2)]
@@ -131,12 +133,12 @@ def tile_list_metabolite_annotation_scores_kernel(
         w8_w = kept("w8_w", [P, 2, N], U32)
         nc.sync.dma_start(out=as_words(w8_w[:]), in_=as_words(w8_words.rearrange("b p n i -> p b (n i)")))
 
-        steps = [(rb, g) for rb in range(2) for g in range(GROUPS)]
-        last = len(steps) - 1
-        log_b, log_a, minus, diff, scaled, made, banks, wa_q, wr_q = {}, {}, {}, {}, {}, {}, {}, {}, {}
+        last = len(STEPS) - 1
+        log_b, log_a, minus, diff, made, banks, wa_q, wr_q = {}, {}, {}, {}, {}, {}, {}, {}
 
-        def library_logs(s, first_bank, logs):
-            rb, g = steps[s]
+        def library_logs(s, first_bank):
+            rb, g = STEPS[s]
+            logs = kept("log_b%d" % s, [P, STEP], F32)
             log_b[s] = logs
             for u in range(2):
                 if s < TURNED:
@@ -158,24 +160,33 @@ def tile_list_metabolite_annotation_scores_kernel(
                     nc.scalar.activation(out=logs[:, u * PASS : (u + 1) * PASS], in_=sums[:].rearrange("p i c -> p (i c)"),
                                          func=ACT.Ln, bias=1.0)
 
-        def sample_logs(s, tiles=(0, 1)):
-            rb, g = steps[s]
-            for u in tiles:
+        def negate(s, dst):
+            for u in range(2):
+                minus[s, u] = dst[:, u * PASS : (u + 1) * PASS]
+            pool_copy(dst, log_b[s][:], -1.0)
+
+        def negate_tile(s, u, dst):
+            minus[s, u] = dst
+            pool_copy(dst, log_b[s][:, u * PASS : (u + 1) * PASS], -1.0)
+
+        def sample_logs(s, first_bank):
+            rb, g = STEPS[s]
+            for u in range(2):
                 if s < TURNED:
                     j0 = g * GROUP + u * P
-                    sums = bank(u + 6 * (1 - s % 2), [P, PASS])
-                    for kp in range(2):
+                    sums = bank(first_bank + u, [P, PASS])
+                    for kp in (1, 0):
                         words, plane = wa_q[kp, rb]
                         nc.tensor.matmul_mx(out=sums[:], lhsT=v_w[kp][:, j0 : j0 + P].bitcast(FP8X4),
                                             lhsT_scale=v_sc[:, kp * S + j0 : kp * S + j0 + P], rhs=words.bitcast(FP8X4),
-                                            rhs_scale=plane, start=(kp == 0), stop=(kp == 1))
-                    log_a[s, u] = work.tile([P, SLOTS, P], F32, name="log_a", bufs=4)
+                                            rhs_scale=plane, start=(kp == 1), stop=(kp == 0))
+                    log_a[s, u] = work.tile([P, SLOTS, P], F32, name="log_a", bufs=6)
                     order = "p (t m) -> p t m" if rb else "p (m t) -> p t m"
                     nc.scalar.activation(out=log_a[s, u][:], in_=sums[:].rearrange(order, t=SLOTS), func=ACT.Ln, bias=1.0)
                 else:
                     if u == 0:
-                        log_a[s] = work.tile([P, SLOTS, GROUP], F32, name="log_a_direct", bufs=3)
-                    sums = bank(u + 4 * (1 - s % 2), [P, 2, GROUP])
+                        log_a[s] = work.tile([P, SLOTS, GROUP], F32, name="log_a_direct")
+                    sums = bank(first_bank + u, [P, 2, GROUP])
                     entries = slice(g * GROUP, (g + 1) * GROUP)
                     for i in range(2):
                         cols = slice((2 * u + i) * P, (2 * u + i + 1) * P)
@@ -193,17 +204,11 @@ def tile_list_metabolite_annotation_scores_kernel(
                 nc.tensor.matmul(out=diff[s, u][:, t, :], lhsT=term[:, t, :], rhs=identity[:], is_transpose=True,
                                  start=(start and t == 0), stop=(stop and t == SLOTS - 1))
 
-        def minus_tile(s, u):
-            return minus[s][:, u * PASS : (u + 1) * PASS].rearrange("p (t m) -> p t m", t=SLOTS)
+        def turn_library(s, u):
+            turn(s, u, by_slots(minus[s, u]), True, False)
 
-        def differences(s, tiles=(0, 1)):
-            for u in tiles:
-                turn(s, u, minus_tile(s, u), True, False)
-                turn(s, u, log_a[s, u][:], False, True)
-
-        direct_values = {}
-        values = kept("values", [P, 2 * BLOCK + 3 * STEP], BF16)
-        e_values = values[:, BLOCK + STEP : BLOCK + 2 * STEP]
+        def turn_sample(s, u):
+            turn(s, u, log_a[s, u][:], False, True)
 
         def sq_values(s):
             first = BLOCK + 2 * STEP * (s % 2)
@@ -213,62 +218,57 @@ def tile_list_metabolite_annotation_scores_kernel(
             first = (BLOCK + 3 * STEP) * (s % 2)
             return values[:, first : first + BLOCK]
 
-        def weave(raw, dst, order, part=slice(0, P)):
-            return (dst.rearrange(order, i=LINE, j=SLOTS)[:, part], raw[:].rearrange("p j (c i) -> p c j i", i=LINE)[:, part])
-
         natural, by_slot = "p (c i j) -> p c j i", "p (i c j) -> p c j i"
 
-        def round_rider(s, raw, order):
-            dst, src = weave(raw, rider_values(s), order)
-            nc.scalar.copy(out=dst, in_=src)
+        def round_rows(copy, raw, dst, order, part):
+            copy(out=dst.rearrange(order, i=LINE, j=SLOTS)[:, part], in_=raw[:].rearrange("p j (c i) -> p c j i", i=LINE)[:, part])
 
-        def quantise_step(s, rider=False):
-            if s >= TURNED:
-                pair = quantise("step%d" % s, direct_values[s][:].rearrange("p x c -> p (x c)"), 2 * GROUP)
-                made[steps[s]] = window(pair, 0, GROUP), window(pair, GROUP, GROUP)
-                return None
+        def quantise_step(s, rider):
             extra = BLOCK if rider else 0
             if s % 2:
                 first, places = BLOCK + STEP, (0, GROUP, 2 * GROUP)
             else:
                 first, places = BLOCK - extra, (extra // SLOTS + GROUP, extra // SLOTS, 0)
             pair = quantise("step%d" % s, values[:, first : first + 2 * STEP + extra], (2 * STEP + extra) // SLOTS)
-            made[steps[s]] = window(pair, places[0], GROUP), window(pair, places[1], GROUP)
+            made[STEPS[s]] = window(pair, places[0], GROUP), window(pair, places[1], GROUP)
             return window(pair, places[2], PASS) if rider else None
-
-        def scale(s, u):
-            rb = steps[s][0]
-            if u == 0:
-                scaled[s] = work.tile([P, 2, P, SLOTS], F32, name="scaled")
-            nc.vector.tensor_tensor(out=scaled[s][:, u], in0=diff[s, u][:].rearrange("p t j -> p j t"),
-                                    in1=gains[:, rb : rb + 1, :].to_broadcast([P, P, SLOTS]), op=ALU.mult)
-
-        def round_e(s):
-            pool_copy(e_values, scaled[s][:].rearrange("p u j t -> p (u j t)"))
-
-        def square(s, u):
-            nc.vector.tensor_tensor(out=sq_values(s)[:, u * PASS : (u + 1) * PASS].rearrange("p (j t) -> p j t", t=SLOTS),
-                                    in0=diff[s, u][:].rearrange("p t j -> p j t"), in1=scaled[s][:, u], op=ALU.mult)
-
-        def subtract(s, part):
-            d = log_a[s][:, :, part]
-            nc.vector.tensor_tensor(out=d, in0=d, in1=log_b[s].rearrange("p (t c) -> p t c", t=SLOTS)[:, :, part], op=ALU.subtract)
-            if part.start == 0:
-                scaled[s] = work.tile([P, SLOTS, GROUP], F32, name="scaled")
-            for t in range(SLOTS):
-                nc.scalar.activation(out=scaled[s][:, t, part], in_=d[:, t, :], func=ACT.Copy, scale=gains[:, 1, t : t + 1])
-            if s < last:
-                direct_values[s] = kept("direct_values%d" % s, [P, 2, STEP], BF16, "wa_raw%d1" % (s - TURNED))
-                round_direct(s, part, direct_values[s][:, 0], nc.scalar.copy)
 
         woven, apart = "p (c i t) -> p c t i", "p t (c i) -> p c t i"
 
+        scaled_all = kept("scaled_all", [P, 4 * STEP], F32)
+
+        def scaled(s):
+            return scaled_all[:, s % 4 * STEP : (s % 4 + 1) * STEP]
+
+        def scale(s, u):
+            rb = STEPS[s][0]
+            nc.vector.tensor_tensor(out=scaled(s)[:, u * PASS : (u + 1) * PASS].rearrange("p (j t) -> p j t", t=SLOTS),
+                                    in0=diff[s, u][:].rearrange("p t j -> p j t"),
+                                    in1=gains[:, rb : rb + 1, :].to_broadcast([P, P, SLOTS]), op=ALU.mult)
+
+        def round_e(s, part=slice(0, STEP)):
+            pool_copy(e_values[:, part], scaled(s)[:, part])
+
+        def square(s, u):
+            tile = slice(u * PASS, (u + 1) * PASS)
+            nc.vector.tensor_tensor(out=sq_values(s)[:, tile].rearrange("p (j t) -> p j t", t=SLOTS), in0=diff[s, u][:].rearrange("p t j -> p j t"),
+                                    in1=scaled(s)[:, tile].rearrange("p (j t) -> p j t", t=SLOTS), op=ALU.mult)
+
+        def by_slots(ap):
+            return ap.rearrange("p (t c) -> p t c", t=SLOTS)
+
+        def subtract(s, part):
+            d = log_a[s][:, :, part]
+            nc.vector.tensor_tensor(out=d, in0=d, in1=by_slots(log_b[s][:])[:, :, part], op=ALU.subtract)
+            for t in range(SLOTS):
+                nc.scalar.activation(out=by_slots(scaled(s))[:, t, part], in_=d[:, t, :], func=ACT.Copy, scale=gains[:, 1, t : t + 1])
+
         def square_direct(s, part, dst):
-            nc.vector.tensor_tensor(out=dst.rearrange(woven, i=LINE, t=SLOTS), in0=scaled[s][:, :, part].rearrange(apart, i=LINE),
+            nc.vector.tensor_tensor(out=dst.rearrange(woven, i=LINE, t=SLOTS), in0=by_slots(scaled(s))[:, :, part].rearrange(apart, i=LINE),
                                     in1=log_a[s][:, :, part].rearrange(apart, i=LINE), op=ALU.mult)
 
         def round_direct(s, part, dst, copy=nc.vector.tensor_copy):
-            copy(out=dst.rearrange(woven, i=LINE, t=SLOTS), in_=scaled[s][:, :, part].rearrange(apart, i=LINE))
+            copy(out=dst.rearrange(woven, i=LINE, t=SLOTS), in_=by_slots(scaled(s))[:, :, part].rearrange(apart, i=LINE))
 
         def passes(dst, rb, nt, e, sq, start, stop):
             cols = slice(nt * P, (nt + 1) * P)
@@ -278,25 +278,25 @@ def tile_list_metabolite_annotation_scores_kernel(
                                 lhsT_scale=w8_sc[:, rb * N + nt * P : rb * N + (nt + 1) * P],
                                 rhs=sq[0].bitcast(FP8X4), rhs_scale=sq[1], start=False, stop=stop)
 
-        score_banks = [6, 2, 4]
-
-        def score_passes(rb, g):
+        def score_passes(rb, g, first_bank=None):
             for pair in range(2):
                 if rb == 0:
-                    banks[g, pair] = bank(score_banks[g] + pair, [P, 2, GROUP])
+                    banks[g, pair] = bank(first_bank + pair, [P, 2, GROUP])
                 for u in range(2):
                     passes(banks[g, pair][:, u, :], rb, 2 * pair + u, made[rb, g][0], made[rb, g][1],
                            rb == 0 and u == 0, rb == 1 and u == 1)
 
         rows = out.rearrange("(nt p) j -> p nt j", p=P)
 
-        def store_scores(g, pairs=(0, 1)):
-            for pair in pairs:
-                staged = kept("staged%d%d" % (g, pair), [P, 2, GROUP], F32, {(0, 0): "tab_w0", (1, 1): "tab_w1"}.get((g, pair)))
+        spent = ["tab2_w", "tab_w0", "wa_raw11", "wa_raw00", "wa_raw10", "wr_raw0"]
+
+        def store_scores(g):
+            for pair in range(2):
+                staged = kept("staged%d%d" % (g, pair), [P, 2, GROUP], F32, spent[2 * g + pair])
                 nc.scalar.copy(out=staged[:], in_=banks[g, pair][:])
                 nc.sync.dma_start(out=rows[:, 2 * pair : 2 * pair + 2, g * GROUP : (g + 1) * GROUP], in_=staged[:])
 
-        last_banks = [[6], [0, 1]]
+        last_banks = [[6], [2, 3]]
 
         def last_passes(rb, u, e, sq):
             count = 4 // (u + 1)
@@ -315,102 +315,101 @@ def tile_list_metabolite_annotation_scores_kernel(
                 nc.sync.dma_start(out=rows[:, i * count : (i + 1) * count, j0 : j0 + P], in_=staged[:])
 
         first_values = kept("first_values", [P, 2 * BLOCK], BF16)
-        def pool_round(raw, dst, part):
-            pool_copy(dst.rearrange("p (c j) -> p c j", j=SLOTS)[:, part], raw[:].rearrange("p j c -> p c j")[:, part])
-
-        def round_first(kp):
-            if kp == 0:
-                dst, src = weave(wa_raw[0, 0], first_values[:, 0:BLOCK], natural, slice(0, P // 2))
-                nc.scalar.copy(out=dst, in_=src)
-                pool_round(wa_raw[0, 0], first_values[:, 0:BLOCK], slice(PASS // 2, PASS))
-            else:
-                for h, copy in enumerate((nc.scalar.copy, nc.vector.tensor_copy)):
-                    dst, src = weave(wa_raw[1, 0], first_values[:, BLOCK:], natural, slice(h * P // 2, (h + 1) * P // 2))
-                    copy(out=dst, in_=src)
-
-        for s in range(2):
-            library_logs(s, 6 * s, kept("log_b%d" % s, [P, STEP], F32)[:])
-        round_first(0)
-        library_logs(2, 0, kept("log_b2", [P, STEP], F32)[:])
-        for s in range(2):
-            minus[s] = kept("minus%d" % s, [P, STEP], F32, None)[:]
-            pool_copy(minus[s], log_b[s], -1.0)
-        v_w = [kept("v_w%d" % kp, [P, S], U32) for kp in range(2)]
-        gather(v_w[0], tab_w[0], list8, [S])
-        round_first(1)
+        library_logs(0, 0)
+        round_rows(nc.scalar.copy, wa_raw[0, 0], first_values[:, 0:BLOCK], natural, slice(0, P))
+        negate(0, log_b[0][:])
+        round_rows(nc.vector.tensor_copy, wa_raw[1, 0], first_values[:, BLOCK:], natural, slice(0, P))
         pair = quantise("wa_first", first_values[:], 2 * PASS)
         for kp in range(2):
             wa_q[kp, 0] = window(pair, kp * PASS, PASS)
-        library_logs(3, 6, kept("log_b3", [P, STEP], F32)[:])
-        late = kept("log_b45", [P, 2, STEP], F32, "wa_raw10")
-        library_logs(4, 6, late[:, 0])
-        library_logs(5, 0, late[:, 1])
-        held = kept("minus23", [P, 2, STEP], F32, "first_values")
-        for s in range(2, TURNED):
-            minus[s] = held[:, s - 2] if s < 4 else kept("minus4", [P, STEP], F32, "log_b2")[:]
-            pool_copy(minus[s], log_b[s], -1.0)
-        gather(v_w[1], tab_w[1], list8, [GROUP, 2 * GROUP, S])
-        for s in range(2):
-            for u in range(2):
-                turn(s, u, minus_tile(s, u), True, False)
-        for s in range(2):
-            sample_logs(s)
-            for u in range(2):
-                turn(s, u, log_a[s, u][:], False, True)
-        scale(0, 0)
-        riders = {0: (wa_raw[0, 1], by_slot), 1: (wa_raw[1, 1], by_slot), 2: (wr_raw[0], natural), 4: (wr_raw[1], natural)}
+        for s in range(1, TURNED):
+            library_logs(s, 6 * (s % 2))
+        negate(1, kept("held", [P, STEP], F32, "first_values")[:])
+        for s in range(2, 4):
+            negate(s, log_b[s - 1][:])
+        v_w = [kept("v_w%d" % kp, [P, S], U32) for kp in range(2)]
+        for kp, first, end in ((0, 0, GROUP), (1, 0, GROUP), (0, GROUP, 2 * GROUP), (1, GROUP, 2 * GROUP), (0, 2 * GROUP, 3 * GROUP),
+                               (1, 2 * GROUP, S), (0, 3 * GROUP, S)):
+            gather(v_w[kp], tab_w[kp], list8, first, end)
+        values = kept("values", [P, 2 * BLOCK + 3 * STEP], BF16, "tab_w1")
+        e_values = values[:, BLOCK + STEP : BLOCK + 2 * STEP]
+        riders = {0: (wa_raw[0, 1], by_slot), 1: (wa_raw[1, 1], by_slot), 3: (wr_raw[0], natural), 4: (wr_raw[1], natural)}
         whole, halves = slice(0, GROUP), [slice(0, P), slice(P, GROUP)]
+
+        def differences(s):
+            for u in range(2):
+                turn_library(s, u)
+            sample_logs(s, 6 * (s % 2))
+            for u in range(2):
+                turn_sample(s, u)
+
+        def round_rider(s):
+            share = SHARES[s]
+            if share:
+                round_rows(nc.vector.tensor_copy, riders[s][0], rider_values(s), riders[s][1], slice(0, share))
+            middle = (share + P) // 2
+            for part in (slice(share, middle), slice(middle, P)):
+                round_rows(nc.scalar.copy, riders[s][0], rider_values(s), riders[s][1], part)
 
         def quantise_before(s):
             carried = quantise_step(s - 1, s - 1 in riders)
             if s - 1 < 2:
                 wa_q[s - 1, 1] = carried
             elif carried:
-                wr_q[(s - 1) // 4] = carried
+                wr_q[s - 4] = carried
 
-        for s in range(last):
-            if s in riders:
-                round_rider(s, *riders[s])
-            if s < TURNED:
+        for s in range(2):
+            differences(s)
+        scale(0, 0)
+        for s in range(TURNED):
+            if s + 1 < TURNED:
                 scale(s, 1)
-            else:
-                subtract(s + 1, whole if s + 1 < last else halves[0])
-            if s:
-                quantise_before(s)
-            if s < TURNED:
+                if s:
+                    quantise_before(s)
                 round_e(s)
-            if s + 2 <= last:
-                sample_logs(s + 2)
-            if 3 <= s <= 4:
-                library_logs(s + 3, 6, kept("log_b%d" % (s + 3), [P, STEP], F32, ["tab2_w", "tab_w0", "tab_w1"][s - 2])[:])
-            if s == GROUPS + 1:
-                score_passes(0, 1)
-            if s > GROUPS:
-                score_passes(1, s - GROUPS - 1)
-                store_scores(s - GROUPS - 1, (0, 1) if s == GROUPS + 1 else (0,))
-            if s < TURNED:
-                square(s, 0)
-                if s + 1 < TURNED:
-                    scale(s + 1, 0)
-                else:
-                    subtract(s + 1, whole)
-                square(s, 1)
-                if s + 2 < TURNED:
-                    differences(s + 2)
             else:
-                square_direct(s, whole, direct_values[s][:, 1])
-            if s == GROUPS:
-                score_passes(0, 0)
-            if s == GROUPS + 1:
-                score_passes(0, 2)
+                subtract(s + 1, whole)
+                direct_values = kept("direct_values", [P, 2, STEP], BF16, "wa_raw01")
+                round_direct(s + 1, whole, direct_values[:, 0], nc.scalar.copy)
+                quantise_before(s)
+                round_e(s, slice(0, PASS))
+                scale(s, 1)
+                round_e(s, slice(PASS, STEP))
+            if s in riders:
+                round_rider(s)
+            if s + 2 <= last:
+                sample_logs(s + 2, 6 * (s % 2) if s + 2 < last else 2)
+            if s in (1, 2):
+                library_logs(s + 5, 6 - 6 * (s % 2))
+            if s == 4:
+                score_passes(0, 0, 6)
+            if s == 5:
+                score_passes(1, 0)
+                score_passes(0, 1, 0)
+            for u in range(2):
+                square(s, u)
+                if u == 0 and s < 4:
+                    negate_tile(4 + s // 2, s % 2, scaled(s)[:, 0:PASS])
+                if s + 2 < TURNED:
+                    turn_library(s + 2, u)
+                    turn_sample(s + 2, u)
+                if u == 0 and s + 1 < TURNED:
+                    scale(s + 1, 0)
+        store_scores(0)
+        subtract(last, halves[0])
+        quantise_before(6)
+        score_passes(1, 1)
+        score_passes(0, 2, 4)
         subtract(last, halves[1])
-        store_scores(1, (1,))
-        quantise_before(last)
+        square_direct(6, whole, direct_values[:, 1])
+        store_scores(1)
+        last_values = kept("last_values", [P, 2, 2, PASS], BF16)
+        square_direct(last, halves[0], last_values[:, 0, 1])
+        pair = quantise("step6", direct_values[:].rearrange("p x c -> p (x c)"), 2 * GROUP)
+        made[STEPS[6]] = window(pair, 0, GROUP), window(pair, GROUP, GROUP)
         for u in range(2):
             last_passes(0, u, window(made[0, 3][0], u * P, P), window(made[0, 3][1], u * P, P))
         score_passes(1, 2)
-        last_values = kept("last_values", [P, 2, 2, PASS], BF16)
-        square_direct(last, halves[0], last_values[:, 0, 1])
         round_direct(last, halves[0], last_values[:, 0, 0])
         square_direct(last, halves[1], last_values[:, 1, 1])
         for u in range(2):

@@ -28,7 +28,7 @@ STEP = SLOTS * GROUP
 BLOCK = SLOTS * PASS
 STEPS = [(rb, g) for rb in range(2) for g in range(GROUPS)]
 TURNED = 6
-SHARES = {0: 64, 1: 32, 3: 32, 4: 0}
+SCALAR_GAINS = ()
 
 
 def tile_list_metabolite_annotation_scores_kernel(
@@ -106,9 +106,10 @@ def tile_list_metabolite_annotation_scores_kernel(
         nc.sync.dma_start(out=as_words(w4_w[:]), in_=as_words(w4_words[0]))
         load_plane(as_words(w4_sc[:]), lambda q: as_words(w4_scales[0])[q, :])
         nc.sync.dma_start(out=as_words(tab_sc[:])[0:P:4, :], in_=as_words(tab_scales).rearrange("a q c -> q a c"))
+        tab_w = []
         for kp in range(2):
             wa_raw[kp, 0] = load_wa(kp, 0)
-        tab_w = [load_table("tab_w%d" % kp, tab_words[kp]) for kp in range(2)]
+            tab_w.append(load_table("tab_w%d" % kp, tab_words[kp]))
 
         v2_sc = kept("v2_sc", [P, S], U8)
         v2_w = kept("v2_w", [P, S], U32)
@@ -136,9 +137,9 @@ def tile_list_metabolite_annotation_scores_kernel(
         last = len(STEPS) - 1
         log_b, log_a, minus, diff, made, banks, wa_q, wr_q = {}, {}, {}, {}, {}, {}, {}, {}
 
-        def library_logs(s, first_bank):
+        def library_logs(s, first_bank, logs=None):
             rb, g = STEPS[s]
-            logs = kept("log_b%d" % s, [P, STEP], F32)
+            logs = kept("log_b%d" % s, [P, STEP], F32)[:] if logs is None else logs
             log_b[s] = logs
             for u in range(2):
                 if s < TURNED:
@@ -163,7 +164,7 @@ def tile_list_metabolite_annotation_scores_kernel(
         def negate(s, dst):
             for u in range(2):
                 minus[s, u] = dst[:, u * PASS : (u + 1) * PASS]
-            pool_copy(dst, log_b[s][:], -1.0)
+            pool_copy(dst, log_b[s], -1.0)
 
         def negate_tile(s, u, dst):
             minus[s, u] = dst
@@ -175,11 +176,11 @@ def tile_list_metabolite_annotation_scores_kernel(
                 if s < TURNED:
                     j0 = g * GROUP + u * P
                     sums = bank(first_bank + u, [P, PASS])
-                    for kp in (1, 0):
+                    for kp in range(2):
                         words, plane = wa_q[kp, rb]
                         nc.tensor.matmul_mx(out=sums[:], lhsT=v_w[kp][:, j0 : j0 + P].bitcast(FP8X4),
                                             lhsT_scale=v_sc[:, kp * S + j0 : kp * S + j0 + P], rhs=words.bitcast(FP8X4),
-                                            rhs_scale=plane, start=(kp == 1), stop=(kp == 0))
+                                            rhs_scale=plane, start=(kp == 0), stop=(kp == 1))
                     log_a[s, u] = work.tile([P, SLOTS, P], F32, name="log_a", bufs=6)
                     order = "p (t m) -> p t m" if rb else "p (m t) -> p t m"
                     nc.scalar.activation(out=log_a[s, u][:], in_=sums[:].rearrange(order, t=SLOTS), func=ACT.Ln, bias=1.0)
@@ -242,15 +243,31 @@ def tile_list_metabolite_annotation_scores_kernel(
 
         def scale(s, u):
             rb = STEPS[s][0]
+            if (s, u) in SCALAR_GAINS:
+                for t in range(SLOTS):
+                    nc.scalar.activation(out=by_slots(scaled(s)[:, u * PASS : (u + 1) * PASS])[:, t, :], in_=diff[s, u][:, t, :],
+                                         func=ACT.Copy, scale=gains[:, rb, t : t + 1])
+                return
             nc.vector.tensor_tensor(out=scaled(s)[:, u * PASS : (u + 1) * PASS].rearrange("p (j t) -> p j t", t=SLOTS),
                                     in0=diff[s, u][:].rearrange("p t j -> p j t"),
                                     in1=gains[:, rb : rb + 1, :].to_broadcast([P, P, SLOTS]), op=ALU.mult)
 
-        def round_e(s, part=slice(0, STEP)):
-            pool_copy(e_values[:, part], scaled(s)[:, part])
+        def round_e(s):
+            pool_copy(e_values, scaled(s))
+
+        def round_tile(s, u):
+            tile = slice(u * PASS, (u + 1) * PASS)
+            if (s, u) in SCALAR_GAINS:
+                pool_copy(e_values[:, tile].rearrange("p (j t) -> p j t", t=SLOTS), by_slots(scaled(s)[:, tile]).rearrange("p t j -> p j t"))
+            else:
+                pool_copy(e_values[:, tile], scaled(s)[:, tile])
 
         def square(s, u):
             tile = slice(u * PASS, (u + 1) * PASS)
+            if (s, u) in SCALAR_GAINS:
+                nc.vector.tensor_tensor(out=sq_values(s)[:, tile].rearrange(woven, i=LINE, t=SLOTS), in0=diff[s, u][:].rearrange(apart, i=LINE),
+                                        in1=by_slots(scaled(s)[:, tile]).rearrange(apart, i=LINE), op=ALU.mult)
+                return
             nc.vector.tensor_tensor(out=sq_values(s)[:, tile].rearrange("p (j t) -> p j t", t=SLOTS), in0=diff[s, u][:].rearrange("p t j -> p j t"),
                                     in1=scaled(s)[:, tile].rearrange("p (j t) -> p j t", t=SLOTS), op=ALU.mult)
 
@@ -259,7 +276,7 @@ def tile_list_metabolite_annotation_scores_kernel(
 
         def subtract(s, part):
             d = log_a[s][:, :, part]
-            nc.vector.tensor_tensor(out=d, in0=d, in1=by_slots(log_b[s][:])[:, :, part], op=ALU.subtract)
+            nc.vector.tensor_tensor(out=d, in0=d, in1=by_slots(log_b[s])[:, :, part], op=ALU.subtract)
             for t in range(SLOTS):
                 nc.scalar.activation(out=by_slots(scaled(s))[:, t, part], in_=d[:, t, :], func=ACT.Copy, scale=gains[:, 1, t : t + 1])
 
@@ -288,12 +305,12 @@ def tile_list_metabolite_annotation_scores_kernel(
 
         rows = out.rearrange("(nt p) j -> p nt j", p=P)
 
-        spent = ["tab2_w", "tab_w0", "wa_raw11", "wa_raw00", "wa_raw10", "wr_raw0"]
+        spent = ["tab2_w", "tab_w0", "log_b0", "wa_raw00", "wa_raw01", "wr_raw0"]
 
-        def store_scores(g):
-            for pair in range(2):
+        def store_scores(g, copies=(nc.scalar.copy, nc.scalar.copy)):
+            for pair, copy in enumerate(copies):
                 staged = kept("staged%d%d" % (g, pair), [P, 2, GROUP], F32, spent[2 * g + pair])
-                nc.scalar.copy(out=staged[:], in_=banks[g, pair][:])
+                copy(out=staged[:], in_=banks[g, pair][:])
                 nc.sync.dma_start(out=rows[:, 2 * pair : 2 * pair + 2, g * GROUP : (g + 1) * GROUP], in_=staged[:])
 
         last_banks = [[6], [2, 3]]
@@ -315,40 +332,40 @@ def tile_list_metabolite_annotation_scores_kernel(
                 nc.sync.dma_start(out=rows[:, i * count : (i + 1) * count, j0 : j0 + P], in_=staged[:])
 
         first_values = kept("first_values", [P, 2 * BLOCK], BF16)
-        library_logs(0, 0)
-        round_rows(nc.scalar.copy, wa_raw[0, 0], first_values[:, 0:BLOCK], natural, slice(0, P))
-        negate(0, log_b[0][:])
-        round_rows(nc.vector.tensor_copy, wa_raw[1, 0], first_values[:, BLOCK:], natural, slice(0, P))
+        low, high = slice(0, P // 2), slice(P // 2, P)
+        for s in range(2):
+            library_logs(s, 6 * s)
+        round_rows(nc.scalar.copy, wa_raw[0, 0], first_values[:, 0:BLOCK], natural, low)
+        pool_copy(first_values[:, BLOCK // 2 : BLOCK].rearrange("p (c j) -> p c j", j=SLOTS),
+                  wa_raw[0, 0][:].rearrange("p j c -> p c j")[:, PASS // 2 :])
+        negate(0, log_b[0])
+        negate(1, log_b[1])
+        library_logs(2, 0)
+        v_w = [kept("v_w%d" % kp, [P, S], U32) for kp in range(2)]
+        gather(v_w[0], tab_w[0], list8, 0, S)
+        round_rows(nc.scalar.copy, wa_raw[1, 0], first_values[:, BLOCK:], natural, low)
+        round_rows(nc.vector.tensor_copy, wa_raw[1, 0], first_values[:, BLOCK:], natural, high)
         pair = quantise("wa_first", first_values[:], 2 * PASS)
         for kp in range(2):
             wa_q[kp, 0] = window(pair, kp * PASS, PASS)
-        for s in range(1, TURNED):
-            library_logs(s, 6 * (s % 2))
-        negate(1, kept("held", [P, STEP], F32, "first_values")[:])
-        for s in range(2, 4):
-            negate(s, log_b[s - 1][:])
-        v_w = [kept("v_w%d" % kp, [P, S], U32) for kp in range(2)]
-        for kp, first, end in ((0, 0, GROUP), (1, 0, GROUP), (0, GROUP, 2 * GROUP), (1, GROUP, 2 * GROUP), (0, 2 * GROUP, 3 * GROUP),
-                               (1, 2 * GROUP, S), (0, 3 * GROUP, S)):
-            gather(v_w[kp], tab_w[kp], list8, first, end)
+        library_logs(3, 6)
+        late = kept("log_b45", [P, 2, STEP], F32, "wa_raw10")
+        for s in range(4, 6):
+            library_logs(s, 6 * (s % 2), late[:, s - 4])
+        library_logs(6, 6)
+        held = kept("held", [P, 2, STEP], F32, "first_values")
+        negate(2, held[:, 0])
+        negate(3, held[:, 1])
+        negate(4, log_b[3])
+        for first, end in ((0, GROUP), (GROUP, 2 * GROUP), (2 * GROUP, S)):
+            gather(v_w[1], tab_w[1], list8, first, end)
         values = kept("values", [P, 2 * BLOCK + 3 * STEP], BF16, "tab_w1")
         e_values = values[:, BLOCK + STEP : BLOCK + 2 * STEP]
-        riders = {0: (wa_raw[0, 1], by_slot), 1: (wa_raw[1, 1], by_slot), 3: (wr_raw[0], natural), 4: (wr_raw[1], natural)}
-        whole, halves = slice(0, GROUP), [slice(0, P), slice(P, GROUP)]
-
-        def differences(s):
-            for u in range(2):
-                turn_library(s, u)
-            sample_logs(s, 6 * (s % 2))
-            for u in range(2):
-                turn_sample(s, u)
+        riders = {0: (wa_raw[0, 1], by_slot), 1: (wa_raw[1, 1], by_slot), 2: (wr_raw[0], natural), 3: (wr_raw[1], natural)}
+        halves = [slice(0, P), slice(P, GROUP)]
 
         def round_rider(s):
-            share = SHARES[s]
-            if share:
-                round_rows(nc.vector.tensor_copy, riders[s][0], rider_values(s), riders[s][1], slice(0, share))
-            middle = (share + P) // 2
-            for part in (slice(share, middle), slice(middle, P)):
+            for part in (low, high):
                 round_rows(nc.scalar.copy, riders[s][0], rider_values(s), riders[s][1], part)
 
         def quantise_before(s):
@@ -356,67 +373,73 @@ def tile_list_metabolite_annotation_scores_kernel(
             if s - 1 < 2:
                 wa_q[s - 1, 1] = carried
             elif carried:
-                wr_q[s - 4] = carried
+                wr_q[s - 3] = carried
 
         for s in range(2):
-            differences(s)
+            for u in range(2):
+                turn_library(s, u)
+            sample_logs(s, 6 * s)
+            for u in range(2):
+                turn_sample(s, u)
         scale(0, 0)
+        whole = slice(0, GROUP)
         for s in range(TURNED):
             if s + 1 < TURNED:
                 scale(s, 1)
                 if s:
                     quantise_before(s)
-                round_e(s)
+                if (s, 1) in SCALAR_GAINS:
+                    round_tile(s, 0)
+                    round_tile(s, 1)
+                else:
+                    round_e(s)
             else:
                 subtract(s + 1, whole)
-                direct_values = kept("direct_values", [P, 2, STEP], BF16, "wa_raw01")
+                direct_values = kept("direct_values", [P, 2, STEP], BF16, "wa_raw11")
                 round_direct(s + 1, whole, direct_values[:, 0], nc.scalar.copy)
                 quantise_before(s)
-                round_e(s, slice(0, PASS))
+                round_tile(s, 0)
                 scale(s, 1)
-                round_e(s, slice(PASS, STEP))
+                round_tile(s, 1)
             if s in riders:
                 round_rider(s)
             if s + 2 <= last:
                 sample_logs(s + 2, 6 * (s % 2) if s + 2 < last else 2)
-            if s in (1, 2):
-                library_logs(s + 5, 6 - 6 * (s % 2))
             if s == 4:
+                library_logs(last, 6)
                 score_passes(0, 0, 6)
             if s == 5:
                 score_passes(1, 0)
                 score_passes(0, 1, 0)
             for u in range(2):
                 square(s, u)
-                if u == 0 and s < 4:
-                    negate_tile(4 + s // 2, s % 2, scaled(s)[:, 0:PASS])
+                if u == 0 and s < 2:
+                    negate_tile(5, s, scaled(s)[:, 0:PASS])
                 if s + 2 < TURNED:
                     turn_library(s + 2, u)
                     turn_sample(s + 2, u)
                 if u == 0 and s + 1 < TURNED:
                     scale(s + 1, 0)
-        store_scores(0)
-        subtract(last, halves[0])
+        subtract(last, whole)
+        last_values = kept("last_values", [P, 2, 2, PASS], BF16)
+        for u in range(2):
+            round_direct(last, halves[u], last_values[:, u, 0], nc.scalar.copy)
         quantise_before(6)
+        store_scores(0)
         score_passes(1, 1)
         score_passes(0, 2, 4)
-        subtract(last, halves[1])
         square_direct(6, whole, direct_values[:, 1])
-        store_scores(1)
-        last_values = kept("last_values", [P, 2, 2, PASS], BF16)
         square_direct(last, halves[0], last_values[:, 0, 1])
         pair = quantise("step6", direct_values[:].rearrange("p x c -> p (x c)"), 2 * GROUP)
         made[STEPS[6]] = window(pair, 0, GROUP), window(pair, GROUP, GROUP)
         for u in range(2):
             last_passes(0, u, window(made[0, 3][0], u * P, P), window(made[0, 3][1], u * P, P))
+        store_scores(1)
         score_passes(1, 2)
-        round_direct(last, halves[0], last_values[:, 0, 0])
         square_direct(last, halves[1], last_values[:, 1, 1])
         for u in range(2):
-            if u:
-                round_direct(last, halves[1], last_values[:, 1, 0])
             pair = quantise("last%d" % u, last_values[:, u].rearrange("p s c -> p (s c)"), 2 * P)
             last_passes(1, u, window(pair, 0, P), window(pair, P, P))
-        store_scores(2)
+        store_scores(2, (nc.scalar.copy, nc.vector.tensor_copy))
         for u in range(2):
             store_last(u)

@@ -106,10 +106,9 @@ def tile_list_metabolite_annotation_scores_kernel(
         nc.sync.dma_start(out=as_words(w4_w[:]), in_=as_words(w4_words[0]))
         load_plane(as_words(w4_sc[:]), lambda q: as_words(w4_scales[0])[q, :])
         nc.sync.dma_start(out=as_words(tab_sc[:])[0:P:4, :], in_=as_words(tab_scales).rearrange("a q c -> q a c"))
-        tab_w = []
         for kp in range(2):
             wa_raw[kp, 0] = load_wa(kp, 0)
-            tab_w.append(load_table("tab_w%d" % kp, tab_words[kp]))
+        tab_w = [load_table("tab_w%d" % kp, tab_words[kp]) for kp in range(2)]
 
         v2_sc = kept("v2_sc", [P, S], U8)
         v2_w = kept("v2_w", [P, S], U32)
@@ -305,7 +304,7 @@ def tile_list_metabolite_annotation_scores_kernel(
 
         rows = out.rearrange("(nt p) j -> p nt j", p=P)
 
-        spent = ["tab2_w", "tab_w0", "log_b0", "wa_raw00", "wa_raw01", "wr_raw0"]
+        spent = ["tab2_w", "tab_w0", "log_b0", "wa_raw10", "wa_raw01", "wr_raw0"]
 
         def store_scores(g, copies=(nc.scalar.copy, nc.scalar.copy)):
             for pair, copy in enumerate(copies):
@@ -333,32 +332,22 @@ def tile_list_metabolite_annotation_scores_kernel(
 
         first_values = kept("first_values", [P, 2 * BLOCK], BF16)
         low, high = slice(0, P // 2), slice(P // 2, P)
-        for s in range(2):
-            library_logs(s, 6 * s)
-        round_rows(nc.scalar.copy, wa_raw[0, 0], first_values[:, 0:BLOCK], natural, low)
-        pool_copy(first_values[:, BLOCK // 2 : BLOCK].rearrange("p (c j) -> p c j", j=SLOTS),
-                  wa_raw[0, 0][:].rearrange("p j c -> p c j")[:, PASS // 2 :])
+        library_logs(0, 0)
         negate(0, log_b[0])
-        negate(1, log_b[1])
-        library_logs(2, 0)
-        v_w = [kept("v_w%d" % kp, [P, S], U32) for kp in range(2)]
-        gather(v_w[0], tab_w[0], list8, 0, S)
-        round_rows(nc.scalar.copy, wa_raw[1, 0], first_values[:, BLOCK:], natural, low)
-        round_rows(nc.vector.tensor_copy, wa_raw[1, 0], first_values[:, BLOCK:], natural, high)
+        for kp, copy in enumerate((nc.scalar.copy, nc.vector.tensor_copy)):
+            round_rows(copy, wa_raw[kp, 0], first_values[:, kp * BLOCK : (kp + 1) * BLOCK], natural, slice(0, P))
         pair = quantise("wa_first", first_values[:], 2 * PASS)
         for kp in range(2):
             wa_q[kp, 0] = window(pair, kp * PASS, PASS)
-        library_logs(3, 6)
-        late = kept("log_b45", [P, 2, STEP], F32, "wa_raw10")
-        for s in range(4, 6):
-            library_logs(s, 6 * (s % 2), late[:, s - 4])
-        library_logs(6, 6)
+        early = kept("log_b12", [P, 2, STEP], F32, "wa_raw00")
+        for s in range(1, TURNED):
+            library_logs(s, 6 * (s % 2), early[:, s - 1] if s < 3 else None)
         held = kept("held", [P, 2, STEP], F32, "first_values")
-        negate(2, held[:, 0])
-        negate(3, held[:, 1])
-        negate(4, log_b[3])
-        for first, end in ((0, GROUP), (GROUP, 2 * GROUP), (2 * GROUP, S)):
-            gather(v_w[1], tab_w[1], list8, first, end)
+        for s in range(1, 4):
+            negate(s, held[:, s - 1] if s < 3 else log_b[2])
+        v_w = [kept("v_w%d" % kp, [P, S], U32) for kp in range(2)]
+        for kp, first, end in ((0, 0, S), (1, 0, GROUP), (1, GROUP, 2 * GROUP), (1, 2 * GROUP, S)):
+            gather(v_w[kp], tab_w[kp], list8, first, end)
         values = kept("values", [P, 2 * BLOCK + 3 * STEP], BF16, "tab_w1")
         e_values = values[:, BLOCK + STEP : BLOCK + 2 * STEP]
         riders = {0: (wa_raw[0, 1], by_slot), 1: (wa_raw[1, 1], by_slot), 2: (wr_raw[0], natural), 3: (wr_raw[1], natural)}
@@ -366,7 +355,8 @@ def tile_list_metabolite_annotation_scores_kernel(
 
         def round_rider(s):
             for part in (low, high):
-                round_rows(nc.scalar.copy, riders[s][0], rider_values(s), riders[s][1], part)
+                copy = nc.vector.tensor_copy if (s, part) == (0, low) else nc.scalar.copy
+                round_rows(copy, riders[s][0], rider_values(s), riders[s][1], part)
 
         def quantise_before(s):
             carried = quantise_step(s - 1, s - 1 in riders)
@@ -405,6 +395,8 @@ def tile_list_metabolite_annotation_scores_kernel(
                 round_rider(s)
             if s + 2 <= last:
                 sample_logs(s + 2, 6 * (s % 2) if s + 2 < last else 2)
+            if s == 3:
+                library_logs(6, 6)
             if s == 4:
                 library_logs(last, 6)
                 score_passes(0, 0, 6)
@@ -413,8 +405,8 @@ def tile_list_metabolite_annotation_scores_kernel(
                 score_passes(0, 1, 0)
             for u in range(2):
                 square(s, u)
-                if u == 0 and s < 2:
-                    negate_tile(5, s, scaled(s)[:, 0:PASS])
+                if u == 0 and s < 4:
+                    negate_tile(4 + s // 2, s % 2, scaled(s)[:, 0:PASS])
                 if s + 2 < TURNED:
                     turn_library(s + 2, u)
                     turn_sample(s + 2, u)

@@ -89,8 +89,8 @@ def tile_list_metabolite_annotation_scores_kernel(
         def pool_copy(out, in_, factor=1.0):
             nc.gpsimd.tensor_scalar(out=out, in0=in_, scalar1=factor, scalar2=0.0, op0=ALU.mult, op1=ALU.add)
 
-        def quantise(name, values, columns):
-            words = kept(name + "_w", [P, columns], U32)
+        def quantise(name, values, columns, buffer=None):
+            words = kept(name + "_w", [P, columns], U32, buffer)
             plane = kept(name + "_sc", [P, columns], U8)
             nc.vector.quantize_mx(out=words[:].bitcast(FP8X4), scales=plane[:], in_=values)
             return words, plane
@@ -185,7 +185,7 @@ def tile_list_metabolite_annotation_scores_kernel(
                     nc.scalar.activation(out=log_a[s, u][:], in_=sums[:].rearrange(order, t=SLOTS), func=ACT.Ln, bias=1.0)
                 else:
                     if u == 0:
-                        log_a[s] = work.tile([P, SLOTS, GROUP], F32, name="log_a_direct")
+                        log_a[s] = kept("log_a%d" % s, [P, SLOTS, GROUP], F32)
                     sums = bank(first_bank + u, [P, 2, GROUP])
                     entries = slice(g * GROUP, (g + 1) * GROUP)
                     for i in range(2):
@@ -210,8 +210,11 @@ def tile_list_metabolite_annotation_scores_kernel(
         def turn_sample(s, u):
             turn(s, u, log_a[s, u][:], False, True)
 
+        def side(s):
+            return min(s, TURNED - 2) % 2
+
         def sq_values(s):
-            first = BLOCK + 2 * STEP * (s % 2)
+            first = BLOCK + 2 * STEP * side(s)
             return values[:, first : first + STEP]
 
         def rider_values(s):
@@ -225,11 +228,12 @@ def tile_list_metabolite_annotation_scores_kernel(
 
         def quantise_step(s, rider):
             extra = BLOCK if rider else 0
-            if s % 2:
+            if side(s):
                 first, places = BLOCK + STEP, (0, GROUP, 2 * GROUP)
             else:
                 first, places = BLOCK - extra, (extra // SLOTS + GROUP, extra // SLOTS, 0)
-            pair = quantise("step%d" % s, values[:, first : first + 2 * STEP + extra], (2 * STEP + extra) // SLOTS)
+            pair = quantise("step%d" % s, values[:, first : first + 2 * STEP + extra], (2 * STEP + extra) // SLOTS,
+                            "log_b%d" % (s + 2) if s + 2 >= TURNED else None)
             made[STEPS[s]] = window(pair, places[0], GROUP), window(pair, places[1], GROUP)
             return window(pair, places[2], PASS) if rider else None
 
@@ -238,7 +242,8 @@ def tile_list_metabolite_annotation_scores_kernel(
         scaled_all = kept("scaled_all", [P, 4 * STEP], F32)
 
         def scaled(s):
-            return scaled_all[:, s % 4 * STEP : (s % 4 + 1) * STEP]
+            place = s % 2 if s < TURNED else s - TURNED + 2
+            return scaled_all[:, place * STEP : (place + 1) * STEP]
 
         def scale(s, u):
             rb = STEPS[s][0]
@@ -274,14 +279,14 @@ def tile_list_metabolite_annotation_scores_kernel(
             return ap.rearrange("p (t c) -> p t c", t=SLOTS)
 
         def subtract(s, part):
-            d = log_a[s][:, :, part]
-            nc.vector.tensor_tensor(out=d, in0=d, in1=by_slots(log_b[s])[:, :, part], op=ALU.subtract)
+            d = by_slots(scaled(s - 2))[:, :, part]
+            nc.vector.tensor_tensor(out=d, in0=log_a[s][:, :, part], in1=by_slots(log_b[s])[:, :, part], op=ALU.subtract)
             for t in range(SLOTS):
                 nc.scalar.activation(out=by_slots(scaled(s))[:, t, part], in_=d[:, t, :], func=ACT.Copy, scale=gains[:, 1, t : t + 1])
 
         def square_direct(s, part, dst):
             nc.vector.tensor_tensor(out=dst.rearrange(woven, i=LINE, t=SLOTS), in0=by_slots(scaled(s))[:, :, part].rearrange(apart, i=LINE),
-                                    in1=log_a[s][:, :, part].rearrange(apart, i=LINE), op=ALU.mult)
+                                    in1=by_slots(scaled(s - 2))[:, :, part].rearrange(apart, i=LINE), op=ALU.mult)
 
         def round_direct(s, part, dst, copy=nc.vector.tensor_copy):
             copy(out=dst.rearrange(woven, i=LINE, t=SLOTS), in_=by_slots(scaled(s))[:, :, part].rearrange(apart, i=LINE))
@@ -304,7 +309,7 @@ def tile_list_metabolite_annotation_scores_kernel(
 
         rows = out.rearrange("(nt p) j -> p nt j", p=P)
 
-        spent = ["tab2_w", "tab_w0", "log_b0", "wa_raw10", "wa_raw01", "wr_raw0"]
+        spent = ["tab2_w", "tab_w0", "log_b4", "wa_raw10", "wa_raw01", "last_values"]
 
         def store_scores(g, copies=(nc.scalar.copy, nc.scalar.copy)):
             for pair, copy in enumerate(copies):
@@ -312,7 +317,7 @@ def tile_list_metabolite_annotation_scores_kernel(
                 copy(out=staged[:], in_=banks[g, pair][:])
                 nc.sync.dma_start(out=rows[:, 2 * pair : 2 * pair + 2, g * GROUP : (g + 1) * GROUP], in_=staged[:])
 
-        last_banks = [[6], [2, 3]]
+        last_banks = [[4], [5, 0]]
 
         def last_passes(rb, u, e, sq):
             count = 4 // (u + 1)
@@ -343,8 +348,8 @@ def tile_list_metabolite_annotation_scores_kernel(
         for s in range(1, TURNED):
             library_logs(s, 6 * (s % 2), early[:, s - 1] if s < 3 else None)
         held = kept("held", [P, 2, STEP], F32, "first_values")
-        for s in range(1, 4):
-            negate(s, held[:, s - 1] if s < 3 else log_b[2])
+        for s in range(1, TURNED):
+            negate(s, held[:, s - 1] if s < 3 else log_b[s - 2])
         v_w = [kept("v_w%d" % kp, [P, S], U32) for kp in range(2)]
         for kp, first, end in ((0, 0, S), (1, 0, GROUP), (1, GROUP, 2 * GROUP), (1, 2 * GROUP, S)):
             gather(v_w[kp], tab_w[kp], list8, first, end)
@@ -355,8 +360,7 @@ def tile_list_metabolite_annotation_scores_kernel(
 
         def round_rider(s):
             for part in (low, high):
-                copy = nc.vector.tensor_copy if (s, part) == (0, low) else nc.scalar.copy
-                round_rows(copy, riders[s][0], rider_values(s), riders[s][1], part)
+                round_rows(nc.scalar.copy, riders[s][0], rider_values(s), riders[s][1], part)
 
         def quantise_before(s):
             carried = quantise_step(s - 1, s - 1 in riders)
@@ -373,60 +377,52 @@ def tile_list_metabolite_annotation_scores_kernel(
                 turn_sample(s, u)
         scale(0, 0)
         whole = slice(0, GROUP)
+        e_direct = kept("e_direct", [P, STEP], BF16, "wa_raw11")
+        last_values = kept("last_values", [P, 2, 2, PASS], BF16)
         for s in range(TURNED):
-            if s + 1 < TURNED:
-                scale(s, 1)
-                if s:
-                    quantise_before(s)
-                if (s, 1) in SCALAR_GAINS:
-                    round_tile(s, 0)
-                    round_tile(s, 1)
-                else:
-                    round_e(s)
-            else:
-                subtract(s + 1, whole)
-                direct_values = kept("direct_values", [P, 2, STEP], BF16, "wa_raw11")
-                round_direct(s + 1, whole, direct_values[:, 0], nc.scalar.copy)
+            scale(s, 1)
+            if s == 5:
+                subtract(6, whole)
+                round_direct(6, whole, e_direct[:], nc.scalar.copy)
+            if s:
                 quantise_before(s)
-                round_tile(s, 0)
-                scale(s, 1)
-                round_tile(s, 1)
+            round_e(s)
             if s in riders:
                 round_rider(s)
-            if s + 2 <= last:
-                sample_logs(s + 2, 6 * (s % 2) if s + 2 < last else 2)
+            if s < 3:
+                sample_logs(s + 2, 6 * (s % 2))
             if s == 3:
+                sample_logs(5, 6)
+                sample_logs(6, 0)
                 library_logs(6, 6)
             if s == 4:
-                library_logs(last, 6)
-                score_passes(0, 0, 6)
+                library_logs(last, 0)
+                sample_logs(last, 6)
+                score_passes(0, 0, 0)
             if s == 5:
                 score_passes(1, 0)
-                score_passes(0, 1, 0)
+                store_scores(0)
+                score_passes(0, 1, 6)
+                score_passes(0, 2, 2)
             for u in range(2):
                 square(s, u)
-                if u == 0 and s < 4:
-                    negate_tile(4 + s // 2, s % 2, scaled(s)[:, 0:PASS])
                 if s + 2 < TURNED:
                     turn_library(s + 2, u)
                     turn_sample(s + 2, u)
                 if u == 0 and s + 1 < TURNED:
                     scale(s + 1, 0)
         subtract(last, whole)
-        last_values = kept("last_values", [P, 2, 2, PASS], BF16)
         for u in range(2):
             round_direct(last, halves[u], last_values[:, u, 0], nc.scalar.copy)
         quantise_before(6)
-        store_scores(0)
         score_passes(1, 1)
-        score_passes(0, 2, 4)
-        square_direct(6, whole, direct_values[:, 1])
+        store_scores(1)
+        sq_direct = kept("sq_direct", [P, STEP], BF16, "log_a%d" % last)
+        square_direct(6, whole, sq_direct[:])
         square_direct(last, halves[0], last_values[:, 0, 1])
-        pair = quantise("step6", direct_values[:].rearrange("p x c -> p (x c)"), 2 * GROUP)
-        made[STEPS[6]] = window(pair, 0, GROUP), window(pair, GROUP, GROUP)
+        made[STEPS[6]] = [window(quantise(name, tile[:], GROUP), 0, GROUP) for name, tile in (("e6", e_direct), ("sq6", sq_direct))]
         for u in range(2):
             last_passes(0, u, window(made[0, 3][0], u * P, P), window(made[0, 3][1], u * P, P))
-        store_scores(1)
         score_passes(1, 2)
         square_direct(last, halves[1], last_values[:, 1, 1])
         for u in range(2):

@@ -108,7 +108,7 @@ def tile_list_metabolite_annotation_scores_kernel(
         nc.sync.dma_start(out=as_words(tab_sc[:])[0:P:4, :], in_=as_words(tab_scales).rearrange("a q c -> q a c"))
         for kp in range(2):
             wa_raw[kp, 0] = load_wa(kp, 0)
-        tab_w = [load_table("tab_w%d" % kp, tab_words[kp]) for kp in range(2)]
+        tab_w = [load_table("tab_w0", tab_words[0])]
 
         v2_sc = kept("v2_sc", [P, S], U8)
         v2_w = kept("v2_w", [P, S], U32)
@@ -125,6 +125,7 @@ def tile_list_metabolite_annotation_scores_kernel(
                               in_=w4_sc[:, PASS : 2 * PASS].rearrange("p (m t) -> p t m", t=SLOTS))
         for d in range(0, P, QUADRANT):
             nc.sync.dma_start(out=as_words(v_sc[:])[d : d + 4, :], in_=as_words(picked_sc[:])[d : d + QUADRANT : 4, :])
+        tab_w.append(load_table("tab_w1", tab_words[1]))
         wa_raw[0, 1] = load_wa(0, 1)
         wa_raw[1, 1] = load_wa(1, 1)
         wr_raw = [load_rows("wr_raw%d" % rb, wr[rb * PASS : (rb + 1) * PASS, :]) for rb in range(2)]
@@ -175,11 +176,11 @@ def tile_list_metabolite_annotation_scores_kernel(
                 if s < TURNED:
                     j0 = g * GROUP + u * P
                     sums = bank(first_bank + u, [P, PASS])
-                    for kp in range(2):
+                    for kp in ((1, 0) if s == 1 else (0, 1)):
                         words, plane = wa_q[kp, rb]
                         nc.tensor.matmul_mx(out=sums[:], lhsT=v_w[kp][:, j0 : j0 + P].bitcast(FP8X4),
                                             lhsT_scale=v_sc[:, kp * S + j0 : kp * S + j0 + P], rhs=words.bitcast(FP8X4),
-                                            rhs_scale=plane, start=(kp == 0), stop=(kp == 1))
+                                            rhs_scale=plane, start=(kp == (s == 1)), stop=(kp != (s == 1)))
                     log_a[s, u] = work.tile([P, SLOTS, P], F32, name="log_a", bufs=6)
                     order = "p (t m) -> p t m" if rb else "p (m t) -> p t m"
                     nc.scalar.activation(out=log_a[s, u][:], in_=sums[:].rearrange(order, t=SLOTS), func=ACT.Ln, bias=1.0)
@@ -351,7 +352,7 @@ def tile_list_metabolite_annotation_scores_kernel(
         for s in range(1, TURNED):
             negate(s, held[:, s - 1] if s < 3 else log_b[s - 2])
         v_w = [kept("v_w%d" % kp, [P, S], U32) for kp in range(2)]
-        for kp, first, end in ((0, 0, S), (1, 0, GROUP), (1, GROUP, 2 * GROUP), (1, 2 * GROUP, S)):
+        for kp, first, end in ((0, 0, 2 * GROUP), (0, 2 * GROUP, S), (1, 0, GROUP), (1, GROUP, 2 * GROUP), (1, 2 * GROUP, S)):
             gather(v_w[kp], tab_w[kp], list8, first, end)
         values = kept("values", [P, 2 * BLOCK + 3 * STEP], BF16, "tab_w1")
         e_values = values[:, BLOCK + STEP : BLOCK + 2 * STEP]

from contextlib import ExitStack

import concourse.mybir as mybir
from concourse.masks import make_identity

K, M, H, N, T, S = 1024, 512, 1024, 512, 2048, 1024
FLOPS = 2 * S * (K * H + M * H + 2 * H * N)

F32 = mybir.dt.float32
BF16 = mybir.dt.bfloat16
I32 = mybir.dt.int32
U32 = mybir.dt.uint32
U16 = mybir.dt.uint16
U8 = mybir.dt.uint8
FP8X4 = mybir.dt.float8_e4m3fn_x4
FP4X4 = mybir.dt.float4_e2m1fn_x4
ACT = mybir.ActivationFunctionType
ALU = mybir.AluOpType

P = 128
SLOTS = 4
PASS = P * SLOTS
QUADRANT = 32
GROUP = 256
GROUPS = S // GROUP
LINE = 4
STEP = SLOTS * GROUP
BLOCK = SLOTS * PASS
STEPS = [(rb, g) for rb in range(2) for g in range(GROUPS)]
TURNED = 6
SCALAR_GAINS = ()


def tile_list_metabolite_annotation_scores_kernel(
    tc, tab_words, tab_scales, offs, tab2_words, tab2_scales, offs2, wa, w4_words, w4_scales,
    gain, wr, w8_words, w8_scales, out,
):
    nc = tc.nc
    with ExitStack() as ctx:
        keep = ctx.enter_context(tc.tile_pool(name="keep", bufs=1))
        work = ctx.enter_context(tc.tile_pool(name="work", bufs=2))
        psum = ctx.enter_context(tc.psum_pool(name="psum", bufs=1))

        def kept(name, shape, dtype, buffer=None):
            return keep.tile(shape, dtype, name=name, tag=buffer or name, align_bytes=64)

        def bank(i, shape):
            return psum.tile(shape, F32, name="bank%d" % i)

        def as_words(ap):
            return ap.bitcast(I32)

        list8 = keep.tile([P, S // 16], U16, name="list8")
        list1 = keep.tile([P, S // 16], U16, name="list1")
        tab_sc = kept("tab_sc", [P, T], U8)
        tab2_sc = kept("tab2_sc", [P, T], U8)
        w4_sc = kept("w4_sc", [P, H], U8)
        w8_sc = kept("w8_sc", [P, 2 * N], U8)
        w4_w = kept("w4_w", [P, 2 * H], U8)
        identity = kept("identity", [P, P], F32)
        v_sc = kept("v_sc", [P, 2 * S], U8)
        for plane in (tab2_sc, w4_sc, tab_sc, w8_sc, v_sc):
            nc.vector.memset(as_words(plane[:]), 0)

        def load_plane(plane, rows):
            for r in range(4):
                nc.sync.dma_start(out=plane[r:P:QUADRANT], in_=rows(slice(r, 16, 4)))

        gains = kept("gains", [P, 2, SLOTS], F32)
        nc.gpsimd.dma_start(out=gains[:], in_=gain.rearrange("(b p t) -> p b t", b=2, t=SLOTS))
        make_identity(nc, identity[:])

        def load_table(name, words):
            tile = kept(name, [P, T], U32)
            nc.sync.dma_start(out=as_words(tile[:]), in_=as_words(words.rearrange("p t i -> p (t i)")))
            return tile

        def load_rows(name, rows):
            tile = kept(name, [P, SLOTS, PASS], F32)
            nc.sync.dma_start(out=tile[:], in_=rows.rearrange("(p j) c -> p j c", j=SLOTS))
            return tile

        def load_wa(kp, rb):
            return load_rows("wa_raw%d%d" % (kp, rb), wa[kp * PASS : (kp + 1) * PASS, rb * PASS : (rb + 1) * PASS])

        def gather(tile, table, offsets, first, end):
            nc.vector.tensor_copy(tile[:, first:end], table[:].indirect(offsets[:, first // 16 : end // 16]))

        def pool_copy(out, in_, factor=1.0):
            nc.gpsimd.tensor_scalar(out=out, in0=in_, scalar1=factor, scalar2=0.0, op0=ALU.mult, op1=ALU.add)

        def quantise(name, values, columns, buffer=None):
            words = kept(name + "_w", [P, columns], U32, buffer)
            plane = kept(name + "_sc", [P, columns], U8)
            nc.vector.quantize_mx(out=words[:].bitcast(FP8X4), scales=plane[:], in_=values)
            return words, plane

        def window(pair, first, width):
            return pair[0][:, first : first + width], pair[1][:, first : first + width]

        wa_raw = {}
        nc.sync.dma_start(list1[:], offs2)
        nc.sync.dma_start(list8[:], offs)
        load_plane(as_words(tab2_sc[:]), lambda q: as_words(tab2_scales[0])[q, :])
        tab2_w = load_table("tab2_w", tab2_words[0])
        nc.sync.dma_start(out=as_words(w4_w[:]), in_=as_words(w4_words[0]))
        load_plane(as_words(w4_sc[:]), lambda q: as_words(w4_scales[0])[q, :])
        nc.sync.dma_start(out=as_words(tab_sc[:])[0:P:4, :], in_=as_words(tab_scales).rearrange("a q c -> q a c"))
        for kp in range(2):
            wa_raw[kp, 0] = load_wa(kp, 0)
        tab_w = [load_table("tab_w0", tab_words[0])]

        v2_sc = kept("v2_sc", [P, S], U8)
        v2_w = kept("v2_w", [P, S], U32)
        picked_sc = kept("picked_sc", [P, S], U8)
        gather(v2_sc, tab2_sc, list1, 0, S)
        gather(v2_w, tab2_w, list1, 0, GROUP)
        gather(v2_w, tab2_w, list1, GROUP, S)
        gather(picked_sc, tab_sc, list8, 0, S)
        w4_slot_w = kept("w4_slot_w", [P, 2 * PASS], U8)
        nc.gpsimd.tensor_copy(out=w4_slot_w[:].rearrange("p (t m b) -> p t m b", t=SLOTS, b=2),
                              in_=w4_w[:, 2 * PASS : 4 * PASS].rearrange("p (m t b) -> p t m b", t=SLOTS, b=2))
        w4_slot_sc = kept("w4_slot_sc", [P, PASS], U8)
        nc.gpsimd.tensor_copy(out=w4_slot_sc[:].rearrange("p (t m) -> p t m", t=SLOTS),
                              in_=w4_sc[:, PASS : 2 * PASS].rearrange("p (m t) -> p t m", t=SLOTS))
        for d in range(0, P, QUADRANT):
            nc.sync.dma_start(out=as_words(v_sc[:])[d : d + 4, :], in_=as_words(picked_sc[:])[d : d + QUADRANT : 4, :])
        tab_w.append(load_table("tab_w1", tab_words[1]))
        wa_raw[0, 1] = load_wa(0, 1)
        wa_raw[1, 1] = load_wa(1, 1)
        wr_raw = [load_rows("wr_raw%d" % rb, wr[rb * PASS : (rb + 1) * PASS, :]) for rb in range(2)]
        load_plane(as_words(w8_sc[:]).rearrange("p (b n) -> p b n", b=2),
                   lambda q: as_words(w8_scales)[:, q, :].rearrange("b r n -> r b n"))
        w8_w = kept("w8_w", [P, 2, N], U32)
        nc.sync.dma_start(out=as_words(w8_w[:]), in_=as_words(w8_words.rearrange("b p n i -> p b (n i)")))

        last = len(STEPS) - 1
        log_b, log_a, minus, diff, made, banks, wa_q, wr_q = {}, {}, {}, {}, {}, {}, {}, {}

        def library_logs(s, first_bank, logs=None):
            rb, g = STEPS[s]
            logs = kept("log_b%d" % s, [P, STEP], F32)[:] if logs is None else logs
            log_b[s] = logs
            for u in range(2):
                if s < TURNED:
                    j0 = g * GROUP + u * P
                    sums = bank(first_bank + u, [P, PASS])
                    nc.tensor.matmul_mx(out=sums[:], lhsT=v2_w[:, j0 : j0 + P].bitcast(FP8X4), lhsT_scale=v2_sc[:, j0 : j0 + P],
                                        rhs=w4_w[:, 2 * rb * PASS : 2 * (rb + 1) * PASS].bitcast(FP4X4),
                                        rhs_scale=w4_sc[:, rb * PASS : (rb + 1) * PASS], start=True, stop=True)
                    nc.scalar.activation(out=logs[:, u * PASS : (u + 1) * PASS].rearrange("p (t m) -> p t m", t=SLOTS),
                                         in_=sums[:].rearrange("p (m t) -> p t m", t=SLOTS), func=ACT.Ln, bias=1.0)
                else:
                    sums = bank(first_bank + u, [P, 2, GROUP])
                    entries = slice(g * GROUP, (g + 1) * GROUP)
                    for i in range(2):
                        c = (2 * u + i) * P
                        nc.tensor.matmul_mx(out=sums[:, i, :], lhsT=w4_slot_w[:, 2 * c : 2 * (c + P)].bitcast(FP4X4),
                                            lhsT_scale=w4_slot_sc[:, c : c + P], rhs=v2_w[:, entries].bitcast(FP8X4),
                                            rhs_scale=v2_sc[:, entries], start=True, stop=True)
                    nc.scalar.activation(out=logs[:, u * PASS : (u + 1) * PASS], in_=sums[:].rearrange("p i c -> p (i c)"),
                                         func=ACT.Ln, bias=1.0)

        def negate(s, dst):
            for u in range(2):
                minus[s, u] = dst[:, u * PASS : (u + 1) * PASS]
            pool_copy(dst, log_b[s], -1.0)

        def negate_tile(s, u, dst):
            minus[s, u] = dst
            pool_copy(dst, log_b[s][:, u * PASS : (u + 1) * PASS], -1.0)

        def sample_logs(s, first_bank):
            rb, g = STEPS[s]
            for u in range(2):
                if s < TURNED:
                    j0 = g * GROUP + u * P
                    sums = bank(first_bank + u, [P, PASS])
                    for kp in ((1, 0) if s == 1 else (0, 1)):
                        words, plane = wa_q[kp, rb]
                        nc.tensor.matmul_mx(out=sums[:], lhsT=v_w[kp][:, j0 : j0 + P].bitcast(FP8X4),
                                            lhsT_scale=v_sc[:, kp * S + j0 : kp * S + j0 + P], rhs=words.bitcast(FP8X4),
                                            rhs_scale=plane, start=(kp == (s == 1)), stop=(kp != (s == 1)))
                    log_a[s, u] = work.tile([P, SLOTS, P], F32, name="log_a", bufs=6)
                    order = "p (t m) -> p t m" if rb else "p (m t) -> p t m"
                    nc.scalar.activation(out=log_a[s, u][:], in_=sums[:].rearrange(order, t=SLOTS), func=ACT.Ln, bias=1.0)
                else:
                    if u == 0:
                        log_a[s] = kept("log_a%d" % s, [P, SLOTS, GROUP], F32)
                    sums = bank(first_bank + u, [P, 2, GROUP])
                    entries = slice(g * GROUP, (g + 1) * GROUP)
                    for i in range(2):
                        cols = slice((2 * u + i) * P, (2 * u + i + 1) * P)
                        for kp in range(2):
                            words, plane = wa_q[kp, rb]
                            nc.tensor.matmul_mx(out=sums[:, i, :], lhsT=words[:, cols].bitcast(FP8X4), lhsT_scale=plane[:, cols],
                                                rhs=v_w[kp][:, entries].bitcast(FP8X4), rhs_scale=v_sc[:, kp * S + g * GROUP : kp * S + (g + 1) * GROUP],
                                                start=(kp == 0), stop=(kp == 1))
                    nc.scalar.activation(out=log_a[s][:, 2 * u : 2 * u + 2, :], in_=sums[:], func=ACT.Ln, bias=1.0)

        def turn(s, u, term, start, stop):
            if start:
                diff[s, u] = bank(2 + (2 * s + u) % 4, [P, SLOTS, P])
            for t in range(SLOTS):
                nc.tensor.matmul(out=diff[s, u][:, t, :], lhsT=term[:, t, :], rhs=identity[:], is_transpose=True,
                                 start=(start and t == 0), stop=(stop and t == SLOTS - 1))

        def turn_library(s, u):
            turn(s, u, by_slots(minus[s, u]), True, False)

        def turn_sample(s, u):
            turn(s, u, log_a[s, u][:], False, True)

        def side(s):
            return min(s, TURNED - 2) % 2

        def sq_values(s):
            first = BLOCK + 2 * STEP * side(s)
            return values[:, first : first + STEP]

        def rider_values(s):
            first = (BLOCK + 3 * STEP) * (s % 2)
            return values[:, first : first + BLOCK]

        natural, by_slot = "p (c i j) -> p c j i", "p (i c j) -> p c j i"

        def round_rows(copy, raw, dst, order, part):
            copy(out=dst.rearrange(order, i=LINE, j=SLOTS)[:, part], in_=raw[:].rearrange("p j (c i) -> p c j i", i=LINE)[:, part])

        def quantise_step(s, rider):
            extra = BLOCK if rider else 0
            if side(s):
                first, places = BLOCK + STEP, (0, GROUP, 2 * GROUP)
            else:
                first, places = BLOCK - extra, (extra // SLOTS + GROUP, extra // SLOTS, 0)
            pair = quantise("step%d" % s, values[:, first : first + 2 * STEP + extra], (2 * STEP + extra) // SLOTS,
                            "log_b%d" % (s + 2) if s + 2 >= TURNED else None)
            made[STEPS[s]] = window(pair, places[0], GROUP), window(pair, places[1], GROUP)
            return window(pair, places[2], PASS) if rider else None

        woven, apart = "p (c i t) -> p c t i", "p t (c i) -> p c t i"

        scaled_all = kept("scaled_all", [P, 4 * STEP], F32)

        def scaled(s):
            place = s % 2 if s < TURNED else s - TURNED + 2
            return scaled_all[:, place * STEP : (place + 1) * STEP]

        def scale(s, u):
            rb = STEPS[s][0]
            if (s, u) in SCALAR_GAINS:
                for t in range(SLOTS):
                    nc.scalar.activation(out=by_slots(scaled(s)[:, u * PASS : (u + 1) * PASS])[:, t, :], in_=diff[s, u][:, t, :],
                                         func=ACT.Copy, scale=gains[:, rb, t : t + 1])
                return
            nc.vector.tensor_tensor(out=scaled(s)[:, u * PASS : (u + 1) * PASS].rearrange("p (j t) -> p j t", t=SLOTS),
                                    in0=diff[s, u][:].rearrange("p t j -> p j t"),
                                    in1=gains[:, rb : rb + 1, :].to_broadcast([P, P, SLOTS]), op=ALU.mult)

        def round_e(s):
            pool_copy(e_values, scaled(s))

        def round_tile(s, u):
            tile = slice(u * PASS, (u + 1) * PASS)
            if (s, u) in SCALAR_GAINS:
                pool_copy(e_values[:, tile].rearrange("p (j t) -> p j t", t=SLOTS), by_slots(scaled(s)[:, tile]).rearrange("p t j -> p j t"))
            else:
                pool_copy(e_values[:, tile], scaled(s)[:, tile])

        def square(s, u):
            tile = slice(u * PASS, (u + 1) * PASS)
            if (s, u) in SCALAR_GAINS:
                nc.vector.tensor_tensor(out=sq_values(s)[:, tile].rearrange(woven, i=LINE, t=SLOTS), in0=diff[s, u][:].rearrange(apart, i=LINE),
                                        in1=by_slots(scaled(s)[:, tile]).rearrange(apart, i=LINE), op=ALU.mult)
                return
            nc.vector.tensor_tensor(out=sq_values(s)[:, tile].rearrange("p (j t) -> p j t", t=SLOTS), in0=diff[s, u][:].rearrange("p t j -> p j t"),
                                    in1=scaled(s)[:, tile].rearrange("p (j t) -> p j t", t=SLOTS), op=ALU.mult)

        def by_slots(ap):
            return ap.rearrange("p (t c) -> p t c", t=SLOTS)

        def subtract(s, part):
            d = by_slots(scaled(s - 2))[:, :, part]
            nc.vector.tensor_tensor(out=d, in0=log_a[s][:, :, part], in1=by_slots(log_b[s])[:, :, part], op=ALU.subtract)
            for t in range(SLOTS):
                nc.scalar.activation(out=by_slots(scaled(s))[:, t, part], in_=d[:, t, :], func=ACT.Copy, scale=gains[:, 1, t : t + 1])

        def square_direct(s, part, dst):
            nc.vector.tensor_tensor(out=dst.rearrange(woven, i=LINE, t=SLOTS), in0=by_slots(scaled(s))[:, :, part].rearrange(apart, i=LINE),
                                    in1=by_slots(scaled(s - 2))[:, :, part].rearrange(apart, i=LINE), op=ALU.mult)

        def round_direct(s, part, dst, copy=nc.vector.tensor_copy):
            copy(out=dst.rearrange(woven, i=LINE, t=SLOTS), in_=by_slots(scaled(s))[:, :, part].rearrange(apart, i=LINE))

        def passes(dst, rb, nt, e, sq, start, stop):
            cols = slice(nt * P, (nt + 1) * P)
            nc.tensor.matmul_mx(out=dst, lhsT=wr_q[rb][0][:, cols].bitcast(FP8X4), lhsT_scale=wr_q[rb][1][:, cols],
                                rhs=e[0].bitcast(FP8X4), rhs_scale=e[1], start=start, stop=False)
            nc.tensor.matmul_mx(out=dst, lhsT=w8_w[:, rb, cols].bitcast(FP8X4),
                                lhsT_scale=w8_sc[:, rb * N + nt * P : rb * N + (nt + 1) * P],
                                rhs=sq[0].bitcast(FP8X4), rhs_scale=sq[1], start=False, stop=stop)

        def score_passes(rb, g, first_bank=None):
            for pair in range(2):
                if rb == 0:
                    banks[g, pair] = bank(first_bank + pair, [P, 2, GROUP])
                for u in range(2):
                    passes(banks[g, pair][:, u, :], rb, 2 * pair + u, made[rb, g][0], made[rb, g][1],
                           rb == 0 and u == 0, rb == 1 and u == 1)

        rows = out.rearrange("(nt p) j -> p nt j", p=P)

        spent = ["tab2_w", "tab_w0", "log_b4", "wa_raw10", "wa_raw01", "last_values"]

        def store_scores(g, copies=(nc.scalar.copy, nc.scalar.copy)):
            for pair, copy in enumerate(copies):
                staged = kept("staged%d%d" % (g, pair), [P, 2, GROUP], F32, spent[2 * g + pair])
                copy(out=staged[:], in_=banks[g, pair][:])
                nc.sync.dma_start(out=rows[:, 2 * pair : 2 * pair + 2, g * GROUP : (g + 1) * GROUP], in_=staged[:])

        last_banks = [[4], [5, 0]]

        def last_passes(rb, u, e, sq):
            count = 4 // (u + 1)
            if rb == 0:
                banks["last", u] = [bank(i, [P, count, P]) for i in last_banks[u]]
            for nt in range(4):
                i, k = divmod(nt, count)
                passes(banks["last", u][i][:, k, :], rb, nt, e, sq, rb == 0 and k == 0, rb == 1 and k == count - 1)

        def store_last(u):
            j0 = S - GROUP + u * P
            count = 4 // (u + 1)
            for i, sums in enumerate(banks["last", u]):
                staged = kept("staged_last%d%d" % (u, i), [P, count, P], F32)
                (nc.scalar.copy if i == 0 else nc.vector.tensor_copy)(out=staged[:], in_=sums[:])
                nc.sync.dma_start(out=rows[:, i * count : (i + 1) * count, j0 : j0 + P], in_=staged[:])

        first_values = kept("first_values", [P, 2 * BLOCK], BF16)
        low, high = slice(0, P // 2), slice(P // 2, P)
        library_logs(0, 0)
        negate(0, log_b[0])
        for kp, copy in enumerate((nc.scalar.copy, nc.vector.tensor_copy)):
            round_rows(copy, wa_raw[kp, 0], first_values[:, kp * BLOCK : (kp + 1) * BLOCK], natural, slice(0, P))
        pair = quantise("wa_first", first_values[:], 2 * PASS)
        for kp in range(2):
            wa_q[kp, 0] = window(pair, kp * PASS, PASS)
        early = kept("log_b12", [P, 2, STEP], F32, "wa_raw00")
        for s in range(1, TURNED):
            library_logs(s, 6 * (s % 2), early[:, s - 1] if s < 3 else None)
        held = kept("held", [P, 2, STEP], F32, "first_values")
        for s in range(1, TURNED):
            negate(s, held[:, s - 1] if s < 3 else log_b[s - 2])
        v_w = [kept("v_w%d" % kp, [P, S], U32) for kp in range(2)]
        for kp, first, end in ((0, 0, 2 * GROUP), (0, 2 * GROUP, S), (1, 0, GROUP), (1, GROUP, 2 * GROUP), (1, 2 * GROUP, S)):
            gather(v_w[kp], tab_w[kp], list8, first, end)
        values = kept("values", [P, 2 * BLOCK + 3 * STEP], BF16, "tab_w1")
        e_values = values[:, BLOCK + STEP : BLOCK + 2 * STEP]
        riders = {0: (wa_raw[0, 1], by_slot), 1: (wa_raw[1, 1], by_slot), 2: (wr_raw[0], natural), 3: (wr_raw[1], natural)}
        halves = [slice(0, P), slice(P, GROUP)]

        def round_rider(s):
            for part in (low, high):
                round_rows(nc.scalar.copy, riders[s][0], rider_values(s), riders[s][1], part)

        def quantise_before(s):
            carried = quantise_step(s - 1, s - 1 in riders)
            if s - 1 < 2:
                wa_q[s - 1, 1] = carried
            elif carried:
                wr_q[s - 3] = carried

        for s in range(2):
            for u in range(2):
                turn_library(s, u)
            sample_logs(s, 6 * s)
            for u in range(2):
                turn_sample(s, u)
        scale(0, 0)
        whole = slice(0, GROUP)
        e_direct = kept("e_direct", [P, STEP], BF16, "wa_raw11")
        last_values = kept("last_values", [P, 2, 2, PASS], BF16)
        for s in range(TURNED):
            scale(s, 1)
            if s == 5:
                subtract(6, whole)
                round_direct(6, whole, e_direct[:], nc.scalar.copy)
            if s:
                quantise_before(s)
            round_e(s)
            if s in riders:
                round_rider(s)
            if s < 3:
                sample_logs(s + 2, 6 * (s % 2))
            if s == 3:
                sample_logs(5, 6)
                sample_logs(6, 0)
                library_logs(6, 6)
            if s == 4:
                library_logs(last, 0)
                sample_logs(last, 6)
                score_passes(0, 0, 0)
            if s == 5:
                score_passes(1, 0)
                store_scores(0)
                score_passes(0, 1, 6)
                score_passes(0, 2, 2)
            for u in range(2):
                square(s, u)
                if s + 2 < TURNED:
                    turn_library(s + 2, u)
                    turn_sample(s + 2, u)
                if u == 0 and s + 1 < TURNED:
                    scale(s + 1, 0)
        subtract(last, whole)
        for u in range(2):
            round_direct(last, halves[u], last_values[:, u, 0], nc.scalar.copy)
        quantise_before(6)
        score_passes(1, 1)
        store_scores(1)
        sq_direct = kept("sq_direct", [P, STEP], BF16, "log_a%d" % last)
        square_direct(6, whole, sq_direct[:])
        square_direct(last, halves[0], last_values[:, 0, 1])
        made[STEPS[6]] = [window(quantise(name, tile[:], GROUP), 0, GROUP) for name, tile in (("e6", e_direct), ("sq6", sq_direct))]
        for u in range(2):
            last_passes(0, u, window(made[0, 3][0], u * P, P), window(made[0, 3][1], u * P, P))
        score_passes(1, 2)
        square_direct(last, halves[1], last_values[:, 1, 1])
        for u in range(2):
            pair = quantise("last%d" % u, last_values[:, u].rearrange("p s c -> p (s c)"), 2 * P)
            last_passes(1, u, window(pair, 0, P), window(pair, P, P))
        store_scores(2, (nc.scalar.copy, nc.vector.tensor_copy))
        for u in range(2):
            store_last(u)
